import numpy as np, ml_dtypes
CORES = [3,11,19,27,35,43,51,59]
N = 8
import mx_ref
BF = ml_dtypes.bfloat16
def gcols(t, e):
    v = np.concatenate([t.reshape(8, 16, -1, 4), np.zeros((8, 16, 1, 4), BF)], axis=2)
    return np.ascontiguousarray(np.stack([v[g][:, e[g]] for g in range(8)])).reshape(128, -1)
def tile(rs):
    return np.stack(rs, axis=2).reshape(128, -1).astype(BF)
def pick(q, e):
    c = np.concatenate([q[0].reshape(128, -1, 4), np.zeros((128, 1, 4), np.uint8)], axis=1); s = np.concatenate([q[1], np.ones((16, 1), np.uint8)], axis=1)
    return (np.ascontiguousarray(c[:, e].reshape(128, -1)), np.ascontiguousarray(s[:, e]))
def join(*qs):
    return (np.concatenate([q[0] for q in qs], axis=1), np.concatenate([q[1] for q in qs], axis=1))
def put(q, e, v):
    c, s = q[0].reshape(128, -1, 4).copy(), q[1].copy(); c[:, e] = v[0].reshape(128, -1, 4); s[:, e] = v[1]
    return (c.reshape(128, -1), s)
def pk(c, s):
    return (np.ascontiguousarray(c), mx_ref.live(s))
def emit(q):
    return q[0], q[1]
def packed(v, rng):
    q = [mx_ref.quantize(np.ascontiguousarray(v[r])) for r in range(N)]
    return np.stack([a for a, b in q]), np.stack([mx_ref.plane(b, rng) for a, b in q])
def values_of_codes():
    e, c = np.zeros((128, 128, 4), np.float32), np.zeros((128, 2, 4), np.uint8)
    e[np.arange(128), np.arange(128), 0] = 1
    c[:127, :, 0] = np.arange(256).reshape(2, 128).T[:127]
    return mx_ref.matmul(mx_ref.quantize(e.reshape(128, 512).astype(BF)), (c.reshape(128, 8), np.full((16, 2), 127, np.uint8))).T.reshape(-1).astype(np.float64)
CODE_VALUE, SCALE_VALUE = values_of_codes(), 2.0 ** (np.arange(256) - 127.0)
def decode(q):
    return (CODE_VALUE[q[0]].reshape(16, 8, -1, 4) * SCALE_VALUE[q[1]][:, None, :, None] + 0.0).reshape(128, -1).astype(np.float32)
def f(rng, *shape):
    return mx_ref.flush((rng.standard_normal(shape, dtype=np.float32) * np.exp2(rng.integers(-2, 3, shape[:-1] + (1,)))).astype(BF))
def wide(rng, *shape, cols=0):
    v = rng.standard_normal(shape, dtype=np.float32) * np.exp2(rng.integers(-12, 13, shape)).astype(np.float32)
    if cols: v *= np.repeat(np.exp2(rng.integers(-cols, cols + 1, shape[:-2] + (1, shape[-1] // 4))) * (rng.random(shape[:-2] + (1, shape[-1] // 4)) > 0.0625), 4, axis=-1).astype(np.float32)
    return mx_ref.flush(v.astype(BF))
C, P, R = 320, 80, 2
def big(v):
    v = v.astype(np.float32)
    v[np.abs(v) < np.float32(2.0 ** -16)] = 0
    return v.astype(BF)
def numbers_of(rng):
    return {"x": big(f(rng, N, 128, 4 * C)), "u": np.array(f(rng, N, 128, 512)), "v": np.array(f(rng, N, 128, 512))}
def layers(rng):
    return big(f(rng, N, 128, 2048)).reshape(N, 8, 16, 4, 8, 16, 4)
def weights(rng, w):
    c, p = packed(np.ascontiguousarray(w).reshape(N, 128, 2048), rng)
    return {"wc": c, "ws": p}
def setup_inputs(rng):
    return {**numbers_of(rng), **weights(rng, layers(rng))}
def setup_inputs_ties(rng):
    d = numbers_of(rng)
    e = rng.permutation(N)
    x = d["x"].reshape(N, 8, 16, C, 4)
    for r in range(N):
        k = rng.permutation(C) % 3
        if r == e[0]: k = np.zeros(C, int)
        elif r in e[2::2]: k = rng.permutation(3)[np.arange(C) % 3]
        a = x[r][:, :8, :3].copy()
        a[:, :, 2] = 0
        x[r][:, :8] = a[:, :, k]
    x[e[1]] = 0
    u = d["u"].reshape(N, 8, 16, 128, 4)
    for i in range(5): u[:, :, 8:, i::16] = 0
    w = layers(rng)
    w[:, :, :, :, :, :8] = 0
    return {"x": x.reshape(N, 128, 4 * C), "u": u.reshape(N, 128, 512), "v": d["v"], **weights(rng, w)}
def setup_inputs_near(rng):
    d = numbers_of(rng)
    x = d["x"].astype(np.float32).reshape(N, 8, 16, C, 4)
    x[:, :, :9] = 0
    u = d["u"].reshape(N, 128, 128, 4)
    for i in range(5): u[:, :, i::16] = 0
    o = rng.permutation(N) % 4
    for r in range(N):
        k = 2.0 ** -30 if o[r] else 1.0
        c = rng.integers(0, 2, (8, 1)) * 2.0 - 1.0
        s = rng.integers(-1, 2, (8, C, 4))
        if o[r] < 2:
            n = rng.integers(0, 16, (8, C))
            x[r, :, 0] = ((n[:, :, None] >> np.arange(4)) & 1) * np.exp2(np.arange(4) - 23.0)
            x[r, :, 1, :, 0] = 2.0 ** -10
            x[r, :, 2] = s * 2.0 ** -10
            x[r, :, 8, :, 0] = c
        else:
            x[r, :, 0, :, 0] = c * rng.integers(1, 16, (8, C)) * 2.0 ** -29
            x[r, :, 2] = s * 2.0 ** -29
        for g in rng.permutation(8)[:4]: x[r, g, 8 if o[r] < 2 else 0, rng.integers(C), 0] = 2.0 ** 29 * (rng.integers(0, 2) * 2.0 - 1.0)
        for h in range(0, 128, 16):
            u[r, h, h + 4] = k
            u[r, h + 1, h + 4, 0] = k
            u[r, h + 8, h + 4, 0] = k
            for i in range(4): u[r, h + 2, h + i, i] = k
    w = layers(rng)
    w[:, :, :9] = 0
    w[:, :, :, :, :, :9] = 0
    return {"x": x.reshape(N, 128, 4 * C).astype(BF), "u": u.reshape(N, 128, 512), "v": d["v"], **weights(rng, w)}
def setup_inputs_skew(rng):
    d = numbers_of(rng)
    x = d["x"].astype(np.float32).reshape(N, 8, 16, C, 4)
    t = (1 + (2 * rng.integers(0, 64, (N, 8, 8, C // 2, 4)) + 1) / 128) * np.exp2(-rng.integers(8, 15, (N, 8, 8, C // 2, 4)).astype(float)) * (rng.integers(0, 2, (N, 8, 8, C // 2, 4)) * 2.0 - 1.0)
    t[:, :, 3, :, 1] = 1.96875
    x[:, :, 8:, ::2] = t * np.exp2(rng.integers(-2, 3, (N, 8, 1, C // 2, 1)).astype(float))
    u = d["u"].reshape(N, 128, 128, 4)
    for i in range(5): u[:, :, i::16] = 0
    for h in range(0, 128, 16):
        for b in range(12): u[:, h + b // 4, h + 4, b % 4] = 2.0 ** b
        for i in range(4): u[:, h + 3, h + i, i] = 1
    n = -(-C // 7)
    n2 = n - (-(C - n) // 5)
    n3 = n2 - (-(C - n2) // 3)
    down = C - 1 - np.arange(C)
    for r in range(N):
        for j, g in enumerate(rng.permutation(8)):
            a = np.append(rng.permutation(np.delete(np.arange(4), j % 4)), j % 4)
            two = np.zeros((C, 4), int)
            if j < 6:
                two[:n, a[0]] = 1
                two[n:n2, a[1]] = 1
            if j < 4: two[n2:n3, a[2]] = 1
            if j >= 6: two[-(-2 * C // 5):] = 1
            o = rng.permutation(C)
            x[r, g][:3, o] = (down[None, :, None] >> (4 * np.arange(3)[:, None, None] + np.arange(4))) & 1
            x[r, g][3, o] = np.where(two > 0, 1, -rng.integers(0, 2, (C, 4)))
    w = layers(rng)
    w[:, :, :, :, :, :4] = 0
    return {"x": x.reshape(N, 128, 4 * C).astype(BF), "u": u.reshape(N, 128, 512), "v": d["v"], **weights(rng, w)}
def setup_inputs_huge(rng):
    d = numbers_of(rng)
    o = rng.permutation(N)
    h = rng.permutation(8)
    x = -0.95 - 0.05 * rng.random((N, 8, 16, C, 4))
    x[:, h[4:]] = (0.75 + 0.1 * rng.random((N, 4, 16, C, 4))) * rng.choice([-1.0, 1.0], (N, 4, 1, C, 1))
    u = d["u"].reshape(N, 128, 128, 4)
    for i in range(5): u[:, :, i::16] = 0
    for r in range(N):
        if o[r] < N // 2: x[r] = (0.8 + 0.1 * rng.random((8, 16, C, 4))) * rng.choice([-1.0, 1.0], (1, 1, C, 1))
        for g in range(8):
            for i in range(5):
                a, n = 16 * int(rng.choice(h[4:])), 16
                if i == 4 and o[r] < N // 2: a, n = 0, 128
                u[r, a:a + n, 16 * g + i] = (2.0 ** 30 * (1 - 0.05 * rng.random((n, 4))) * rng.choice([-1.0, 1.0])).astype(np.float32).astype(BF)
    w = np.zeros((N, 128, 4, 128, 4), np.float32)
    i = np.arange(128)
    for b in range(4): w[:, i, b, i, b] = -1
    return {"x": (2.0 ** 30 * x).astype(np.float32).reshape(N, 128, 4 * C).astype(BF), "u": u.reshape(N, 128, 512), "v": d["v"], **weights(rng, w.astype(BF))}
def setup_inputs_spread(rng):
    d = setup_inputs(rng)
    d["x"] = big(wide(rng, N, 128, 4 * C, cols=6))
    return d
def check_inputs(d):
    b = []
    for k in ("x", "u", "v"):
        a = np.abs(d[k].astype(np.float32))
        if not (np.isfinite(a).all() and ((a == 0) | (a >= 2.0 ** -30) & (a <= 2.0 ** 30)).all()): b.append("a value of " + k)
    none, least, most = [emit(mx_ref.quantize(np.full((128, 16), k, np.float32).astype(BF)))[1][0, 0] for k in (0.0, 2.0 ** -30, 2.0 ** 30)]
    for r in range(N):
        if ((d["wc"][r] == 0x7F) | (d["wc"][r] == 0xFF)).any(): b.append("wc: a code that is no number")
        s = mx_ref.live(d["ws"][r])
        if ((s != none) & ((s < least) | (s > most))).any(): b.append("ws: a scale out of range")
    return b
def divide(sums):
    g = np.arange(8)
    first, end = np.zeros((4, 8), np.int64), np.full((4, 8), C)
    a, left = np.zeros(8, np.int64), np.ones((4, 8), bool)
    for m in (4, 3, 2):
        worth = sums - np.stack([sums[k, g, a] for k in range(4)])[:, :, None]
        e = np.sum(m * worth < worth[:, :, -1:], axis=2)
        e[~left] = C + 1
        k = np.argmin(e, axis=0)
        first[k, g] = a
        a = e[k, g]
        end[k, g] = a
        left[k, g] = False
    first[np.argmax(left, axis=0), g] = a
    return first, end
def reference(x, u, v, wc, ws):
    qu = [mx_ref.quantize(u[r]) for r in range(N)]
    lay = [pk(wc[r], ws[r]) for r in range(N)]
    now = [x[r] for r in range(N)]
    of = [np.arange(k * P, k * P + P) for k in range(4)]
    slot_of = np.zeros((N, 8, C), np.int64)
    for t in range(R):
        sent, best, made = [], [], []
        slot_of[:] = -1
        for r in range(N):
            s = mx_ref.matmul(qu[r], mx_ref.quantize(now[r])) + np.float32(0.0)
            o = np.argsort(-s[4::16], axis=1, kind="stable")
            worth = np.stack([1 + (np.take_along_axis(s[k::16], o, axis=1) > 0) for k in range(4)])
            first, end = divide(np.concatenate([np.zeros((4, 8, 1), np.int64), np.cumsum(worth, axis=2)], axis=2))
            slots = []
            for k in range(4):
                i = first[k][:, None] + np.arange(P)
                slots.append(np.where(i < end[k][:, None], np.take_along_axis(o, np.minimum(i, C - 1), axis=1), -1))
            slots = np.concatenate(slots, axis=1)
            for g in range(8):
                j = np.nonzero(slots[g] >= 0)[0]
                slot_of[r, g, slots[g, j]] = j
            sent.append(mx_ref.quantize(gcols(now[r], slots)))
            best.append(gcols(now[r], o[:, :P]))
        for r in range(N):
            came = decode(join(*[pick(sent[(r - k) % N], of[k]) for k in range(4)]))
            z = mx_ref.quantize(((came + np.tile(best[r].astype(np.float32), (1, 4))) * np.float32(0.5)).astype(BF))
            made.append(mx_ref.quantize(tile([mx_ref.matmul(pick(lay[r], np.arange(128 * b, 128 * b + 128)), z) * np.float32(0.03125) for b in range(4)])))
        for r in range(N):
            back = decode(join(*[pick(made[(r + k) % N], of[k]) for k in range(4)])).astype(BF)
            now[r] = (now[r].astype(np.float32) + gcols(back, slot_of[r]).astype(np.float32)).astype(BF)
    y, sl = np.zeros((N, 128, C), np.float32), np.zeros((N, 8, C), np.float32)
    oc, osc = np.zeros((N, 128, 4 * C), np.uint8), np.zeros((N, 16, C), np.uint8)
    for r in range(N):
        q = mx_ref.quantize(now[r])
        y[r] = mx_ref.matmul(mx_ref.quantize(v[r]), q)
        sl[r] = slot_of[r]
        oc[r], osc[r] = emit(q)
    return {"y": y, "sl": sl, "oc": oc, "osc": osc}

@@ -1,0 +1,534 @@
+from concourse.bass import DstId, RemoteDMATransfer
+from concourse.mybir import dt, AluOpType as OP, AxisListType, ActivationFunctionType as AF
+
+F32, BF, I32, U16, U8, F8 = "float32", "bfloat16", "int32", "uint16", "uint8", "float8_e4m3fn_x4"
+NR = 2
+UNIT = 2.0 ** 20
+NEG = 2.0 ** 97
+B16 = 1024.0
+B4 = 2.0 ** 21
+
+
+def _scratch():
+    s = {}
+
+    def sb(dtype, **kw):
+        for n in kw:
+            s[n] = ("sbuf", [128, kw[n]], dtype)
+
+    def code(n, w):
+        s[n] = ("sbuf", [128, w], F8)
+        s[n + "s"] = ("sbuf", [128, w], U8)
+    sb(BF, x0=1296, x1=1296, x2=1296, ut=512, vt=512, eg=512, one=512, half=512, id4=512, un=2048, btile=1472, eh=960,
+       z0=512, h0=512, z1=960, h1=960, bk=1296, junk=1280, ct0=1280, ct1=1280, ct2=1280)
+    for n, w in (("qu", 128), ("qur", 128), ("qv", 128), ("wq", 512), ("qx", 320), ("qeg", 128), ("qun", 512),
+                 ("qbo", 128), ("qzo", 128), ("qho", 128), ("qz1", 240), ("qb", 240), ("qh", 240),
+                 ("qc0", 320), ("qc1", 320), ("qc2", 320)):
+        code(n, w)
+    for r in range(NR):
+        for n in ("came", "back"):
+            code("%s%d" % (n, r), 240)
+    sb(F32, i16=320, i4=400, ij=336, mm=320, d0=320, rs=320, k16=320, k4=400, ta=400, tb=400, d1=320,
+       st=320, eq=320, rc=336, rcb=20, pc=8, v4=320, wrow=336, cw=328, on=320, rx=320, rk=20, acc=8, rsum=32, ncq=20,
+       gg=48, ee=48, iw=336, lm=24, sm=128, tab=16, te=48, sc=20, pl=80, wsl=400, ox=400, tf=160, rks=80, kc=80,
+       sl1=400, sl2=80)
+    sb(I32, pi=8, xi=64, oi=200, po=20)
+    sb(U16, ul=8, xl=4, l80=10, rk16=20, e16=8, off16=20, off4=100, po16=100)
+    for b in range(8):
+        s["p%d" % b] = ("psum", [128, 512], F32)
+    return s
+
+
+SCRATCH = _scratch()
+SEMAPHORES = (["sV", "sA", "sP", "sG", "gd", "lqb", "lqh", "dx", "du", "dw", "dv", "out"]
+              + [p + str(r) for p in ("came", "back") for r in range(NR)])
+
+
+def tracker(g, T):
+    eng = {"V": g.vector, "A": g.scalar, "P": g.tensor, "G": g, "S": g.sync}
+    sem = {"V": "sV", "A": "sA", "P": "sP", "G": "sG"}
+    count = {q: 0 for q in sem}
+    known = {q: {} for q in eng}
+    known["far"] = {}
+    clock = {}
+    log = {}
+
+    def split(k):
+        a = k.split("/")
+        return a[0], (a[1] if len(a) > 1 else None)
+
+    def need(q, reads, writes, acc):
+        out = {}
+        for keys, w in ((reads, False), (writes, True)):
+            for k in keys:
+                n, s = split(k)
+                psum = n[0] == "p" and n[1:].isdigit()
+                for (s2, q2, tok, w2) in log.get(n, []):
+                    if not psum and s is not None and s2 is not None and s != s2:
+                        continue
+                    dma = tok[0] not in ("sV", "sA", "sP", "sG")
+                    if q2 == q and not dma:
+                        if (not w2 and not w) or (acc and w):
+                            continue
+                    elif not w and not w2 and not psum:
+                        continue
+                    out[tok[0]] = max(out.get(tok[0], 0), tok[1])
+        return out
+
+    def wait(q, toks):
+        for s in sorted(toks):
+            if known[q].get(s, 0) < toks[s]:
+                eng[q].wait_ge(T.sem[s], toks[s])
+                for (s2, v2) in clock.get((s, toks[s]), {}).items():
+                    known[q][s2] = max(known[q].get(s2, 0), v2)
+                known[q][s] = max(known[q].get(s, 0), toks[s])
+
+    def note(q, tok, reads, writes):
+        c = dict(known[q])
+        c[tok[0]] = max(c.get(tok[0], 0), tok[1])
+        if tok in clock:
+            for s2 in clock[tok]:
+                c[s2] = max(c.get(s2, 0), clock[tok][s2])
+        clock[tok] = c
+        for k in writes:
+            n, s = split(k)
+            log[n] = [e for e in log.get(n, []) if not (s is None or e[0] == s)] + [(s, q, tok, True)]
+        for k in reads:
+            n, s = split(k)
+            log[n] = [e for e in log.get(n, []) if not (not e[3] and e[1] == q and e[0] == s)] + [(s, q, tok, False)]
+
+    def tr(q, fn, reads, writes, acc=False):
+        wait(q, need(q, reads, writes, acc))
+        count[q] += 1
+        fn(eng[q]).then_inc(T.sem[sem[q]], 1)
+        note(q, (sem[q], count[q]), reads, writes)
+
+    def dma(q, fn, tok, reads, writes):
+        wait(q, need(q, reads, writes, False))
+        fn(eng[q]).then_inc(T.sem[tok[0]], 16)
+        note(q, tok, reads, writes)
+
+    def remote(fn, tok, reads):
+        wait("G", need("G", reads, [], False))
+        fn(g)
+        note("G", tok, reads, [])
+
+    def arrive(tok, writes):
+        note("far", tok, [], writes)
+    return tr, dma, remote, arrive
+
+
+def rank_program(g, core, T, topo):
+    rank = T.rank_of(core)
+    if rank is None:
+        return
+    N = len(T.cores)
+    tr, dma, remote, arrive = tracker(g, T)
+
+    def V(fn, r, w):
+        tr("V", fn, r, w)
+
+    def ts(out, in0, s1, s2, op0, op1, r, w):
+        if op1 is None:
+            V(lambda e: e.tensor_scalar(out, in0, s1, None, op0), r, w)
+        else:
+            V(lambda e: e.tensor_scalar(out, in0, s1, s2, op0, op1), r, w)
+
+    def tt(out, a, b, op, r, w):
+        V(lambda e: e.tensor_tensor(out, a, b, op), r, w)
+
+    def cp(out, in_, r, w):
+        V(lambda e: e.tensor_copy(out, in_), r, w)
+
+    def scan(out, a, b, init, op0, op1, r, w):
+        V(lambda e: e.tensor_tensor_scan(out, a, b, init, op0, op1), r, w)
+
+    def fill(ap, c, w):
+        V(lambda e: e.memset(ap, c), [], w)
+
+    def act(out, in_, func, r, w, **kw):
+        tr("A", lambda e: e.activation(out, in_, func, **kw), r, w)
+
+    def iota(out, pat, base, cm, w, flag=True):
+        if flag:
+            tr("G", lambda e: e.iota(out, pat, base, cm, allow_small_or_imprecise_dtypes=True), [], w)
+        else:
+            tr("G", lambda e: e.iota(out, pat, base, cm), [], w)
+
+    def select(out, in_, pat, op, base, cm, r, w):
+        tr("G", lambda e: e.affine_select(out, in_, pat, op, 0.0, base, cm), r, w)
+
+    def quant(name, a, b, src, lo, r):
+        V(lambda e: e.quantize_mx(T[name][:, a:b], T[name + "s"][:, a:b], T[src][:, lo:lo + 4 * (b - a)]),
+          r, [name, name + "s"])
+
+    def mm(bank, n, sta, sa, mov, ma, start=True, stop=True):
+        p = "p%d" % bank
+        tr("P", lambda e: e.matmul_mx(T[p][:, 0:n], T[sta][:, sa:sa + 128], T[sta + "s"][:, sa:sa + 128],
+                                      T[mov][:, ma:ma + n], T[mov + "s"][:, ma:ma + n], start, stop),
+           [sta, sta + "s", mov, mov + "s"], [p], acc=not start)
+
+    dma("S", lambda e: e.dma_start(T.x0[:, 0:1280], T.x[:]), ("dx", 16), [], ["x0/x"])
+    dma("A", lambda e: e.dma_start(T.ut[:], T.u[:]), ("du", 16), [], ["ut"])
+    dma("S", lambda e: e.dma_start(T.wq[:].bitcast(dt.uint8), T.wc[:]), ("dw", 32), [], ["wq"])
+    dma("S", lambda e: e.dma_start(T.wqs[:], T.ws[:]), ("dw", 32), [], ["wqs"])
+    dma("S", lambda e: e.dma_start(T.vt[:], T.v[:]), ("dv", 16), [], ["vt"])
+
+    iota(T.pi[:, 0:1], [[0, 1]], 0, 1, ["pi/0"], False)
+    iota(T.xi[:, 0:8], [[16, 8]], 4, 0, ["xi/u"], False)
+    iota(T.i16[:], [[0, 20], [1, 16]], 0, 0, ["i16"])
+    iota(T.i4[:], [[0, 100], [1, 4]], 0, 0, ["i4"])
+    iota(T.ij[:], [[1, 336]], 0, 0, ["ij"])
+    fill(T.one[:], 1.0, ["one"])
+    select(T.id4[:], T.one[:], [[-16, 8], [0, 64]], OP.is_ge, 0, 1, ["one"], ["id4"])
+    select(T.eg[:], T.id4[:], [[16, 8], [0, 64]], OP.is_ge, 15, -1, ["id4"], ["eg"])
+    iota(T.sl1[:, 0:20], [[0, 4], [16, 5]], 0, 0, ["sl1"])
+    iota(T.xi[:, 8:11], [[16, 3]], 0, 0, ["xi/a"], False)
+    iota(T.xi[:, 16:26], [[16, 10]], 0, 0, ["xi/b"], False)
+
+    cp(T.ul[:], T.xi[:, 0:8], ["xi/u"], ["ul"])
+    ts(T.pi[:, 1:2], T.pi[:, 0:1], 15, None, OP.bitwise_and, None, ["pi/0"], ["pi/1"])
+    ts(T.pi[:, 2:3], T.pi[:, 0:1], 3, None, OP.bitwise_and, None, ["pi/0"], ["pi/2"])
+    ts(T.pi[:, 3:4], T.pi[:, 1:2], 2, None, OP.logical_shift_right, None, ["pi/1"], ["pi/3"])
+    cp(T.pc[:, 0:3], T.pi[:, 1:4], ["pi"], ["pc/0"])
+    ts(T.mm[:], T.i16[:], T.pc[:, 0:1], -2.0 * NEG, OP.not_equal, OP.mult, ["i16", "pc/0"], ["mm"])
+    ts(T.d0[:], T.i16[:], 2.0 * NEG, -NEG, OP.mult, OP.add, ["i16"], ["d0"])
+    act(T.rs[:], T.i16[:], AF.Sign, ["i16"], ["rs"])
+    act(T.tb[:, 0:320], T.rs[:], AF.Copy, ["rs"], ["tb"], scale=32 * B16, bias=-33 * B16)
+    ts(T.ta[:, 0:320], T.i16[:], T.pc[:, 0:1], 2 * B16, OP.is_gt, OP.mult, ["i16", "pc/0"], ["ta"])
+    tt(T.k16[:], T.ta[:, 0:320], T.tb[:, 0:320], OP.add, ["ta", "tb"], ["k16"])
+    quant("qu", 0, 128, "ut", 0, ["ut"])
+    cp(T.qur[:].bitcast(dt.uint32), T.qu[:].bitcast(dt.uint32).indirect(T.ul[:, 0:8]), ["qu", "ul"], ["qur"])
+    act(T.on[:], T.i16[:], AF.Copy, ["i16"], ["on"], scale=0.0, bias=UNIT)
+    act(T.cw[:, 0:320], T.i16[:], AF.Copy, ["i16"], ["cw/a"], scale=0.0, bias=0.125 * UNIT)
+    act(T.cw[:, 320:328], T.i16[:, 0:8], AF.Copy, ["i16"], ["cw/b"], scale=0.0, bias=0.125 * UNIT)
+    act(T.qurs[:], T.qus[:].indirect(T.ul[:, 0:8]), AF.Copy, ["qus", "ul"], ["qurs"])
+    act(T.ct2[:, 3:1280:4], T.i16[:], AF.Copy, ["i16"], ["ct2/n"], scale=0.0)
+    act(T.half[:], T.one[:], AF.Copy, ["one"], ["half"], scale=0.5)
+    for c in range(10):
+        act(T["ct%d" % (c // 4)][:, 64 * c + c % 4:64 * c + 64:4], T.i16[:, 0:16], AF.Copy, ["i16"],
+            ["ct%d/h%d" % (c // 4, c)], scale=0.0)
+    act(T.ox[:], T.i4[:], AF.Sign, ["i4"], ["ox"])
+    act(T.wsl[:], T.ox[:], AF.Copy, ["ox"], ["wsl"], scale=8 * B4, bias=-9 * B4)
+    act(T.wrow[:], T.ij[:], AF.Copy, ["ij"], ["wrow"], scale=0.0, bias=320.0)
+    fill(T.x0[:, 1280:1296], 0.0, ["x0/z"])
+    select(T.id4[:], T.half[:], [[-1, 128], [0, 4]], OP.is_equal, 0, 1, ["half"], ["id4"])
+
+    def unpack_constants():
+        for b in range(4):
+            select(T.un[:, 512 * b:512 * b + 512], T.id4[:], [[0, 128], [1, 4]], OP.is_equal, -b, 0, ["id4"],
+                   ["un/%d" % b])
+
+    def product_constants():
+        for j in range(4):
+            fill(T.lm[:, j:j + 1], (-0.3125 + j / 64.0) * UNIT, ["lm/0"])
+        fill(T.rsum[:, 19:21], 0.0, ["rsum/z"])
+
+    def order_constants():
+        ts(T.pc[:, 3:4], T.pc[:, 0:1], 1.0 - B16, 15 * B16 - 191.0, OP.mult, OP.add, ["pc/0"], ["pc/3"])
+        ts(T.pc[:, 4:5], T.pc[:, 0:1], 1.0 - B16, 15 * B16 - 175.0, OP.mult, OP.add, ["pc/0"], ["pc/4"])
+        ts(T.ncq[:, 0:10], T.i4[:, 0:10], 0.0, T.pc[:, 3:4], OP.mult, OP.add, ["i4", "pc/3"], ["ncq/a"])
+        ts(T.ncq[:, 10:20], T.i4[:, 0:10], 0.0, T.pc[:, 4:5], OP.mult, OP.add, ["i4", "pc/4"], ["ncq/b"])
+
+    def claim_constants():
+        act(T.iw[:], T.ij[:], AF.Copy, ["ij"], ["iw"], scale=UNIT, bias=0.375 * UNIT)
+        ts(T.ta[:], T.i4[:], T.pc[:, 2:3], 2 * B4, OP.is_gt, OP.mult, ["i4", "pc/0"], ["ta"])
+        ts(T.sl2[:, 0:3], T.xi[:, 8:11], T.pc[:, 0:1], 13.0, OP.add, OP.mult, ["xi/a", "pc/0"], ["sl2/a"])
+        ts(T.sc[:], T.sl1[:, 0:20], T.pc[:, 0:1], 16.125, OP.add, OP.add, ["sl1", "pc/0"], ["sc"])
+        cp(T.xi[:, 28:31], T.sl2[:, 0:3], ["sl2/a"], ["xi/c"])
+        tt(T.k4[:], T.ta[:], T.wsl[:], OP.add, ["ta", "wsl"], ["k4"])
+        ts(T.xi[:, 44:47], T.xi[:, 28:31], 6, None, OP.logical_shift_right, None, ["xi/c"], ["xi/e"])
+        ts(T.sc[:], T.sc[:], UNIT, None, OP.mult, None, ["sc"], ["sc"])
+        fill(T.btile[:, 1280:1472], 0.0, ["btile/pad"])
+        ts(T.xi[:, 8:11], T.xi[:, 44:47], 1.0, None, OP.add, None, ["xi/e"], ["xi/a"])
+        ts(T.xi[:, 60:63], T.xi[:, 44:47], 4, None, OP.bitwise_and, None, ["xi/e"], ["xi/g"])
+        ts(T.xi[:, 28:31], T.xi[:, 8:11], 3, None, OP.bitwise_and, None, ["xi/a"], ["xi/c"])
+        tt(T.xi[:, 8:11], T.xi[:, 28:31], T.xi[:, 60:63], OP.add, ["xi/c", "xi/g"], ["xi/a"])
+        cp(T.xl[:, 0:3], T.xi[:, 8:11], ["xi/a"], ["xl"])
+
+    def first_flight_constants():
+        quant("qun", 0, 512, "un", 0, ["un"])
+        fill(T.z0[:, 320:512], 0.0, ["z0/pad"])
+        fill(T.h0[:, 320:512], 0.0, ["h0/pad"])
+
+    def second_flight_constants():
+        ts(T.sl2[:, 4:14], T.xi[:, 16:26], T.pc[:, 0:1], 205.0, OP.add, OP.mult, ["xi/b", "pc/0"], ["sl2/b"])
+        fill(T.bk[:, 1280:1296], 0.0, ["bk/z"])
+        cp(T.xi[:, 32:42], T.sl2[:, 4:14], ["sl2/b"], ["xi/d"])
+        for k in range(4):
+            fill(T.kc[:, 20 * k:20 * k + 20], 80.0 * ((k + 3) % 4) - 320.0, ["kc/%d" % k])
+        ts(T.xi[:, 48:58], T.xi[:, 32:42], 12, None, OP.logical_shift_right, None, ["xi/d"], ["xi/f"])
+        fill(T.x1[:, 1280:1296], 0.0, ["x1/z"])
+        cp(T.l80[:], T.xi[:, 48:58], ["xi/f"], ["l80"])
+
+    gdn, jn = [0], [0]
+    lsn = {"qb": 0, "qh": 0}
+
+    def send(src, dst, step):
+        got = 0
+        for planes in (False, True):
+            trs = []
+            for i in range(3):
+                to = T.cores[(rank + step * (i + 1)) % N]
+                en = topo.engines(core, to)
+                h = len(en) // 8
+                if planes:
+                    en = en[4 * h:6 * h] if i == 0 else en[6 * h:8 * h] if i == 1 else en[0:4 * h]
+                else:
+                    en = en[0:2 * h] if i == 0 else en[2 * h:4 * h] if i == 1 else en[4 * h:8 * h]
+                mask = 0
+                for x in en:
+                    mask |= 1 << x
+                ad = topo.addr(to)
+                a, b = 80 * i, 80 * i + 80
+                if planes:
+                    s_ap, d_ap = T[src + "s"][:, a:b], T[dst + "s"][:, a:b]
+                else:
+                    s_ap, d_ap = T[src][:, a:b].bitcast(dt.uint8), T[dst][:, a:b].bitcast(dt.uint8)
+                trs.append(RemoteDMATransfer(dst_ids=[DstId(rid=ad[0], pnc=ad[1])], dma_engine_mask=mask,
+                                             remote_sem=T.sem[dst], src=s_ap, dst=d_ap))
+                lsn[src] += len(en)
+                got += len(en)
+            remote(lambda e: e.remote_dma_fused(trs, local_sem=T.sem["l" + src]), ("l" + src, lsn[src]),
+                   [src + "s"] if planes else [src])
+        arrive((dst, got), [dst, dst + "s"])
+
+    for r in range(NR):
+        X, XN = "x%d" % r, "x%d" % (r + 1)
+        xa, xn = T[X], T[XN]
+        quant("qx", 0, 320, X, 0, [X])
+        mm(0, 320, "qur", 0, "qx", 0)
+        mm(2, 320, "qu", 0, "qx", 0)
+        if r == 0:
+            product_constants()
+        tt(T.d1[:], T.p0[:, 0:320], T.mm[:], OP.add, ["p0", "mm"], ["d1"])
+        scan(T.st[:], T.d0[:], T.d1[:], -NEG, OP.min, OP.max, ["d0", "d1"], ["st"])
+        act(T.v4[:], T.p2[:, 0:320], AF.Sign, ["p2"], ["v4"])
+        act(T.v4[:], T.v4[:], AF.Relu, ["v4"], ["v4"], scale=UNIT)
+        gdn[0] += 16
+        dma("G", lambda e: e.dma_start(T.v4[:], T.ij[:, 0:320], accum_op=OP.add), ("gd", gdn[0]), ["ij"], ["v4"])
+        if r == 0:
+            unpack_constants()
+
+        def compare(c):
+            n, t = "ct%d" % (c // 4), c % 4
+            for (k, lo, hi, op, col) in ((c, c + 1, c + 11, OP.is_le, c), (c + 10, c + 11, 20, OP.is_le, 10 + c),
+                                         (c + 10, 0, c, OP.is_lt, 20 + c)):
+                if lo < hi:
+                    o, key = T[n][:, 64 * lo + t:64 * hi:4], "%s/%d" % (n, col)
+                    ts(o, T.p0[:, 16 * lo:16 * hi], T.st[:, 16 * k + 15:16 * k + 16], None, op, None, ["p0", "st"],
+                       [key])
+                    jn[0] = (jn[0] + 1) % 8
+                    act(T.junk[:, 160 * jn[0]:160 * jn[0] + 16 * (hi - lo)], o, AF.Copy, [key],
+                        ["junk/%d" % jn[0], "rsum/%d" % col], accum_out=T.rsum[:, col:col + 1])
+
+        def count(b):
+            quant("qc%d" % b, 0, 320, "ct%d" % b, 0, ["ct%d" % b])
+            mm(3, 320, "qeg", 0, "qc%d" % b, 0, b == 0, b == 2)
+        for c in range(4):
+            compare(c)
+        if r == 0:
+            quant("qeg", 0, 128, "eg", 0, ["eg"])
+        count(0)
+        if r == 0:
+            order_constants()
+        for c in range(4, 8):
+            compare(c)
+        count(1)
+        tt(T.ct2[:, 2:1280:4], T.st[:], T.p0[:, 0:320], OP.is_ge, ["p0", "st"], ["ct2/d"])
+        compare(8)
+        compare(9)
+        count(2)
+        scan(T.rc[:, 0:320], T.rs[:], T.ct2[:, 2:1280:4], 0.0, OP.mult, OP.add, ["rs", "ct2/d"], ["rc"])
+        tt(T.rcb[:], T.rc[:, 15:320:16], T.ncq[:], OP.add, ["rc", "ncq"], ["rcb"])
+        tt(T.rcb[:], T.rcb[:], T.rsum[:, 0:20], OP.add, ["rcb", "rsum/z"] + ["rsum/%d" % c for c in range(19)], ["rcb"])
+        tt(T.rcb[:, 10:20], T.rcb[:, 10:20], T.rsum[:, 20:30], OP.add,
+           ["rcb", "rsum/z"] + ["rsum/%d" % c for c in range(21, 30)], ["rcb"])
+        scan(T.rx[:], T.k16[:], T.p3[:, 0:320], 0.0, OP.add, OP.max, ["k16", "p3"], ["rx"])
+        tt(T.rk[:], T.rx[:, 15:320:16], T.rcb[:], OP.subtract, ["rx", "rcb"], ["rk"])
+        cp(T.rk16[:], T.rk[:], ["rk"], ["rk16"])
+        cp(T.wrow[:, 0:336].indirect(T.rk16[:, 0:20]), T.v4[:], ["rk16", "v4"], ["wrow"])
+        scan(T.cw[:, 1:321], T.wrow[:, 16:336], T.on[:], 0.125 * UNIT, OP.add, OP.add, ["wrow", "on"], ["cw"])
+        tot = T.cw[:, 320:321]
+        act(T.junk[:, 0:320], T.cw[:, 0:320], AF.Sign, ["cw"], ["junk/0", "junk/1", "acc/0"], bias=tot, scale=-4.0,
+            accum_out=T.acc[:, 0:1])
+        sm, lm = T.sm, T.lm
+        ts(sm[:, 20:21], tot, 0.5, None, OP.mult, None, ["cw"], ["sm/t2"])
+        ts(lm[:, 12:16], lm[:, 0:4], sm[:, 20:21], None, OP.add, None, ["lm/0", "sm/t2"], ["lm/t0"])
+        if r == 0:
+            claim_constants()
+
+        def ends(s):
+            ts(T.e16[:, 2 * s:2 * s + 1], T.acc[:, s:s + 1], 0.5, 160.0, OP.mult, OP.add, ["acc/%d" % s],
+               ["e16/%d" % s])
+
+        def show(buf, win, w, s):
+            cp(T[buf][:, 16 * s:16 * s + 16], T[win][:, 0:w].indirect(T.e16[:, 2 * s:2 * s + 1]),
+               [win, "e16/%d" % s], ["%s/%d" % (buf, s)])
+        ke = [sm[:, 0:1], sm[:, 1:2], sm[:, 2:3]]
+        em = [sm[:, 4:8], sm[:, 8:12], sm[:, 12:16]]
+        for s in range(3):
+            m = 4 - s
+            lmc = lm[:, 4 * s:4 * s + 4]
+            ends(s)
+            if s < 2:
+                show("gg", "cw", 328, s)
+                tt(sm[:, 16:20], T.gg[:, 16 * s:16 * s + 4], lm[:, 12 + 4 * s:16 + 4 * s], OP.add,
+                   ["gg/%d" % s, "lm/t%d" % s], ["sm/gm"])
+                V(lambda e, s=s: e.tensor_reduce(sm[:, 21 + s:22 + s], sm[:, 16:20], AxisListType.X, OP.min),
+                  ["sm/gm"], ["sm/th%d" % s])
+                act(T.junk[:, 320 * s + 320:320 * s + 640], T.cw[:, 0:320], AF.Sign, ["cw", "sm/th%d" % s],
+                    ["junk/%d" % (2 * s + 2), "junk/%d" % (2 * s + 3), "acc/%d" % (s + 1)],
+                    bias=sm[:, 21 + s:22 + s], scale=-float(m - 1) / (m - 2), accum_out=T.acc[:, s + 1:s + 2])
+                ts(sm[:, 24:28], sm[:, 16:20], sm[:, 21 + s:22 + s], 2.0 ** 32, OP.is_equal, OP.mult,
+                   ["sm/gm", "sm/th%d" % s], ["sm/w"])
+            show("ee", "iw", 336, s)
+            if s < 2:
+                tt(lm[:, 4 * s + 4:4 * s + 8], lmc, sm[:, 24:28], OP.add, ["sm/w", "lm/%d" % s],
+                   ["lm/%d" % (s + 1)])
+            tt(em[s], T.ee[:, 16 * s:16 * s + 4], lmc, OP.add, ["ee/%d" % s, "lm/%d" % s], ["sm/em%d" % s])
+            if s == 0:
+                ts(lm[:, 16:20], lm[:, 4:8], tot, None, OP.add, None, ["lm/1", "cw"], ["lm/t1"])
+            if s == 1:
+                ts(sm[:, 44:48], lm[:, 8:12], 2.0 ** 31, None, OP.is_lt, None, ["lm/2"], ["sm/l3"])
+            V(lambda e, s=s: e.tensor_reduce(ke[s], em[s], AxisListType.X, OP.min), ["sm/em%d" % s], ["sm/ke%d" % s])
+            w = ["sm/em%d" % s, "sm/ke%d" % s]
+            if s == 0:
+                act(T.wsl[:, 320:400], T.wrow[:, 16:96], AF.Copy, ["wrow"], ["wsl/e"])
+            elif s == 1:
+                ts(sm[:, 48:52], sm[:, 44:48], 320.0625 * UNIT, 16.0 * UNIT, OP.mult, OP.add, ["sm/l3"], ["sm/nl"])
+                ts(sm[:, 28:32], em[0], ke[0], ke[0], OP.is_equal, OP.mult, ["sm/em0", "sm/ke0"], ["sm/n1"])
+                ts(sm[:, 36:40], em[1], ke[1], ke[1], OP.is_equal, OP.mult, w, ["sm/n2"])
+                tt(sm[:, 40:44], sm[:, 28:32], sm[:, 48:52], OP.add, ["sm/n1", "sm/nl"], ["sm/n12"])
+                ts(sm[:, 32:36], em[1], ke[1], ke[0], OP.is_equal, OP.mult, w + ["sm/ke0"], ["sm/f2"])
+                tt(sm[:, 52:56], sm[:, 40:44], sm[:, 36:40], OP.add, ["sm/n12", "sm/n2"], ["sm/nb"])
+            else:
+                ts(sm[:, 56:57], ke[2], -1.0, ke[1], OP.mult, OP.add, ["sm/ke2", "sm/ke1"], ["sm/d"])
+                ts(sm[:, 57:58], ke[2], -320.0625 * UNIT, None, OP.add, None, ["sm/ke2"], ["sm/d2"])
+                ts(sm[:, 60:64], sm[:, 44:48], ke[2], None, OP.mult, None, ["sm/l3", "sm/ke2"], ["sm/lk"])
+                ts(sm[:, 64:68], em[2], ke[2], sm[:, 56:57], OP.is_equal, OP.mult, w + ["sm/d"], ["sm/fa"])
+                ts(sm[:, 68:72], em[2], ke[2], sm[:, 57:58], OP.is_equal, OP.mult, w + ["sm/d2"], ["sm/na"])
+                tt(sm[:, 72:76], sm[:, 60:64], sm[:, 32:36], OP.add, ["sm/lk", "sm/f2"], ["sm/f"])
+                tt(T.tab[:, 4:8], sm[:, 52:56], sm[:, 68:72], OP.add, ["sm/nb", "sm/na"], ["tab/n"])
+                tt(T.tab[:, 0:4], sm[:, 72:76], sm[:, 64:68], OP.add, ["sm/f", "sm/fa"], ["tab/f"])
+        tabs = ["tab/f", "tab/n"]
+        cp(T.te[:], T.tab[:, 0:8].indirect(T.xl[:, 0:3]), tabs + ["xl"], ["te"])
+        tt(T.pl[:, 0:20], T.te[:, 0:20], T.sc[:], OP.add, ["te", "sc"], ["pl/a"])
+        tt(T.pl[:, 20:40], T.pl[:, 0:20], T.te[:, 20:40], OP.is_lt, ["pl/a", "te"], ["pl/b"])
+        tt(T.pl[:, 40:60], T.pl[:, 0:20], T.pl[:, 20:40], OP.mult, ["pl/a", "pl/b"], ["pl/c"])
+        ts(T.off16[:], T.pl[:, 40:60], 1.0 / UNIT, None, OP.mult, None, ["pl/c"], ["off16"])
+        cp(T.wsl[:, 0:320], T.wrow[:, 0:336].indirect(T.off16[:, 0:20]), ["wrow", "off16"], ["wsl/s"])
+        scan(T.ox[:], T.k4[:], T.wsl[:], 0.0, OP.add, OP.max, ["k4", "wsl"], ["ox"])
+        cp(T.oi[:, 0:100], T.ox[:, 3:400:4], ["ox"], ["oi/a"])
+        ts(T.oi[:, 100:200], T.oi[:, 0:100], 511, None, OP.bitwise_and, None, ["oi/a"], ["oi/b"])
+        ts(T.off4[:], T.oi[:, 100:200], 4.0, T.pc[:, 1:2], OP.mult, OP.add, ["oi/b", "pc/0"], ["off4"])
+        win = xa[:, 0:1296]
+
+        def take(eng, lo, n):
+            o, i = T.btile[:, 4 * lo:4 * lo + 4 * n], win.indirect(T.off4[:, lo // 4:(lo + n) // 4])
+            k = ["btile/%d" % lo]
+            if eng == "V":
+                cp(o, i, [X, "off4"], k)
+            else:
+                act(o, i, AF.Copy, [X, "off4"], k)
+        came, back = "came%d" % r, "back%d" % r
+        take("A", 0, 120)
+        take("V", 120, 120)
+        quant("qb", 0, 240, "btile", 0, ["btile/0", "btile/120"])
+        send("qb", came, 1)
+        if r == 0:
+            first_flight_constants()
+        take("A", 240, 80)
+        quant("qbo", 0, 128, "btile", 960, ["btile/240", "btile/pad"])
+        act(T.eh[:, 0:320], win.indirect(T.off4[:, 80:100]), AF.Copy, [X, "off4"], ["eh/0"], scale=0.5)
+        for b in range(4):
+            mm(4 + b, 128, "qun", 128 * b, "qbo", 0)
+        for b in range(4):
+            tt(T.z0[:, b:320:4], T["p%d" % (4 + b)][:, 0:80], T.eh[:, b:320:4], OP.add, ["p%d" % (4 + b), "eh/0"],
+               ["z0/%d" % b])
+        act(T.eh[:, 320:640], T.eh[:, 0:320], AF.Copy, ["eh/0"], ["eh/1"])
+        act(T.eh[:, 640:960], T.eh[:, 0:320], AF.Copy, ["eh/0"], ["eh/2"])
+        quant("qzo", 0, 128, "z0", 0, ["z0"])
+        for b in range(4):
+            mm(b, 128, "wq", 128 * b, "qzo", 0)
+        for b in range(4):
+            act(T.h0[:, b:320:4], T["p%d" % b][:, 0:80], AF.Copy, ["p%d" % b], ["h0/%d" % b], scale=0.03125)
+        for b in range(4):
+            mm(4 + b, 240, "qun", 128 * b, came, 0)
+        for b in range(4):
+            tt(T.z1[:, b:960:4], T["p%d" % (4 + b)][:, 0:240], T.eh[:, b:960:4], OP.add, ["p%d" % (4 + b), "eh"],
+               ["z1/%d" % b])
+        quant("qz1", 0, 240, "z1", 0, ["z1"])
+        for b in range(4):
+            mm(b, 240, "wq", 128 * b, "qz1", 0)
+        for b in range(4):
+            o, i = T.h1[:, b:960:4], T["p%d" % b][:, 0:240]
+            if b % 2:
+                ts(o, i, 0.03125, None, OP.mult, None, ["p%d" % b], ["h1/%d" % b])
+            else:
+                act(o, i, AF.Copy, ["p%d" % b], ["h1/%d" % b], scale=0.03125)
+        quant("qh", 0, 240, "h1", 0, ["h1"])
+        send("qh", back, -1)
+        quant("qho", 0, 128, "h0", 0, ["h0"])
+        for b in range(4):
+            mm(4 + b, 128, "qun", 128 * b, "qho", 0)
+        if r == 0:
+            second_flight_constants()
+        ts(sm[:, 80:84], T.tab[:, 4:8], -16.0 * UNIT, None, OP.add, None, tabs, ["sm/la"])
+        ts(sm[:, 84:88], T.tab[:, 0:4], 80.0 * UNIT, None, OP.add, None, tabs, ["sm/lb"])
+        cp(T.tab[:, 8:12], T.tab[:, 0:4], tabs, ["tab/g"])
+        tt(T.tab[:, 12:16], sm[:, 80:84], sm[:, 84:88], OP.min, ["sm/la", "sm/lb"], ["tab/l"])
+        for k in range(4):
+            ts(T.rks[:, 20 * k:20 * k + 20], T.rk[:], -15.875, UNIT, OP.add, OP.mult, ["rk"], ["rks/%d" % k])
+        cp(T.tf[:], T.tab[:, 8:16].indirect(T.l80[:, 0:10]), ["tab/g", "tab/l", "l80"], ["tf"])
+        s1, s2 = T.sl1, T.sl2
+        tt(s1[:, 0:80], T.rks[:], T.tf[:, 80:160], OP.is_lt, ["rks", "tf"], ["sl1/a"])
+        tt(s1[:, 80:160], T.rks[:], T.tf[:, 0:80], OP.is_ge, ["rks", "tf"], ["sl1/b"])
+        tt(s1[:, 160:240], T.rks[:], T.tf[:, 0:80], OP.subtract, ["rks", "tf"], ["sl1/c"])
+        tt(s1[:, 240:320], s1[:, 0:80], s1[:, 80:160], OP.mult, ["sl1/a", "sl1/b"], ["sl1/d"])
+        ts(s1[:, 320:400], s1[:, 160:240], 1.0 / UNIT, None, OP.mult, None, ["sl1/c"], ["sl1/e"])
+        tt(T.pl[:], s1[:, 320:400], T.kc[:], OP.add, ["sl1/e", "kc"], ["pl"])
+        tt(s1[:, 0:80], T.pl[:], s1[:, 240:320], OP.mult, ["pl", "sl1/d"], ["sl1/a"])
+        tt(s2[:, 0:40], s1[:, 0:40], s1[:, 40:80], OP.add, ["sl1/a"], ["sl2/a"])
+        tt(s2[:, 40:60], s2[:, 0:20], s2[:, 20:40], OP.add, ["sl2/a"], ["sl2/b"])
+        ts(s2[:, 60:80], s2[:, 40:60], 320.0, None, OP.add, None, ["sl2/b"], ["sl2/c"])
+        cp(T.po[:], s2[:, 60:80], ["sl2/c"], ["po"])
+        for t in range(4):
+            ts(T.po16[:, 20 * t:20 * t + 20], T.po[:], 4.0, float(t), OP.mult, OP.add, ["po"], ["po16/%d" % t])
+        for b in range(4):
+            o, i = T.bk[:, 960 + b:1280:4], T["p%d" % (4 + b)][:, 0:80]
+            act(o, i, AF.Copy, ["p%d" % (4 + b)], ["bk/own%d" % b], scale=2.0)
+        if r == NR - 1:
+            ts(T.rc[:, 0:240], T.ij[:, 0:240], 80.0, None, OP.add, None, ["ij"], ["rc/a"])
+            ts(T.rc[:, 240:320], T.ij[:, 240:320], -240.0, None, OP.add, None, ["ij"], ["rc/b"])
+            fill(T.rc[:, 320:336], -1.0, ["rc/c"])
+            cp(T.po16[:, 80:100], T.po[:], ["po"], ["po16/s"])
+            act(T.eq[:], T.rc[:, 0:336].indirect(T.po16[:, 80:100]), AF.Copy, ["rc", "po16/s"], ["eq"])
+            for q in range(8):
+                dma("S", lambda e, q=q: e.dma_start(T.sl[q:q + 1, :], T.eq[16 * q:16 * q + 1, :]), ("out", 0),
+                    ["eq"], [])
+            quant("qv", 0, 128, "vt", 0, ["vt"])
+        for b in range(4):
+            mm(b, 240, "qun", 128 * b, back, 0)
+        for b in range(4):
+            o, i = T.bk[:, b:960:4], T["p%d" % b][:, 0:240]
+            if b % 2:
+                ts(o, i, 2.0, None, OP.mult, None, ["p%d" % b], ["bk/%d" % b])
+            else:
+                act(o, i, AF.Copy, ["p%d" % b], ["bk/%d" % b], scale=2.0)
+        for t in range(4):
+            tt(xn[:, t:1280:4], T.bk[:, 0:1296].indirect(T.po16[:, 20 * t:20 * t + 20]), xa[:, t:1280:4], OP.add,
+               ["bk", "po16/%d" % t, X], [XN + "/x%d" % t])
+
+    X = "x%d" % NR
+    quant("qx", 0, 320, X, 0, [X + "/x%d" % t for t in range(4)])
+    mm(4, 320, "qv", 0, "qx", 0)
+    dma("S", lambda e: e.dma_start(T.oc[:], T.qx[:].bitcast(dt.uint8)), ("out", 0), ["qx"], [])
+    for k in range(4):
+        dma("S", lambda e, k=k: e.dma_start(T.osc[4 * k:4 * k + 4, :], T.qxs[32 * k:32 * k + 4, :]), ("out", 0),
+            ["qxs"], [])
+    act(T.d1[:], T.p4[:, 0:320], AF.Copy, ["p4"], ["d1"])
+    dma("A", lambda e: e.dma_start(T.y[:], T.d1[:]), ("out", 0), ["d1"], [])
+    g.wait_ge(T.sem.out, 16 * (8 + 1 + 4 + 1))
+    for n in sorted(lsn):
+        g.wait_ge(T.sem["l" + n], lsn[n])

@@ -7,6 +7,9 @@ UNIT = 2.0 ** 20
 NEG = 2.0 ** 97
 B16 = 1024.0
 B4 = 2.0 ** 21
+CUT = ((46, 128), (101, 224), (174, 288))
+CT = (0, 320, 576, 768, 896, 1024)
+ALONE = (16, 15)
 
 
 def _scratch():
@@ -19,29 +22,30 @@ def _scratch():
     def code(n, w):
         s[n] = ("sbuf", [128, w], F8)
         s[n + "s"] = ("sbuf", [128, w], U8)
-    sb(BF, x0=1296, x1=1296, x2=1296, ut=512, vt=512, eg=512, one=512, half=512, id4=512, un=2048, btile=1472, eh=960,
-       z0=512, h0=512, z1=960, h1=960, bk=1296, junk=1280, ct0=1280, ct1=1280, ct2=1280)
-    for n, w in (("qu", 128), ("qur", 128), ("qv", 128), ("wq", 512), ("qx", 320), ("qeg", 128), ("qun", 512),
-                 ("qbo", 128), ("qzo", 128), ("qho", 128), ("qz1", 240), ("qb", 240), ("qh", 240),
-                 ("qc0", 320), ("qc1", 320), ("qc2", 320)):
+    sb(BF, x0=2560, x1=2560, x2=1280, xs=1296, ut=512, vt=512, eg=512, one=528, id4=512, uo=528, uh=528, bt=1472,
+       eh=320, z=1472, h=1472, junk=1280, sg=640, ct=4096)
+    for n, w in (("qu", 128), ("qur", 128), ("qv", 128), ("wq", 512), ("qx", 320), ("qeg", 128), ("quh", 512),
+                 ("quo", 512), ("qz", 512), ("qc", 1024)):
         code(n, w)
     for r in range(NR):
         for n in ("came", "back"):
-            code("%s%d" % (n, r), 240)
-    sb(F32, i16=320, i4=400, ij=336, mm=320, d0=320, rs=320, k16=320, k4=400, ta=400, tb=400, d1=320,
-       st=320, eq=320, rc=336, rcb=20, pc=8, v4=320, wrow=336, cw=328, on=320, rx=320, rk=20, acc=8, rsum=32, ncq=20,
-       gg=48, ee=48, iw=336, lm=24, sm=128, tab=16, te=48, sc=20, pl=80, wsl=400, ox=400, tf=160, rks=80, kc=80,
-       sl1=400, sl2=80)
-    sb(I32, pi=8, xi=64, oi=200, po=20)
-    sb(U16, ul=8, xl=4, l80=10, rk16=20, e16=8, off16=20, off4=100, po16=100)
+            code("%s%d" % (n, r), 368)
+        for n in ("qb", "qh"):
+            code("%s%d" % (n, r), 384)
+    sb(F32, i16=320, i4=320, ij=320, mm=320, d0=320, rs=320, k16=320, k4=320, d1=320, st=320, eq=320, rc=320,
+       rcb=20, pc=8, v4=320, wrow=320, cw=656, on=320, rx=320, rk=20, acc=8, rsum=32, ox=320, cst=8, fm=32, m2=32,
+       m3=16, g1=32, g2=32, g3=16, sm=64, ge=8, ta=8, tb=8, cz=20, ncs=20, old=20, kc=4, ya=80, za=80, wa=80, sa=80,
+       sc=80, se=80, sf=80, it=640, slt=640)
+    sb(I32, pi=8, xi=8, oi=160)
+    sb(U16, ul=8, rk16=20, e16=8, ol=80, ob=80, po16=100)
     for b in range(8):
         s["p%d" % b] = ("psum", [128, 512], F32)
     return s
 
 
 SCRATCH = _scratch()
-SEMAPHORES = (["sV", "sA", "sP", "sG", "gd", "lqb", "lqh", "dx", "du", "dw", "dv", "out"]
-              + [p + str(r) for p in ("came", "back") for r in range(NR)])
+SEMAPHORES = (["sV", "sA", "sP", "sG", "gd", "ls", "dx", "du", "dw", "dv", "out"]
+              + ["%s%d_%d" % (p, r, i) for p in ("came", "back") for r in range(NR) for i in (1, 2, 3)])
 
 
 def tracker(g, T):
@@ -115,7 +119,10 @@ def tracker(g, T):
 
     def arrive(tok, writes):
         note("far", tok, [], writes)
-    return tr, dma, remote, arrive
+
+    def finish():
+        wait("G", {sem[q]: count[q] for q in sem if count[q]})
+    return tr, dma, remote, arrive, finish
 
 
 def rank_program(g, core, T, topo):
@@ -123,7 +130,7 @@ def rank_program(g, core, T, topo):
     if rank is None:
         return
     N = len(T.cores)
-    tr, dma, remote, arrive = tracker(g, T)
+    tr, dma, remote, arrive, finish = tracker(g, T)
 
     def V(fn, r, w):
         tr("V", fn, r, w)
@@ -143,6 +150,9 @@ def rank_program(g, core, T, topo):
     def scan(out, a, b, init, op0, op1, r, w):
         V(lambda e: e.tensor_tensor_scan(out, a, b, init, op0, op1), r, w)
 
+    def most(out, in_, r, w):
+        V(lambda e: e.tensor_reduce(out, in_, AxisListType.X, OP.max), r, w)
+
     def fill(ap, c, w):
         V(lambda e: e.memset(ap, c), [], w)
 
@@ -155,18 +165,23 @@ def rank_program(g, core, T, topo):
         else:
             tr("G", lambda e: e.iota(out, pat, base, cm), [], w)
 
-    def select(out, in_, pat, op, base, cm, r, w):
-        tr("G", lambda e: e.affine_select(out, in_, pat, op, 0.0, base, cm), r, w)
+    def select(out, in_, pat, op, base, cm, r, w, c=0.0):
+        tr("G", lambda e: e.affine_select(out, in_, pat, op, c, base, cm), r, w)
 
-    def quant(name, a, b, src, lo, r):
+    def keys(n, subs):
+        if subs is None:
+            return [n, n + "s"]
+        return [n + x + "/" + str(s) for s in subs for x in ("", "s")]
+
+    def quant(name, a, b, src, lo, r, sub=None):
         V(lambda e: e.quantize_mx(T[name][:, a:b], T[name + "s"][:, a:b], T[src][:, lo:lo + 4 * (b - a)]),
-          r, [name, name + "s"])
+          r, keys(name, sub))
 
-    def mm(bank, n, sta, sa, mov, ma, start=True, stop=True):
+    def mm(bank, n, sta, sa, mov, ma, start=True, stop=True, ssub=None, msub=None):
         p = "p%d" % bank
         tr("P", lambda e: e.matmul_mx(T[p][:, 0:n], T[sta][:, sa:sa + 128], T[sta + "s"][:, sa:sa + 128],
                                       T[mov][:, ma:ma + n], T[mov + "s"][:, ma:ma + n], start, stop),
-           [sta, sta + "s", mov, mov + "s"], [p], acc=not start)
+           keys(sta, ssub) + keys(mov, msub), [p], acc=not start)
 
     dma("S", lambda e: e.dma_start(T.x0[:, 0:1280], T.x[:]), ("dx", 16), [], ["x0/x"])
     dma("A", lambda e: e.dma_start(T.ut[:], T.u[:]), ("du", 16), [], ["ut"])
@@ -175,360 +190,364 @@ def rank_program(g, core, T, topo):
     dma("S", lambda e: e.dma_start(T.vt[:], T.v[:]), ("dv", 16), [], ["vt"])
 
     iota(T.pi[:, 0:1], [[0, 1]], 0, 1, ["pi/0"], False)
-    iota(T.xi[:, 0:8], [[16, 8]], 4, 0, ["xi/u"], False)
+    iota(T.xi[:, 0:8], [[16, 8]], 4, 0, ["xi"], False)
     iota(T.i16[:], [[0, 20], [1, 16]], 0, 0, ["i16"])
-    iota(T.i4[:], [[0, 100], [1, 4]], 0, 0, ["i4"])
-    iota(T.ij[:], [[1, 336]], 0, 0, ["ij"])
     fill(T.one[:], 1.0, ["one"])
-    select(T.id4[:], T.one[:], [[-16, 8], [0, 64]], OP.is_ge, 0, 1, ["one"], ["id4"])
+    select(T.id4[:], T.one[:, 0:512], [[-16, 8], [0, 64]], OP.is_ge, 0, 1, ["one"], ["id4"])
+    iota(T.ij[:], [[1, 320]], 0, 0, ["ij"])
     select(T.eg[:], T.id4[:], [[16, 8], [0, 64]], OP.is_ge, 15, -1, ["id4"], ["eg"])
-    iota(T.sl1[:, 0:20], [[0, 4], [16, 5]], 0, 0, ["sl1"])
-    iota(T.xi[:, 8:11], [[16, 3]], 0, 0, ["xi/a"], False)
-    iota(T.xi[:, 16:26], [[16, 10]], 0, 0, ["xi/b"], False)
 
-    cp(T.ul[:], T.xi[:, 0:8], ["xi/u"], ["ul"])
+    cp(T.ul[:], T.xi[:], ["xi"], ["ul"])
     ts(T.pi[:, 1:2], T.pi[:, 0:1], 15, None, OP.bitwise_and, None, ["pi/0"], ["pi/1"])
     ts(T.pi[:, 2:3], T.pi[:, 0:1], 3, None, OP.bitwise_and, None, ["pi/0"], ["pi/2"])
+    for b in range(5):
+        fill(T.ct[:, 4 * (CT[b + 1] - (48 if b < 4 else 112)):4 * CT[b + 1]], 0.0, ["ct/z%d" % b])
     ts(T.pi[:, 3:4], T.pi[:, 1:2], 2, None, OP.logical_shift_right, None, ["pi/1"], ["pi/3"])
+    fill(T.rsum[:, 0:1], 0.0, ["rsum/0"])
+    fill(T.m2[:], 0.0, ["m2"])
     cp(T.pc[:, 0:3], T.pi[:, 1:4], ["pi"], ["pc/0"])
+    fill(T.m3[:], 0.0, ["m3"])
+    fill(T.cw[:, 320:336], 0.0, ["cw/z"])
+    fill(T.xs[:, 0:16], 0.0, ["xs/z"])
+    ts(T.pc[:, 3:4], T.pc[:, 0:1], 1.0 - B16, 15 * B16 - 15.0, OP.mult, OP.add, ["pc/0"], ["pc/3"])
+    for s in range(3):
+        lo, hi = CUT[s]
+        fill(T.cst[:, 2 * s:2 * s + 1], float(lo + hi - 2), ["cst/%da" % s])
+        fill(T.cst[:, 2 * s + 1:2 * s + 2], float(lo + hi - 2 + 672), ["cst/%db" % s])
     ts(T.mm[:], T.i16[:], T.pc[:, 0:1], -2.0 * NEG, OP.not_equal, OP.mult, ["i16", "pc/0"], ["mm"])
-    ts(T.d0[:], T.i16[:], 2.0 * NEG, -NEG, OP.mult, OP.add, ["i16"], ["d0"])
-    act(T.rs[:], T.i16[:], AF.Sign, ["i16"], ["rs"])
-    act(T.tb[:, 0:320], T.rs[:], AF.Copy, ["rs"], ["tb"], scale=32 * B16, bias=-33 * B16)
-    ts(T.ta[:, 0:320], T.i16[:], T.pc[:, 0:1], 2 * B16, OP.is_gt, OP.mult, ["i16", "pc/0"], ["ta"])
-    tt(T.k16[:], T.ta[:, 0:320], T.tb[:, 0:320], OP.add, ["ta", "tb"], ["k16"])
+    ts(T.k16[:], T.i16[:], T.pc[:, 0:1], 34 * B16, OP.is_gt, OP.mult, ["i16", "pc/0"], ["k16"])
+    act(T.d0[:], T.i16[:], AF.Copy, ["i16"], ["d0"], scale=2.0 * NEG, bias=-NEG)
+    act(T.fm[:, 0:16], T.i16[:, 0:16], AF.Copy, ["i16"], ["fm/a"], scale=0.0, bias=1.0)
+    act(T.fm[:, 16:32], T.i16[:, 0:16], AF.Copy, ["i16"], ["fm/b"], scale=-2.0 ** -16, bias=1.0)
+    act(T.kc[:], T.i16[:, 0:4], AF.Copy, ["i16"], ["kc"], scale=320.0, bias=1279.0)
+    act(T.on[:], T.i16[:], AF.Copy, ["i16"], ["on"], scale=0.0, bias=-UNIT)
     quant("qu", 0, 128, "ut", 0, ["ut"])
     cp(T.qur[:].bitcast(dt.uint32), T.qu[:].bitcast(dt.uint32).indirect(T.ul[:, 0:8]), ["qu", "ul"], ["qur"])
-    act(T.on[:], T.i16[:], AF.Copy, ["i16"], ["on"], scale=0.0, bias=UNIT)
-    act(T.cw[:, 0:320], T.i16[:], AF.Copy, ["i16"], ["cw/a"], scale=0.0, bias=0.125 * UNIT)
-    act(T.cw[:, 320:328], T.i16[:, 0:8], AF.Copy, ["i16"], ["cw/b"], scale=0.0, bias=0.125 * UNIT)
     act(T.qurs[:], T.qus[:].indirect(T.ul[:, 0:8]), AF.Copy, ["qus", "ul"], ["qurs"])
-    act(T.ct2[:, 3:1280:4], T.i16[:], AF.Copy, ["i16"], ["ct2/n"], scale=0.0)
-    act(T.half[:], T.one[:], AF.Copy, ["one"], ["half"], scale=0.5)
-    for c in range(10):
-        act(T["ct%d" % (c // 4)][:, 64 * c + c % 4:64 * c + 64:4], T.i16[:, 0:16], AF.Copy, ["i16"],
-            ["ct%d/h%d" % (c // 4, c)], scale=0.0)
-    act(T.ox[:], T.i4[:], AF.Sign, ["i4"], ["ox"])
-    act(T.wsl[:], T.ox[:], AF.Copy, ["ox"], ["wsl"], scale=8 * B4, bias=-9 * B4)
-    act(T.wrow[:], T.ij[:], AF.Copy, ["ij"], ["wrow"], scale=0.0, bias=320.0)
-    fill(T.x0[:, 1280:1296], 0.0, ["x0/z"])
-    select(T.id4[:], T.half[:], [[-1, 128], [0, 4]], OP.is_equal, 0, 1, ["half"], ["id4"])
+    act(T.k16[:], T.k16[:], AF.Copy, ["k16"], ["k16"], bias=-33 * B16)
+    for n in ("bt", "z", "h"):
+        act(T[n][:, 0:192], T.i16[:, 0:192], AF.Copy, ["i16"], [n + "/pad"], scale=0.0)
 
-    def unpack_constants():
-        for b in range(4):
-            select(T.un[:, 512 * b:512 * b + 512], T.id4[:], [[0, 128], [1, 4]], OP.is_equal, -b, 0, ["id4"],
-                   ["un/%d" % b])
+    def late_constants():
+        iota(T.rs[:], [[-16, 20], [32767, 16]], 0, 0, ["rs"])
+        iota(T.i4[:], [[0, 80], [1, 4]], 0, 0, ["i4"])
+        iota(T.cw[:, 336:656], [[-4, 320]], 1276, 0, ["cw/i"])
+        select(T.uo[:], T.one[:], [[1, 528]], OP.is_equal, -3, -4, ["one"], ["uo"])
 
-    def product_constants():
-        for j in range(4):
-            fill(T.lm[:, j:j + 1], (-0.3125 + j / 64.0) * UNIT, ["lm/0"])
-        fill(T.rsum[:, 19:21], 0.0, ["rsum/z"])
+    gdn, jn, lsn = [0], [0], [0]
 
-    def order_constants():
-        ts(T.pc[:, 3:4], T.pc[:, 0:1], 1.0 - B16, 15 * B16 - 191.0, OP.mult, OP.add, ["pc/0"], ["pc/3"])
-        ts(T.pc[:, 4:5], T.pc[:, 0:1], 1.0 - B16, 15 * B16 - 175.0, OP.mult, OP.add, ["pc/0"], ["pc/4"])
-        ts(T.ncq[:, 0:10], T.i4[:, 0:10], 0.0, T.pc[:, 3:4], OP.mult, OP.add, ["i4", "pc/3"], ["ncq/a"])
-        ts(T.ncq[:, 10:20], T.i4[:, 0:10], 0.0, T.pc[:, 4:5], OP.mult, OP.add, ["i4", "pc/4"], ["ncq/b"])
-
-    def claim_constants():
-        act(T.iw[:], T.ij[:], AF.Copy, ["ij"], ["iw"], scale=UNIT, bias=0.375 * UNIT)
-        ts(T.ta[:], T.i4[:], T.pc[:, 2:3], 2 * B4, OP.is_gt, OP.mult, ["i4", "pc/0"], ["ta"])
-        ts(T.sl2[:, 0:3], T.xi[:, 8:11], T.pc[:, 0:1], 13.0, OP.add, OP.mult, ["xi/a", "pc/0"], ["sl2/a"])
-        ts(T.sc[:], T.sl1[:, 0:20], T.pc[:, 0:1], 16.125, OP.add, OP.add, ["sl1", "pc/0"], ["sc"])
-        cp(T.xi[:, 28:31], T.sl2[:, 0:3], ["sl2/a"], ["xi/c"])
-        tt(T.k4[:], T.ta[:], T.wsl[:], OP.add, ["ta", "wsl"], ["k4"])
-        ts(T.xi[:, 44:47], T.xi[:, 28:31], 6, None, OP.logical_shift_right, None, ["xi/c"], ["xi/e"])
-        ts(T.sc[:], T.sc[:], UNIT, None, OP.mult, None, ["sc"], ["sc"])
-        fill(T.btile[:, 1280:1472], 0.0, ["btile/pad"])
-        ts(T.xi[:, 8:11], T.xi[:, 44:47], 1.0, None, OP.add, None, ["xi/e"], ["xi/a"])
-        ts(T.xi[:, 60:63], T.xi[:, 44:47], 4, None, OP.bitwise_and, None, ["xi/e"], ["xi/g"])
-        ts(T.xi[:, 28:31], T.xi[:, 8:11], 3, None, OP.bitwise_and, None, ["xi/a"], ["xi/c"])
-        tt(T.xi[:, 8:11], T.xi[:, 28:31], T.xi[:, 60:63], OP.add, ["xi/c", "xi/g"], ["xi/a"])
-        cp(T.xl[:, 0:3], T.xi[:, 8:11], ["xi/a"], ["xl"])
-
-    def first_flight_constants():
-        quant("qun", 0, 512, "un", 0, ["un"])
-        fill(T.z0[:, 320:512], 0.0, ["z0/pad"])
-        fill(T.h0[:, 320:512], 0.0, ["h0/pad"])
-
-    def second_flight_constants():
-        ts(T.sl2[:, 4:14], T.xi[:, 16:26], T.pc[:, 0:1], 205.0, OP.add, OP.mult, ["xi/b", "pc/0"], ["sl2/b"])
-        fill(T.bk[:, 1280:1296], 0.0, ["bk/z"])
-        cp(T.xi[:, 32:42], T.sl2[:, 4:14], ["sl2/b"], ["xi/d"])
-        for k in range(4):
-            fill(T.kc[:, 20 * k:20 * k + 20], 80.0 * ((k + 3) % 4) - 320.0, ["kc/%d" % k])
-        ts(T.xi[:, 48:58], T.xi[:, 32:42], 12, None, OP.logical_shift_right, None, ["xi/d"], ["xi/f"])
-        fill(T.x1[:, 1280:1296], 0.0, ["x1/z"])
-        cp(T.l80[:], T.xi[:, 48:58], ["xi/f"], ["l80"])
-
-    gdn, jn = [0], [0]
-    lsn = {"qb": 0, "qh": 0}
-
-    def send(src, dst, step):
-        got = 0
+    def send(src, i, dst, step):
+        to = T.cores[(rank + step * i) % N]
+        en = topo.engines(core, to)
+        mask = topo.mask(core, to)
+        ad = topo.addr(to)
+        a, b = 128 * i - 80, 48 + 80 * i
+        name = "%s_%d" % (dst, i)
         for planes in (False, True):
-            trs = []
-            for i in range(3):
-                to = T.cores[(rank + step * (i + 1)) % N]
-                en = topo.engines(core, to)
-                h = len(en) // 8
-                if planes:
-                    en = en[4 * h:6 * h] if i == 0 else en[6 * h:8 * h] if i == 1 else en[0:4 * h]
-                else:
-                    en = en[0:2 * h] if i == 0 else en[2 * h:4 * h] if i == 1 else en[4 * h:8 * h]
-                mask = 0
-                for x in en:
-                    mask |= 1 << x
-                ad = topo.addr(to)
-                a, b = 80 * i, 80 * i + 80
-                if planes:
-                    s_ap, d_ap = T[src + "s"][:, a:b], T[dst + "s"][:, a:b]
-                else:
-                    s_ap, d_ap = T[src][:, a:b].bitcast(dt.uint8), T[dst][:, a:b].bitcast(dt.uint8)
-                trs.append(RemoteDMATransfer(dst_ids=[DstId(rid=ad[0], pnc=ad[1])], dma_engine_mask=mask,
-                                             remote_sem=T.sem[dst], src=s_ap, dst=d_ap))
-                lsn[src] += len(en)
-                got += len(en)
-            remote(lambda e: e.remote_dma_fused(trs, local_sem=T.sem["l" + src]), ("l" + src, lsn[src]),
-                   [src + "s"] if planes else [src])
-        arrive((dst, got), [dst, dst + "s"])
+            if planes:
+                s_ap, d_ap = T[src + "s"][:, a:a + 80], T[dst + "s"][:, b:b + 80]
+            else:
+                s_ap, d_ap = T[src][:, a:a + 80].bitcast(dt.uint8), T[dst][:, b:b + 80].bitcast(dt.uint8)
+            lsn[0] += len(en)
+            remote(lambda e: e.remote_dma(d_ap, s_ap, T.sem[name], T.sem.ls, ad[1], ad[0], mask), ("ls", lsn[0]),
+                   ["%s%s/%d" % (src, "s" if planes else "", i)])
+        arrive((name, 2 * len(en)), keys(dst, [i]))
 
     for r in range(NR):
         X, XN = "x%d" % r, "x%d" % (r + 1)
         xa, xn = T[X], T[XN]
-        quant("qx", 0, 320, X, 0, [X])
+        xk = [X + "/x"] if r == 0 else [X + "/x%d" % t for t in range(4)]
+        came, back, qb, qh = "came%d" % r, "back%d" % r, "qb%d" % r, "qh%d" % r
+        quant("qx", 0, 320, X, 0, xk)
         mm(0, 320, "qur", 0, "qx", 0)
         mm(2, 320, "qu", 0, "qx", 0)
-        if r == 0:
-            product_constants()
+        mm(1, 320, "qur", 0, "qx", 0)
         tt(T.d1[:], T.p0[:, 0:320], T.mm[:], OP.add, ["p0", "mm"], ["d1"])
         scan(T.st[:], T.d0[:], T.d1[:], -NEG, OP.min, OP.max, ["d0", "d1"], ["st"])
         act(T.v4[:], T.p2[:, 0:320], AF.Sign, ["p2"], ["v4"])
-        act(T.v4[:], T.v4[:], AF.Relu, ["v4"], ["v4"], scale=UNIT)
+        act(T.v4[:], T.v4[:], AF.Relu, ["v4"], ["v4", "acc/t"], scale=UNIT, accum_out=T.acc[:, 4:5])
         gdn[0] += 16
-        dma("G", lambda e: e.dma_start(T.v4[:], T.ij[:, 0:320], accum_op=OP.add), ("gd", gdn[0]), ["ij"], ["v4"])
+        dma("G", lambda e: e.dma_start(T.v4[:], T.ij[:], accum_op=OP.add), ("gd", gdn[0]), ["ij"], ["v4"])
         if r == 0:
-            unpack_constants()
+            late_constants()
+        if r == NR - 1:
+            iota(T.it[:], [[1, 640]], -320, 0, ["it"])
+            select(T.slt[:], T.it[:], [[1, 640]], OP.is_ge, -320, 0, ["it"], ["slt"], -1.0)
+
+        def place(c):
+            b, t = (20 - c) // 4, (20 - c) % 4
+            return T.ct[:, 4 * CT[b] + t:4 * (CT[b] + 16 * c):4], "ct/%d" % c
+
+        def own(c):
+            return T.st[:, 16 * c + 15:16 * c + 16]
 
         def compare(c):
-            n, t = "ct%d" % (c // 4), c % 4
-            for (k, lo, hi, op, col) in ((c, c + 1, c + 11, OP.is_le, c), (c + 10, c + 11, 20, OP.is_le, 10 + c),
-                                         (c + 10, 0, c, OP.is_lt, 20 + c)):
-                if lo < hi:
-                    o, key = T[n][:, 64 * lo + t:64 * hi:4], "%s/%d" % (n, col)
-                    ts(o, T.p0[:, 16 * lo:16 * hi], T.st[:, 16 * k + 15:16 * k + 16], None, op, None, ["p0", "st"],
-                       [key])
-                    jn[0] = (jn[0] + 1) % 8
-                    act(T.junk[:, 160 * jn[0]:160 * jn[0] + 16 * (hi - lo)], o, AF.Copy, [key],
-                        ["junk/%d" % jn[0], "rsum/%d" % col], accum_out=T.rsum[:, col:col + 1])
+            o, key = place(c)
+            ts(o, T.p0[:, 0:16 * c], own(c), None, OP.is_lt, None, ["p0", "st", "ct/z%d" % ((20 - c) // 4)], [key])
+
+        def rows(c):
+            o, key = place(c)
+            jn[0] = (jn[0] + 1) % 4
+            act(T.junk[:, 320 * jn[0]:320 * jn[0] + 16 * c], o, AF.Copy, [key], ["junk/%d" % jn[0], "rsum/%d" % c],
+                accum_out=T.rsum[:, c:c + 1])
+
+        def alone(cs):
+            for i, c in enumerate(cs):
+                act(T.sg[:, 320 * i:320 * i + 16 * c], T.p1[:, 0:16 * c], AF.Sign, ["p1", "st"], ["sg/%d" % i],
+                    scale=-1.0, bias=own(c))
+            for i, c in enumerate(cs):
+                o, key = place(c)
+                act(o, T.sg[:, 320 * i:320 * i + 16 * c], AF.Relu, ["sg/%d" % i, "ct/z%d" % ((20 - c) // 4)],
+                    [key, "rsum/%d" % c], accum_out=T.rsum[:, c:c + 1])
 
         def count(b):
-            quant("qc%d" % b, 0, 320, "ct%d" % b, 0, ["ct%d" % b])
-            mm(3, 320, "qeg", 0, "qc%d" % b, 0, b == 0, b == 2)
-        for c in range(4):
+            w = CT[b + 1] - CT[b]
+            quant("qc", CT[b], CT[b + 1], "ct", 4 * CT[b],
+                  ["ct/z%d" % b] + ["ct/%d" % (20 - 4 * b - t) for t in range(4)], [b])
+            mm(3, w, "qeg", 0, "qc", CT[b], b == 0, b == 4, msub=[b])
+        alone(ALONE)
+        act(T.acc[:, 5:6], T.acc[:, 4:5], AF.Copy, ["acc/t"], ["acc/T"], bias=319.6 * UNIT)
+        for c in (19, 18, 17):
             compare(c)
+            rows(c)
+        tt(T.ct[:, 0:1280:4], T.st[:], T.p0[:, 0:320], OP.is_ge, ["p0", "st", "ct/z0"], ["ct/20"])
         if r == 0:
             quant("qeg", 0, 128, "eg", 0, ["eg"])
         count(0)
+        for c in range(16, 0, -1):
+            if c not in ALONE:
+                compare(c)
+                rows(c)
+            if c % 4 == 1:
+                count((20 - c) // 4)
+            if r == 0 and c == 9:
+                ts(T.rs[:], T.rs[:], T.pc[:, 3:4], None, OP.add, None, ["rs", "pc/3"], ["rs"])
+        scan(T.rc[:], T.rs[:], T.ct[:, 0:1280:4], 1.0e6, OP.min, OP.add, ["rs", "ct/20"], ["rc"])
         if r == 0:
-            order_constants()
-        for c in range(4, 8):
-            compare(c)
-        count(1)
-        tt(T.ct2[:, 2:1280:4], T.st[:], T.p0[:, 0:320], OP.is_ge, ["p0", "st"], ["ct2/d"])
-        compare(8)
-        compare(9)
-        count(2)
-        scan(T.rc[:, 0:320], T.rs[:], T.ct2[:, 2:1280:4], 0.0, OP.mult, OP.add, ["rs", "ct2/d"], ["rc"])
-        tt(T.rcb[:], T.rc[:, 15:320:16], T.ncq[:], OP.add, ["rc", "ncq"], ["rcb"])
-        tt(T.rcb[:], T.rcb[:], T.rsum[:, 0:20], OP.add, ["rcb", "rsum/z"] + ["rsum/%d" % c for c in range(19)], ["rcb"])
-        tt(T.rcb[:, 10:20], T.rcb[:, 10:20], T.rsum[:, 20:30], OP.add,
-           ["rcb", "rsum/z"] + ["rsum/%d" % c for c in range(21, 30)], ["rcb"])
+            act(T.k4[:], T.i4[:], AF.Sign, ["i4", "pc/0"], ["k4"], scale=-1.0, bias=T.pc[:, 2:3])
+            act(T.k4[:], T.k4[:], AF.Relu, ["k4"], ["k4"], scale=-9 * B4)
+            act(T.k4[:], T.k4[:], AF.Copy, ["k4"], ["k4"], bias=-8 * B4)
+            ts(T.cz[:], T.ij[:, 0:320:16], T.pc[:, 0:1], 1296.0, OP.add, OP.add, ["ij", "pc/0"], ["cz"])
+        tt(T.rcb[:], T.rc[:, 15:320:16], T.rsum[:, 0:20], OP.add, ["rc", "rsum"], ["rcb"])
         scan(T.rx[:], T.k16[:], T.p3[:, 0:320], 0.0, OP.add, OP.max, ["k16", "p3"], ["rx"])
+        if r == 0:
+            ts(T.ncs[:], T.cz[:], -1.0, 1295.5, OP.mult, OP.add, ["cz"], ["ncs"])
         tt(T.rk[:], T.rx[:, 15:320:16], T.rcb[:], OP.subtract, ["rx", "rcb"], ["rk"])
         cp(T.rk16[:], T.rk[:], ["rk"], ["rk16"])
-        cp(T.wrow[:, 0:336].indirect(T.rk16[:, 0:20]), T.v4[:], ["rk16", "v4"], ["wrow"])
-        scan(T.cw[:, 1:321], T.wrow[:, 16:336], T.on[:], 0.125 * UNIT, OP.add, OP.add, ["wrow", "on"], ["cw"])
-        tot = T.cw[:, 320:321]
-        act(T.junk[:, 0:320], T.cw[:, 0:320], AF.Sign, ["cw"], ["junk/0", "junk/1", "acc/0"], bias=tot, scale=-4.0,
-            accum_out=T.acc[:, 0:1])
-        sm, lm = T.sm, T.lm
-        ts(sm[:, 20:21], tot, 0.5, None, OP.mult, None, ["cw"], ["sm/t2"])
-        ts(lm[:, 12:16], lm[:, 0:4], sm[:, 20:21], None, OP.add, None, ["lm/0", "sm/t2"], ["lm/t0"])
-        if r == 0:
-            claim_constants()
+        cp(T.wrow[:].indirect(T.rk16[:, 0:20]), T.v4[:], ["rk16", "v4"], ["wrow"])
+        scan(T.cw[:, 0:320], T.on[:], T.wrow[:], T.acc[:, 5:6], OP.add, OP.subtract, ["wrow", "on", "acc/T"],
+             ["cw/s"])
+        sm = T.sm
+        th = [T.acc[:, 5:6], sm[:, 0:1], sm[:, 1:2]]
+        ke = [sm[:, 2:3], sm[:, 3:4], sm[:, 4:5]]
+
+        def cut(s):
+            lo, hi = CUT[s]
+            act(T.junk[:, 320 * s:320 * s + hi - lo], T.cw[:, lo - 1:hi - 1], AF.Sign,
+                ["cw/s", "acc/T" if s == 0 else "sm/th%d" % s], ["junk/%d" % s, "acc/%d" % s],
+                bias=th[s], scale=-(4.0 - s) / (3.0 - s), accum_out=T.acc[:, s:s + 1])
 
         def ends(s):
-            ts(T.e16[:, 2 * s:2 * s + 1], T.acc[:, s:s + 1], 0.5, 160.0, OP.mult, OP.add, ["acc/%d" % s],
-               ["e16/%d" % s])
+            a = 2 * s + (s == 2)
+            ts(T.e16[:, 2 * s:2 * s + 2 * s + 2 - a], T.cst[:, a:2 * s + 2], T.acc[:, s:s + 1], 0.5, OP.subtract,
+               OP.mult, ["acc/%d" % s, "cst"], ["e16/%d" % s])
 
-        def show(buf, win, w, s):
-            cp(T[buf][:, 16 * s:16 * s + 16], T[win][:, 0:w].indirect(T.e16[:, 2 * s:2 * s + 1]),
-               [win, "e16/%d" % s], ["%s/%d" % (buf, s)])
-        ke = [sm[:, 0:1], sm[:, 1:2], sm[:, 2:3]]
-        em = [sm[:, 4:8], sm[:, 8:12], sm[:, 12:16]]
-        for s in range(3):
-            m = 4 - s
-            lmc = lm[:, 4 * s:4 * s + 4]
-            ends(s)
-            if s < 2:
-                show("gg", "cw", 328, s)
-                tt(sm[:, 16:20], T.gg[:, 16 * s:16 * s + 4], lm[:, 12 + 4 * s:16 + 4 * s], OP.add,
-                   ["gg/%d" % s, "lm/t%d" % s], ["sm/gm"])
-                V(lambda e, s=s: e.tensor_reduce(sm[:, 21 + s:22 + s], sm[:, 16:20], AxisListType.X, OP.min),
-                  ["sm/gm"], ["sm/th%d" % s])
-                act(T.junk[:, 320 * s + 320:320 * s + 640], T.cw[:, 0:320], AF.Sign, ["cw", "sm/th%d" % s],
-                    ["junk/%d" % (2 * s + 2), "junk/%d" % (2 * s + 3), "acc/%d" % (s + 1)],
-                    bias=sm[:, 21 + s:22 + s], scale=-float(m - 1) / (m - 2), accum_out=T.acc[:, s + 1:s + 2])
-                ts(sm[:, 24:28], sm[:, 16:20], sm[:, 21 + s:22 + s], 2.0 ** 32, OP.is_equal, OP.mult,
-                   ["sm/gm", "sm/th%d" % s], ["sm/w"])
-            show("ee", "iw", 336, s)
-            if s < 2:
-                tt(lm[:, 4 * s + 4:4 * s + 8], lmc, sm[:, 24:28], OP.add, ["sm/w", "lm/%d" % s],
-                   ["lm/%d" % (s + 1)])
-            tt(em[s], T.ee[:, 16 * s:16 * s + 4], lmc, OP.add, ["ee/%d" % s, "lm/%d" % s], ["sm/em%d" % s])
-            if s == 0:
-                ts(lm[:, 16:20], lm[:, 4:8], tot, None, OP.add, None, ["lm/1", "cw"], ["lm/t1"])
-            if s == 1:
-                ts(sm[:, 44:48], lm[:, 8:12], 2.0 ** 31, None, OP.is_lt, None, ["lm/2"], ["sm/l3"])
-            V(lambda e, s=s: e.tensor_reduce(ke[s], em[s], AxisListType.X, OP.min), ["sm/em%d" % s], ["sm/ke%d" % s])
-            w = ["sm/em%d" % s, "sm/ke%d" % s]
-            if s == 0:
-                act(T.wsl[:, 320:400], T.wrow[:, 16:96], AF.Copy, ["wrow"], ["wsl/e"])
-            elif s == 1:
-                ts(sm[:, 48:52], sm[:, 44:48], 320.0625 * UNIT, 16.0 * UNIT, OP.mult, OP.add, ["sm/l3"], ["sm/nl"])
-                ts(sm[:, 28:32], em[0], ke[0], ke[0], OP.is_equal, OP.mult, ["sm/em0", "sm/ke0"], ["sm/n1"])
-                ts(sm[:, 36:40], em[1], ke[1], ke[1], OP.is_equal, OP.mult, w, ["sm/n2"])
-                tt(sm[:, 40:44], sm[:, 28:32], sm[:, 48:52], OP.add, ["sm/n1", "sm/nl"], ["sm/n12"])
-                ts(sm[:, 32:36], em[1], ke[1], ke[0], OP.is_equal, OP.mult, w + ["sm/ke0"], ["sm/f2"])
-                tt(sm[:, 52:56], sm[:, 40:44], sm[:, 36:40], OP.add, ["sm/n12", "sm/n2"], ["sm/nb"])
+        def sort(lo, hi, eng="A"):
+            o, i = T.xs[:, 16 + 4 * lo:16 + 4 * hi], xa[:, 0:1280].indirect(T.ol[:, lo // 4:hi // 4])
+            if eng == "A":
+                act(o, i, AF.Copy, xk + ["ol"], ["xs/%d" % lo])
             else:
-                ts(sm[:, 56:57], ke[2], -1.0, ke[1], OP.mult, OP.add, ["sm/ke2", "sm/ke1"], ["sm/d"])
-                ts(sm[:, 57:58], ke[2], -320.0625 * UNIT, None, OP.add, None, ["sm/ke2"], ["sm/d2"])
-                ts(sm[:, 60:64], sm[:, 44:48], ke[2], None, OP.mult, None, ["sm/l3", "sm/ke2"], ["sm/lk"])
-                ts(sm[:, 64:68], em[2], ke[2], sm[:, 56:57], OP.is_equal, OP.mult, w + ["sm/d"], ["sm/fa"])
-                ts(sm[:, 68:72], em[2], ke[2], sm[:, 57:58], OP.is_equal, OP.mult, w + ["sm/d2"], ["sm/na"])
-                tt(sm[:, 72:76], sm[:, 60:64], sm[:, 32:36], OP.add, ["sm/lk", "sm/f2"], ["sm/f"])
-                tt(T.tab[:, 4:8], sm[:, 52:56], sm[:, 68:72], OP.add, ["sm/nb", "sm/na"], ["tab/n"])
-                tt(T.tab[:, 0:4], sm[:, 72:76], sm[:, 64:68], OP.add, ["sm/f", "sm/fa"], ["tab/f"])
-        tabs = ["tab/f", "tab/n"]
-        cp(T.te[:], T.tab[:, 0:8].indirect(T.xl[:, 0:3]), tabs + ["xl"], ["te"])
-        tt(T.pl[:, 0:20], T.te[:, 0:20], T.sc[:], OP.add, ["te", "sc"], ["pl/a"])
-        tt(T.pl[:, 20:40], T.pl[:, 0:20], T.te[:, 20:40], OP.is_lt, ["pl/a", "te"], ["pl/b"])
-        tt(T.pl[:, 40:60], T.pl[:, 0:20], T.pl[:, 20:40], OP.mult, ["pl/a", "pl/b"], ["pl/c"])
-        ts(T.off16[:], T.pl[:, 40:60], 1.0 / UNIT, None, OP.mult, None, ["pl/c"], ["off16"])
-        cp(T.wsl[:, 0:320], T.wrow[:, 0:336].indirect(T.off16[:, 0:20]), ["wrow", "off16"], ["wsl/s"])
-        scan(T.ox[:], T.k4[:], T.wsl[:], 0.0, OP.add, OP.max, ["k4", "wsl"], ["ox"])
-        cp(T.oi[:, 0:100], T.ox[:, 3:400:4], ["ox"], ["oi/a"])
-        ts(T.oi[:, 100:200], T.oi[:, 0:100], 511, None, OP.bitwise_and, None, ["oi/a"], ["oi/b"])
-        ts(T.off4[:], T.oi[:, 100:200], 4.0, T.pc[:, 1:2], OP.mult, OP.add, ["oi/b", "pc/0"], ["off4"])
-        win = xa[:, 0:1296]
+                cp(o, i, xk + ["ol"], ["xs/%d" % lo])
+        g1, g2, g3 = T.g1, T.g2, T.g3
+        cut(0)
+        scan(T.ox[:], T.k4[:], T.wrow[:], 0.0, OP.add, OP.max, ["k4", "wrow"], ["ox"])
+        ends(0)
+        cp(T.oi[:, 0:80], T.ox[:, 3:320:4], ["ox"], ["oi/a"])
+        tt(g1[:], T.cw[:].indirect(T.e16[:, 0:2]), T.fm[:], OP.mult, ["cw", "e16/0", "fm"], ["g1"])
+        ts(T.oi[:, 80:160], T.oi[:, 0:80], 511, None, OP.bitwise_and, None, ["oi/a"], ["oi/b"])
+        most(th[1], g1[:, 0:4], ["g1"], ["sm/th1"])
+        cut(1)
+        ts(T.ol[:], T.oi[:, 80:160], 4.0, T.pc[:, 1:2], OP.mult, OP.add, ["oi/b", "pc/0"], ["ol"])
+        sort(0, 64)
+        most(ke[0], g1[:, 16:20], ["g1"], ["sm/ke0"])
+        ends(1)
+        ts(T.m2[:, 0:4], g1[:, 16:20], ke[0], None, OP.not_equal, None, ["g1", "sm/ke0"], ["m2/a"])
+        ts(sm[:, 8:12], g1[:, 16:20], ke[0], 1280.0, OP.is_equal, OP.mult, ["g1", "sm/ke0"], ["sm/a1"])
+        tt(T.m2[:, 16:20], T.m2[:, 0:4], T.fm[:, 16:20], OP.mult, ["m2/a", "fm"], ["m2/b"])
+        ts(sm[:, 12:16], g1[:, 16:20], ke[0], ke[0], OP.is_equal, OP.mult, ["g1", "sm/ke0"], ["sm/a2"])
+        tt(g2[:], T.cw[:].indirect(T.e16[:, 2:4]), T.m2[:], OP.mult, ["cw", "e16/1", "m2"], ["g2"])
+        most(th[2], g2[:, 0:4], ["g2"], ["sm/th2"])
+        cut(2)
+        sort(64, 160)
+        sort(160, 256)
+        most(ke[1], g2[:, 16:20], ["g2"], ["sm/ke1"])
+        sort(256, 320, "V")
+        ts(sm[:, 24:28], g2[:, 16:20], ke[1], None, OP.not_equal, None, ["g2", "sm/ke1"], ["sm/n2"])
+        ends(2)
+        tt(T.m3[:, 0:4], sm[:, 24:28], T.m2[:, 16:20], OP.mult, ["sm/n2", "m2/b"], ["m3/a"])
+        ts(sm[:, 16:20], g2[:, 16:20], ke[1], ke[0], OP.is_equal, OP.mult, ["g2", "sm/ke1", "sm/ke0"], ["sm/b1"])
+        tt(g3[:], T.cw[:].indirect(T.e16[:, 4:5]), T.m3[:], OP.mult, ["cw", "e16/2", "m3"], ["g3"])
+        ts(sm[:, 20:24], g2[:, 16:20], ke[1], ke[1], OP.is_equal, OP.mult, ["g2", "sm/ke1"], ["sm/b2"])
+        most(ke[2], g3[:, 0:4], ["g3"], ["sm/ke2"])
+        tt(T.tb[:], sm[:, 8:16], sm[:, 16:24], OP.add, ["sm/a1", "sm/a2", "sm/b1", "sm/b2"], ["tb"])
+        ts(T.ta[:, 0:4], g3[:, 0:4], ke[2], ke[1], OP.is_equal, OP.mult, ["g3", "sm/ke2", "sm/ke1"], ["ta/a"])
+        ts(T.ta[:, 4:8], g3[:, 0:4], ke[2], ke[2], OP.is_equal, OP.mult, ["g3", "sm/ke2"], ["ta/b"])
+        ts(T.tb[:, 0:4], T.tb[:, 0:4], ke[2], None, OP.max, None, ["tb", "sm/ke2"], ["tb"])
+        tt(T.ge[:], T.ta[:], T.tb[:], OP.max, ["ta", "tb"], ["ge"])
 
-        def take(eng, lo, n):
-            o, i = T.btile[:, 4 * lo:4 * lo + 4 * n], win.indirect(T.off4[:, lo // 4:(lo + n) // 4])
-            k = ["btile/%d" % lo]
+        def slots(i):
+            k = (i + 1) % 4
+            ts(T.ya[:, 20 * i:20 * i + 20], T.ncs[:], T.ge[:, k:k + 1], T.ge[:, 4 + k:5 + k], OP.add, OP.is_gt,
+               ["ncs", "ge"], ["ya/%d" % i])
+            ts(T.za[:, 20 * i:20 * i + 20], T.cz[:], T.ge[:, k:k + 1], None, OP.subtract, None, ["cz", "ge"],
+               ["za/%d" % i])
+
+        def slots2(a, b):
+            tt(T.wa[:, 20 * a:20 * b], T.ya[:, 20 * a:20 * b], T.za[:, 20 * a:20 * b], OP.mult,
+               ["%s/%d" % (n, i) for n in ("ya", "za") for i in range(a, b)], ["wa/%d" % a])
+
+        def slots3(a, b):
+            cp(T.ob[:, 20 * a:20 * b], T.wa[:, 20 * a:20 * b], ["wa/%d" % a], ["ob/%d" % i for i in range(a, b)])
+
+        def take(eng, i, lo, hi):
+            o = T.bt[:, 192 + 320 * i + 4 * lo:192 + 320 * i + 4 * hi]
+            w = T.xs[:].indirect(T.ob[:, 20 * i + lo // 4:20 * i + hi // 4])
+            k = ["bt/%d%s" % (i, "a" if lo == 0 else "b")] + (["bt/%db" % i] if (lo, hi) == (0, 80) else [])
             if eng == "V":
-                cp(o, i, [X, "off4"], k)
+                cp(o, w, ["xs", "ob/%d" % i], k)
             else:
-                act(o, i, AF.Copy, [X, "off4"], k)
-        came, back = "came%d" % r, "back%d" % r
-        take("A", 0, 120)
-        take("V", 120, 120)
-        quant("qb", 0, 240, "btile", 0, ["btile/0", "btile/120"])
-        send("qb", came, 1)
-        if r == 0:
-            first_flight_constants()
-        take("A", 240, 80)
-        quant("qbo", 0, 128, "btile", 960, ["btile/240", "btile/pad"])
-        act(T.eh[:, 0:320], win.indirect(T.off4[:, 80:100]), AF.Copy, [X, "off4"], ["eh/0"], scale=0.5)
-        for b in range(4):
-            mm(4 + b, 128, "qun", 128 * b, "qbo", 0)
-        for b in range(4):
-            tt(T.z0[:, b:320:4], T["p%d" % (4 + b)][:, 0:80], T.eh[:, b:320:4], OP.add, ["p%d" % (4 + b), "eh/0"],
-               ["z0/%d" % b])
-        act(T.eh[:, 320:640], T.eh[:, 0:320], AF.Copy, ["eh/0"], ["eh/1"])
-        act(T.eh[:, 640:960], T.eh[:, 0:320], AF.Copy, ["eh/0"], ["eh/2"])
-        quant("qzo", 0, 128, "z0", 0, ["z0"])
-        for b in range(4):
-            mm(b, 128, "wq", 128 * b, "qzo", 0)
-        for b in range(4):
-            act(T.h0[:, b:320:4], T["p%d" % b][:, 0:80], AF.Copy, ["p%d" % b], ["h0/%d" % b], scale=0.03125)
-        for b in range(4):
-            mm(4 + b, 240, "qun", 128 * b, came, 0)
-        for b in range(4):
-            tt(T.z1[:, b:960:4], T["p%d" % (4 + b)][:, 0:240], T.eh[:, b:960:4], OP.add, ["p%d" % (4 + b), "eh"],
-               ["z1/%d" % b])
-        quant("qz1", 0, 240, "z1", 0, ["z1"])
-        for b in range(4):
-            mm(b, 240, "wq", 128 * b, "qz1", 0)
-        for b in range(4):
-            o, i = T.h1[:, b:960:4], T["p%d" % b][:, 0:240]
-            if b % 2:
-                ts(o, i, 0.03125, None, OP.mult, None, ["p%d" % b], ["h1/%d" % b])
+                act(o, w, AF.Copy, ["xs", "ob/%d" % i], k)
+
+        def two(n, i):
+            return ["%s/%d%s" % (n, j, x) if j >= 0 else n + "/pad" for j in (i - 1, i) for x in "ab"]
+
+        def pack_b(i):
+            if i < 3:
+                quant(qb, 128 * i, 128 * i + 128, "bt", 320 * i, two("bt", i), [i + 1])
+                send(qb, i + 1, came, 1)
             else:
-                act(o, i, AF.Copy, ["p%d" % b], ["h1/%d" % b], scale=0.03125)
-        quant("qh", 0, 240, "h1", 0, ["h1"])
-        send("qh", back, -1)
-        quant("qho", 0, 128, "h0", 0, ["h0"])
-        for b in range(4):
-            mm(4 + b, 128, "qun", 128 * b, "qho", 0)
+                quant(came, 0, 128, "bt", 960, two("bt", 3), [0])
+        slots(0)
+        slots(1)
+        slots2(0, 1)
+        slots(2)
+        slots3(0, 1)
+        take("A", 0, 0, 40)
+        take("V", 0, 40, 80)
+        slots(3)
+        slots2(1, 4)
+        pack_b(0)
+        slots3(1, 4)
+        take("A", 1, 0, 40)
+        take("V", 1, 40, 80)
+        take("A", 2, 0, 80)
+        pack_b(1)
+        act(T.eh[:], T.xs[:, 16:336], AF.Copy, ["xs"], ["eh"], scale=0.5)
         if r == 0:
-            second_flight_constants()
-        ts(sm[:, 80:84], T.tab[:, 4:8], -16.0 * UNIT, None, OP.add, None, tabs, ["sm/la"])
-        ts(sm[:, 84:88], T.tab[:, 0:4], 80.0 * UNIT, None, OP.add, None, tabs, ["sm/lb"])
-        cp(T.tab[:, 8:12], T.tab[:, 0:4], tabs, ["tab/g"])
-        tt(T.tab[:, 12:16], sm[:, 80:84], sm[:, 84:88], OP.min, ["sm/la", "sm/lb"], ["tab/l"])
+            act(T.uh[:], T.uo[:], AF.Copy, ["uo"], ["uh"], scale=0.5)
+        take("V", 3, 0, 80)
+        pack_b(2)
+        pack_b(3)
+        if r == 0:
+            for b in range(4):
+                quant("quh", 128 * b, 128 * b + 128, "uh", 3 - b, ["uh"], [b])
+
+        def layer(i):
+            for b in range(4):
+                mm(4 + b, 128, "quh", 128 * b, came, 80 * i, ssub=[b], msub=[max(i - 1, 0), i])
+            for b in range(4):
+                tt(T.z[:, 192 + 320 * i + b:512 + 320 * i:4], T["p%d" % (4 + b)][:, 48:128], T.eh[:, b:320:4], OP.add,
+                   ["p%d" % (4 + b), "eh"], ["z/%d%s" % (i, "abcd"[b])])
+            quant("qz", 128 * i, 128 * i + 128, "z", 320 * i, four("z", i), [i])
+            for b in range(4):
+                mm(b, 128, "wq", 128 * b, "qz", 128 * i, msub=[i])
+            for b in range(4):
+                act(T.h[:, 192 + 320 * i + b:512 + 320 * i:4], T["p%d" % b][:, 48:128], AF.Copy, ["p%d" % b],
+                    ["h/%d%s" % (i, "abcd"[b])], scale=0.03125)
+
+        def four(n, i):
+            return ["%s/%d%s" % (n, j, x) if j >= 0 else n + "/pad" for j in (i - 1, i) for x in "abcd"]
+
+        def pack_h(i):
+            if i == 0:
+                quant(back, 0, 128, "h", 0, four("h", 0), [0])
+            else:
+                quant(qh, 128 * i - 128, 128 * i, "h", 320 * i, four("h", i), [i])
+                send(qh, i, back, -1)
+
+        def renew(k):
+            i = (k + 3) % 4
+            for b in range(4):
+                mm(4 + b, 128, "quo", 128 * b, back, 80 * k, ssub=[b], msub=[max(k - 1, 0), k])
+            for b in range(4):
+                tt(xa[:, 1280 + 320 * k + b:1600 + 320 * k:4], T["p%d" % (4 + b)][:, 48:128],
+                   T.bt[:, 192 + 320 * i + b:512 + 320 * i:4], OP.add,
+                   ["p%d" % (4 + b), "bt/%da" % i, "bt/%db" % i], ["%s/n%d%d" % (X, k, b)])
+        layer(0)
+        ge, sa, sc, se, sf = T.ge, T.sa, T.sc, T.se, T.sf
+        ts(se[:, 60:80], T.rk[:], -4.0, 1279.0, OP.mult, OP.add, ["rk"], ["se/r"])
+        ts(sm[:, 32:36], ge[:, 0:4], -320.0, None, OP.add, None, ["ge"], ["sm/l1"])
+        tt(sm[:, 40:44], ge[:, 0:4], T.kc[:], OP.add, ["ge", "kc"], ["sm/h"])
+        tt(sm[:, 36:40], sm[:, 32:36], ge[:, 4:8], OP.max, ["ge", "sm/l1"], ["sm/lo"])
+        if r == 0:
+            ts(T.old[:], T.cz[:], -1296.0, 4.0, OP.add, OP.mult, ["cz"], ["old"])
         for k in range(4):
-            ts(T.rks[:, 20 * k:20 * k + 20], T.rk[:], -15.875, UNIT, OP.add, OP.mult, ["rk"], ["rks/%d" % k])
-        cp(T.tf[:], T.tab[:, 8:16].indirect(T.l80[:, 0:10]), ["tab/g", "tab/l", "l80"], ["tf"])
-        s1, s2 = T.sl1, T.sl2
-        tt(s1[:, 0:80], T.rks[:], T.tf[:, 80:160], OP.is_lt, ["rks", "tf"], ["sl1/a"])
-        tt(s1[:, 80:160], T.rks[:], T.tf[:, 0:80], OP.is_ge, ["rks", "tf"], ["sl1/b"])
-        tt(s1[:, 160:240], T.rks[:], T.tf[:, 0:80], OP.subtract, ["rks", "tf"], ["sl1/c"])
-        tt(s1[:, 240:320], s1[:, 0:80], s1[:, 80:160], OP.mult, ["sl1/a", "sl1/b"], ["sl1/d"])
-        ts(s1[:, 320:400], s1[:, 160:240], 1.0 / UNIT, None, OP.mult, None, ["sl1/c"], ["sl1/e"])
-        tt(T.pl[:], s1[:, 320:400], T.kc[:], OP.add, ["sl1/e", "kc"], ["pl"])
-        tt(s1[:, 0:80], T.pl[:], s1[:, 240:320], OP.mult, ["pl", "sl1/d"], ["sl1/a"])
-        tt(s2[:, 0:40], s1[:, 0:40], s1[:, 40:80], OP.add, ["sl1/a"], ["sl2/a"])
-        tt(s2[:, 40:60], s2[:, 0:20], s2[:, 20:40], OP.add, ["sl2/a"], ["sl2/b"])
-        ts(s2[:, 60:80], s2[:, 40:60], 320.0, None, OP.add, None, ["sl2/b"], ["sl2/c"])
-        cp(T.po[:], s2[:, 60:80], ["sl2/c"], ["po"])
+            ts(sa[:, 20 * k:20 * k + 20], se[:, 60:80], ge[:, k:k + 1], sm[:, 40 + k:41 + k], OP.is_lt, OP.mult,
+               ["se/r", "ge", "sm/h"], ["sa/%d" % k])
+        pack_h(0)
+        for k in range(4):
+            ts(sc[:, 20 * k:20 * k + 20], se[:, 60:80], sm[:, 36 + k:37 + k], None, OP.is_gt, None,
+               ["se/r", "sm/lo"], ["sc/%d" % k])
+        tt(sf[:], sa[:], sc[:], OP.mult, ["sa", "sc"], ["sf"])
+        if r == 0:
+            quant("quo", 0, 128, "uo", 3, ["uo"], [0])
+        tt(se[:, 0:40], sf[:, 0:40], sf[:, 40:80], OP.add, ["sf"], ["se/a"])
+        if r == 0:
+            quant("quo", 128, 256, "uo", 2, ["uo"], [1])
+        tt(se[:, 40:60], se[:, 0:20], se[:, 20:40], OP.add, ["se/a"], ["se/b"])
+        layer(1)
+        pack_h(1)
+        layer(2)
+        pack_h(2)
+        layer(3)
+        pack_h(3)
+        tt(sa[:, 0:20], se[:, 40:60], se[:, 60:80], OP.subtract, ["se/b", "se/r"], ["sa/0"])
+        if r == 0:
+            quant("quo", 256, 384, "uo", 1, ["uo"], [2])
+        tt(sa[:, 20:40], sa[:, 0:20], T.old[:], OP.max, ["sa/0", "old"], ["sa/1"])
+        if r == 0:
+            quant("quo", 384, 512, "uo", 0, ["uo"], [3])
         for t in range(4):
-            ts(T.po16[:, 20 * t:20 * t + 20], T.po[:], 4.0, float(t), OP.mult, OP.add, ["po"], ["po16/%d" % t])
-        for b in range(4):
-            o, i = T.bk[:, 960 + b:1280:4], T["p%d" % (4 + b)][:, 0:80]
-            act(o, i, AF.Copy, ["p%d" % (4 + b)], ["bk/own%d" % b], scale=2.0)
+            ts(T.po16[:, 20 * t:20 * t + 20], sa[:, 20:40], float(t), None, OP.add, None, ["sa/1"], ["po16/%d" % t])
+        renew(0)
         if r == NR - 1:
-            ts(T.rc[:, 0:240], T.ij[:, 0:240], 80.0, None, OP.add, None, ["ij"], ["rc/a"])
-            ts(T.rc[:, 240:320], T.ij[:, 240:320], -240.0, None, OP.add, None, ["ij"], ["rc/b"])
-            fill(T.rc[:, 320:336], -1.0, ["rc/c"])
-            cp(T.po16[:, 80:100], T.po[:], ["po"], ["po16/s"])
-            act(T.eq[:], T.rc[:, 0:336].indirect(T.po16[:, 80:100]), AF.Copy, ["rc", "po16/s"], ["eq"])
+            ts(T.po16[:, 80:100], sa[:, 20:40], 0.25, None, OP.mult, None, ["sa/1"], ["po16/s"])
+            act(T.eq[:], T.slt[:].indirect(T.po16[:, 80:100]), AF.Copy, ["slt", "po16/s"], ["eq"])
             for q in range(8):
                 dma("S", lambda e, q=q: e.dma_start(T.sl[q:q + 1, :], T.eq[16 * q:16 * q + 1, :]), ("out", 0),
                     ["eq"], [])
             quant("qv", 0, 128, "vt", 0, ["vt"])
-        for b in range(4):
-            mm(b, 240, "qun", 128 * b, back, 0)
-        for b in range(4):
-            o, i = T.bk[:, b:960:4], T["p%d" % b][:, 0:240]
-            if b % 2:
-                ts(o, i, 2.0, None, OP.mult, None, ["p%d" % b], ["bk/%d" % b])
-            else:
-                act(o, i, AF.Copy, ["p%d" % b], ["bk/%d" % b], scale=2.0)
+        for k in (1, 2, 3):
+            renew(k)
         for t in range(4):
-            tt(xn[:, t:1280:4], T.bk[:, 0:1296].indirect(T.po16[:, 20 * t:20 * t + 20]), xa[:, t:1280:4], OP.add,
-               ["bk", "po16/%d" % t, X], [XN + "/x%d" % t])
+            o, w = xn[:, t:1280:4], xa[:].indirect(T.po16[:, 20 * t:20 * t + 20])
+            if t % 2:
+                act(o, w, AF.Copy, [X, "po16/%d" % t], [XN + "/x%d" % t])
+            else:
+                cp(o, w, [X, "po16/%d" % t], [XN + "/x%d" % t])
 
     X = "x%d" % NR
     quant("qx", 0, 320, X, 0, [X + "/x%d" % t for t in range(4)])
-    mm(4, 320, "qv", 0, "qx", 0)
+    mm(0, 160, "qv", 0, "qx", 0)
+    mm(1, 160, "qv", 0, "qx", 160)
     dma("S", lambda e: e.dma_start(T.oc[:], T.qx[:].bitcast(dt.uint8)), ("out", 0), ["qx"], [])
     for k in range(4):
-        dma("S", lambda e, k=k: e.dma_start(T.osc[4 * k:4 * k + 4, :], T.qxs[32 * k:32 * k + 4, :]), ("out", 0),
-            ["qxs"], [])
-    act(T.d1[:], T.p4[:, 0:320], AF.Copy, ["p4"], ["d1"])
-    dma("A", lambda e: e.dma_start(T.y[:], T.d1[:]), ("out", 0), ["d1"], [])
-    g.wait_ge(T.sem.out, 16 * (8 + 1 + 4 + 1))
-    for n in sorted(lsn):
-        g.wait_ge(T.sem["l" + n], lsn[n])
+        dma("SA"[k % 2], lambda e, k=k: e.dma_start(T.osc[4 * k:4 * k + 4, :], T.qxs[32 * k:32 * k + 4, :]),
+            ("out", 0), ["qxs"], [])
+    cp(T.d1[:, 0:160], T.p0[:, 0:160], ["p0"], ["d1/a"])
+    act(T.d1[:, 160:320], T.p1[:, 0:160], AF.Copy, ["p1"], ["d1/b"])
+    dma("S", lambda e: e.dma_start(T.y[:, 0:160], T.d1[:, 0:160]), ("out", 0), ["d1/a"], [])
+    dma("A", lambda e: e.dma_start(T.y[:, 160:320], T.d1[:, 160:320]), ("out", 0), ["d1/b"], [])
+    g.wait_ge(T.sem.out, 16 * (8 + 1 + 4 + 2))
+    g.wait_ge(T.sem.ls, lsn[0])
+    finish()

@@ -10,6 +10,11 @@ B4 = 2.0 ** 21
 CUT = ((46, 128), (101, 224), (174, 288))
 CT = (0, 320, 576, 768, 896, 1024)
 ALONE = (16, 15)
+LATER = ()
+RCFIRST = False
+VSORT = 32
+PLAN = "U1 Z1 U2 Z2 W1 H1 U3 Z3 W2 H2 W3 H3"
+BACK = "1 2 3"
 
 
 def _scratch():
@@ -23,7 +28,7 @@ def _scratch():
         s[n] = ("sbuf", [128, w], F8)
         s[n + "s"] = ("sbuf", [128, w], U8)
     sb(BF, x0=2560, x1=2560, x2=1280, xs=1296, ut=512, vt=512, eg=512, one=528, id4=512, uo=528, uh=528, bt=1472,
-       eh=320, z=1472, h=1472, junk=1280, sg=640, ct=4096)
+       eh=960, z=1472, h=1472, junk=1280, sg=640, ct=4096)
     for n, w in (("qu", 128), ("qur", 128), ("qv", 128), ("wq", 512), ("qx", 320), ("qeg", 128), ("quh", 512),
                  ("quo", 512), ("qz", 512), ("qc", 1024)):
         code(n, w)
@@ -35,7 +40,7 @@ def _scratch():
     sb(F32, i16=320, i4=320, ij=320, mm=320, d0=320, rs=320, k16=320, k4=320, d1=320, st=320, eq=320, rc=320,
        rcb=20, pc=8, v4=320, wrow=320, cw=656, on=320, rx=320, rk=20, acc=8, rsum=32, ox=320, cst=8, fm=32, m2=32,
        m3=16, g1=32, g2=32, g3=16, sm=64, ge=8, ta=8, tb=8, cz=20, ncs=20, old=20, kc=4, ya=80, za=80, wa=80, sa=80,
-       sc=80, se=80, sf=80, it=640, slt=640)
+       sc=80, se=80, sf=80, slt=640)
     sb(I32, pi=8, xi=8, oi=160)
     sb(U16, ul=8, rk16=20, e16=8, ol=80, ob=80, po16=100)
     for b in range(8):
@@ -185,7 +190,7 @@ def rank_program(g, core, T, topo):
 
     dma("S", lambda e: e.dma_start(T.x0[:, 0:1280], T.x[:]), ("dx", 16), [], ["x0/x"])
     dma("A", lambda e: e.dma_start(T.ut[:], T.u[:]), ("du", 16), [], ["ut"])
-    dma("S", lambda e: e.dma_start(T.wq[:].bitcast(dt.uint8), T.wc[:]), ("dw", 32), [], ["wq"])
+    dma("S", lambda e: e.dma_start(T.wq[:].bitcast(dt.uint8), T.wc[:]), ("dw", 32), ["x0/x", "ut"], ["wq"])
     dma("S", lambda e: e.dma_start(T.wqs[:], T.ws[:]), ("dw", 32), [], ["wqs"])
     dma("S", lambda e: e.dma_start(T.vt[:], T.v[:]), ("dv", 16), [], ["vt"])
 
@@ -194,8 +199,8 @@ def rank_program(g, core, T, topo):
     iota(T.i16[:], [[0, 20], [1, 16]], 0, 0, ["i16"])
     fill(T.one[:], 1.0, ["one"])
     select(T.id4[:], T.one[:, 0:512], [[-16, 8], [0, 64]], OP.is_ge, 0, 1, ["one"], ["id4"])
-    iota(T.ij[:], [[1, 320]], 0, 0, ["ij"])
     select(T.eg[:], T.id4[:], [[16, 8], [0, 64]], OP.is_ge, 15, -1, ["id4"], ["eg"])
+    iota(T.ij[:], [[1, 320]], 0, 0, ["ij"])
 
     cp(T.ul[:], T.xi[:], ["xi"], ["ul"])
     ts(T.pi[:, 1:2], T.pi[:, 0:1], 15, None, OP.bitwise_and, None, ["pi/0"], ["pi/1"])
@@ -210,6 +215,7 @@ def rank_program(g, core, T, topo):
     fill(T.cw[:, 320:336], 0.0, ["cw/z"])
     fill(T.xs[:, 0:16], 0.0, ["xs/z"])
     ts(T.pc[:, 3:4], T.pc[:, 0:1], 1.0 - B16, 15 * B16 - 15.0, OP.mult, OP.add, ["pc/0"], ["pc/3"])
+    ts(T.pc[:, 4:5], T.pc[:, 0:1], 1296.0, None, OP.add, None, ["pc/0"], ["pc/4"])
     for s in range(3):
         lo, hi = CUT[s]
         fill(T.cst[:, 2 * s:2 * s + 1], float(lo + hi - 2), ["cst/%da" % s])
@@ -219,7 +225,6 @@ def rank_program(g, core, T, topo):
     act(T.d0[:], T.i16[:], AF.Copy, ["i16"], ["d0"], scale=2.0 * NEG, bias=-NEG)
     act(T.fm[:, 0:16], T.i16[:, 0:16], AF.Copy, ["i16"], ["fm/a"], scale=0.0, bias=1.0)
     act(T.fm[:, 16:32], T.i16[:, 0:16], AF.Copy, ["i16"], ["fm/b"], scale=-2.0 ** -16, bias=1.0)
-    act(T.kc[:], T.i16[:, 0:4], AF.Copy, ["i16"], ["kc"], scale=320.0, bias=1279.0)
     act(T.on[:], T.i16[:], AF.Copy, ["i16"], ["on"], scale=0.0, bias=-UNIT)
     quant("qu", 0, 128, "ut", 0, ["ut"])
     cp(T.qur[:].bitcast(dt.uint32), T.qu[:].bitcast(dt.uint32).indirect(T.ul[:, 0:8]), ["qu", "ul"], ["qur"])
@@ -236,12 +241,23 @@ def rank_program(g, core, T, topo):
 
     gdn, jn, lsn = [0], [0], [0]
 
-    def send(src, i, dst, step):
-        to = T.cores[(rank + step * i) % N]
+    def hops(k):
+        n = 0
+        for i in range(N):
+            a, b = topo.chip(T.cores[i]), topo.chip(T.cores[(i + k) % N])
+            n += 0 if a == b else 1 if topo.mates(a, b) or topo.same_plane(a, b) else 2
+        return n
+    far = [0] + sorted((1, 2, 3), key=lambda k: -hops(k))
+
+    for k in range(4):
+        act(T.kc[:, k:k + 1], T.i16[:, 0:1], AF.Copy, ["i16"], ["kc/%d" % k], bias=1279.0 + 320 * far.index(k))
+
+    def send(src, a, i, dst, step):
+        to = T.cores[(rank + step * far[i]) % N]
         en = topo.engines(core, to)
         mask = topo.mask(core, to)
         ad = topo.addr(to)
-        a, b = 128 * i - 80, 48 + 80 * i
+        b = 48 + 80 * i
         name = "%s_%d" % (dst, i)
         for planes in (False, True):
             if planes:
@@ -262,6 +278,8 @@ def rank_program(g, core, T, topo):
         mm(0, 320, "qur", 0, "qx", 0)
         mm(2, 320, "qu", 0, "qx", 0)
         mm(1, 320, "qur", 0, "qx", 0)
+        if r == 0:
+            quant("qeg", 0, 128, "eg", 0, ["eg"])
         tt(T.d1[:], T.p0[:, 0:320], T.mm[:], OP.add, ["p0", "mm"], ["d1"])
         scan(T.st[:], T.d0[:], T.d1[:], -NEG, OP.min, OP.max, ["d0", "d1"], ["st"])
         act(T.v4[:], T.p2[:, 0:320], AF.Sign, ["p2"], ["v4"])
@@ -271,8 +289,9 @@ def rank_program(g, core, T, topo):
         if r == 0:
             late_constants()
         if r == NR - 1:
-            iota(T.it[:], [[1, 640]], -320, 0, ["it"])
-            select(T.slt[:], T.it[:], [[1, 640]], OP.is_ge, -320, 0, ["it"], ["slt"], -1.0)
+            iota(T.slt[:, 0:320], [[0, 320]], -1, 0, ["slt/n"])
+            for j in range(4):
+                iota(T.slt[:, 320 + 80 * j:400 + 80 * j], [[1, 80]], 80 * far[j], 0, ["slt/%d" % j])
 
         def place(c):
             b, t = (20 - c) // 4, (20 - c) % 4
@@ -311,29 +330,40 @@ def rank_program(g, core, T, topo):
             compare(c)
             rows(c)
         tt(T.ct[:, 0:1280:4], T.st[:], T.p0[:, 0:320], OP.is_ge, ["p0", "st", "ct/z0"], ["ct/20"])
-        if r == 0:
-            quant("qeg", 0, 128, "eg", 0, ["eg"])
-        count(0)
+        due = [0]
         for c in range(16, 0, -1):
-            if c not in ALONE:
+            if c in LATER:
+                alone((c,))
+            elif c not in ALONE:
                 compare(c)
                 rows(c)
+                for b in due:
+                    count(b)
+                due = []
             if c % 4 == 1:
-                count((20 - c) // 4)
-            if r == 0 and c == 9:
-                ts(T.rs[:], T.rs[:], T.pc[:, 3:4], None, OP.add, None, ["rs", "pc/3"], ["rs"])
-        scan(T.rc[:], T.rs[:], T.ct[:, 0:1280:4], 1.0e6, OP.min, OP.add, ["rs", "ct/20"], ["rc"])
+                due.append((20 - c) // 4)
+        if RCFIRST:
+            scan(T.rc[:], T.rs[:], T.ct[:, 0:1280:4], 1.0e6, OP.min, OP.add, ["rs", "ct/20"], ["rc"])
+        count(4)
+        if not RCFIRST:
+            scan(T.rc[:], T.rs[:], T.ct[:, 0:1280:4], 1.0e6, OP.min, OP.add, ["rs", "ct/20"], ["rc"])
         if r == 0:
             act(T.k4[:], T.i4[:], AF.Sign, ["i4", "pc/0"], ["k4"], scale=-1.0, bias=T.pc[:, 2:3])
             act(T.k4[:], T.k4[:], AF.Relu, ["k4"], ["k4"], scale=-9 * B4)
             act(T.k4[:], T.k4[:], AF.Copy, ["k4"], ["k4"], bias=-8 * B4)
-            ts(T.cz[:], T.ij[:, 0:320:16], T.pc[:, 0:1], 1296.0, OP.add, OP.add, ["ij", "pc/0"], ["cz"])
-        tt(T.rcb[:], T.rc[:, 15:320:16], T.rsum[:, 0:20], OP.add, ["rc", "rsum"], ["rcb"])
-        scan(T.rx[:], T.k16[:], T.p3[:, 0:320], 0.0, OP.add, OP.max, ["k16", "p3"], ["rx"])
-        if r == 0:
-            ts(T.ncs[:], T.cz[:], -1.0, 1295.5, OP.mult, OP.add, ["cz"], ["ncs"])
-        tt(T.rk[:], T.rx[:, 15:320:16], T.rcb[:], OP.subtract, ["rx", "rcb"], ["rk"])
-        cp(T.rk16[:], T.rk[:], ["rk"], ["rk16"])
+            act(T.cz[:], T.ij[:, 0:320:16], AF.Identity, ["ij", "pc/4"], ["cz"], bias=T.pc[:, 4:5])
+            act(T.ncs[:], T.cz[:], AF.Copy, ["cz"], ["ncs"], scale=-1.0, bias=1295.5)
+            act(T.old[:], T.cz[:], AF.Copy, ["cz"], ["old"], scale=4.0, bias=-4.0 * 1296)
+            act(T.uh[:], T.uo[:], AF.Copy, ["uo"], ["uh"], scale=0.5)
+        if RCFIRST:
+            tt(T.rcb[:], T.rc[:, 15:320:16], T.rsum[:, 0:20], OP.add, ["rc", "rsum"], ["rcb"])
+            scan(T.rx[:], T.k16[:], T.p3[:, 0:320], 0.0, OP.add, OP.max, ["k16", "p3"], ["rx"])
+            tt(T.rk[:], T.rx[:, 15:320:16], T.rcb[:], OP.subtract, ["rx", "rcb"], ["rk"])
+        else:
+            scan(T.rx[:], T.k16[:], T.p3[:, 0:320], 0.0, OP.add, OP.max, ["k16", "p3"], ["rx"])
+            tt(T.rcb[:], T.rc[:, 15:320:16], T.rsum[:, 0:20], OP.add, ["rc", "rsum"], ["rcb"])
+            tt(T.rk[:], T.rx[:, 15:320:16], T.rcb[:], OP.subtract, ["rx", "rcb"], ["rk"])
+        ts(T.rk16[:], T.rk[:], T.pc[:, 3:4], None, OP.subtract, None, ["rk", "pc/3"], ["rk16"])
         cp(T.wrow[:].indirect(T.rk16[:, 0:20]), T.v4[:], ["rk16", "v4"], ["wrow"])
         scan(T.cw[:, 0:320], T.on[:], T.wrow[:], T.acc[:, 5:6], OP.add, OP.subtract, ["wrow", "on", "acc/T"],
              ["cw/s"])
@@ -378,10 +408,10 @@ def rank_program(g, core, T, topo):
         tt(g2[:], T.cw[:].indirect(T.e16[:, 2:4]), T.m2[:], OP.mult, ["cw", "e16/1", "m2"], ["g2"])
         most(th[2], g2[:, 0:4], ["g2"], ["sm/th2"])
         cut(2)
-        sort(64, 160)
-        sort(160, 256)
+        sort(64, 320 - VSORT)
         most(ke[1], g2[:, 16:20], ["g2"], ["sm/ke1"])
-        sort(256, 320, "V")
+        if VSORT:
+            sort(320 - VSORT, 320, "V")
         ts(sm[:, 24:28], g2[:, 16:20], ke[1], None, OP.not_equal, None, ["g2", "sm/ke1"], ["sm/n2"])
         ends(2)
         tt(T.m3[:, 0:4], sm[:, 24:28], T.m2[:, 16:20], OP.mult, ["sm/n2", "m2/b"], ["m3/a"])
@@ -396,7 +426,7 @@ def rank_program(g, core, T, topo):
         tt(T.ge[:], T.ta[:], T.tb[:], OP.max, ["ta", "tb"], ["ge"])
 
         def slots(i):
-            k = (i + 1) % 4
+            k = far[(i + 1) % 4]
             ts(T.ya[:, 20 * i:20 * i + 20], T.ncs[:], T.ge[:, k:k + 1], T.ge[:, 4 + k:5 + k], OP.add, OP.is_gt,
                ["ncs", "ge"], ["ya/%d" % i])
             ts(T.za[:, 20 * i:20 * i + 20], T.cz[:], T.ge[:, k:k + 1], None, OP.subtract, None, ["cz", "ge"],
@@ -424,7 +454,7 @@ def rank_program(g, core, T, topo):
         def pack_b(i):
             if i < 3:
                 quant(qb, 128 * i, 128 * i + 128, "bt", 320 * i, two("bt", i), [i + 1])
-                send(qb, i + 1, came, 1)
+                send(qb, 128 * i + 48, i + 1, came, 1)
             else:
                 quant(came, 0, 128, "bt", 960, two("bt", 3), [0])
         slots(0)
@@ -440,61 +470,83 @@ def rank_program(g, core, T, topo):
         slots3(1, 4)
         take("A", 1, 0, 40)
         take("V", 1, 40, 80)
-        take("A", 2, 0, 80)
+        take("A", 2, 0, 56)
         pack_b(1)
-        act(T.eh[:], T.xs[:, 16:336], AF.Copy, ["xs"], ["eh"], scale=0.5)
-        if r == 0:
-            act(T.uh[:], T.uo[:], AF.Copy, ["uo"], ["uh"], scale=0.5)
-        take("V", 3, 0, 80)
+        take("V", 2, 56, 80)
+        take("A", 3, 0, 40)
         pack_b(2)
-        pack_b(3)
+        take("V", 3, 40, 80)
+        for i in range(max(int(s[-1]) - int(s[1]) + 1 for s in PLAN.split() if s[0] == "U")):
+            act(T.eh[:, 320 * i:320 * i + 320], T.xs[:, 16:336], AF.Copy, ["xs"], ["eh/%d" % i], scale=0.5)
         if r == 0:
             for b in range(4):
                 quant("quh", 128 * b, 128 * b + 128, "uh", 3 - b, ["uh"], [b])
+        pack_b(3)
 
-        def layer(i):
-            for b in range(4):
-                mm(4 + b, 128, "quh", 128 * b, came, 80 * i, ssub=[b], msub=[max(i - 1, 0), i])
-            for b in range(4):
-                tt(T.z[:, 192 + 320 * i + b:512 + 320 * i:4], T["p%d" % (4 + b)][:, 48:128], T.eh[:, b:320:4], OP.add,
-                   ["p%d" % (4 + b), "eh"], ["z/%d%s" % (i, "abcd"[b])])
-            quant("qz", 128 * i, 128 * i + 128, "z", 320 * i, four("z", i), [i])
-            for b in range(4):
-                mm(b, 128, "wq", 128 * b, "qz", 128 * i, msub=[i])
-            for b in range(4):
-                act(T.h[:, 192 + 320 * i + b:512 + 320 * i:4], T["p%d" % b][:, 48:128], AF.Copy, ["p%d" % b],
-                    ["h/%d%s" % (i, "abcd"[b])], scale=0.03125)
+        def span(lo, hi):
+            n = 80 * (hi - lo + 1)
+            return n, max(n, 128), 128 + 80 * hi
 
-        def four(n, i):
-            return ["%s/%d%s" % (n, j, x) if j >= 0 else n + "/pad" for j in (i - 1, i) for x in "abcd"]
+        def four(n, lo, hi, x="abcd"):
+            return ["%s/%d%s" % (n, j, c) if j >= 0 else n + "/pad" for j in range(lo, hi + 1) for c in x]
 
-        def pack_h(i):
-            if i == 0:
-                quant(back, 0, 128, "h", 0, four("h", 0), [0])
+        def unpack(lo, hi):
+            n, w, end = span(lo, hi)
+            for b in range(4):
+                mm(4 + b, w, "quh", 128 * b, came, end - w, ssub=[b], msub=range(max(lo - 1, 0), hi + 1))
+            for b in range(4):
+                tt(T.z[:, 4 * (end - n) + b:4 * end:4], T["p%d" % (4 + b)][:, w - n:w], T.eh[:, b:4 * n:4], OP.add,
+                   ["p%d" % (4 + b)] + ["eh/%d" % i for i in range(n // 80)], four("z", lo, hi, "abcd"[b]))
+        at = {"z": 0, "h": 0}
+
+        def pack_z(lo, hi):
+            n, w, end = span(lo, hi)
+            at[lo] = at["z"]
+            at["z"] += w
+            quant("qz", at[lo], at[lo] + w, "z", 4 * (end - w), four("z", lo - 1, hi), range(lo, hi + 1))
+
+        def layer(lo, hi):
+            n, w, end = span(lo, hi)
+            for b in range(4):
+                mm(b, w, "wq", 128 * b, "qz", at[lo], msub=[lo])
+            for b in range(4):
+                o, i = T.h[:, 4 * (end - n) + b:4 * end:4], T["p%d" % b][:, w - n:w]
+                if n > 80 and b % 2:
+                    ts(o, i, 0.03125, None, OP.mult, None, ["p%d" % b], four("h", lo, hi, "abcd"[b]))
+                else:
+                    act(o, i, AF.Copy, ["p%d" % b], four("h", lo, hi, "abcd"[b]), scale=0.03125)
+
+        def pack_h(lo, hi):
+            n, w, end = span(lo, hi)
+            if lo == 0:
+                quant(back, 0, 128, "h", 0, four("h", -1, 0), [0])
             else:
-                quant(qh, 128 * i - 128, 128 * i, "h", 320 * i, four("h", i), [i])
-                send(qh, i, back, -1)
+                quant(qh, at["h"], at["h"] + w, "h", 4 * (end - w), four("h", lo - 1, hi), range(lo, hi + 1))
+                for i in range(lo, hi + 1):
+                    send(qh, at["h"] + w - 80 * (hi + 1 - i), i, back, -1)
+                at["h"] += w
 
-        def renew(k):
-            i = (k + 3) % 4
+        def renew(lo, hi):
+            n, w, end = span(lo, hi)
+            i = (lo + 3) % 4
             for b in range(4):
-                mm(4 + b, 128, "quo", 128 * b, back, 80 * k, ssub=[b], msub=[max(k - 1, 0), k])
+                mm(4 + b, w, "quo", 128 * b, back, end - w, ssub=[b], msub=range(max(lo - 1, 0), hi + 1))
             for b in range(4):
-                tt(xa[:, 1280 + 320 * k + b:1600 + 320 * k:4], T["p%d" % (4 + b)][:, 48:128],
-                   T.bt[:, 192 + 320 * i + b:512 + 320 * i:4], OP.add,
-                   ["p%d" % (4 + b), "bt/%da" % i, "bt/%db" % i], ["%s/n%d%d" % (X, k, b)])
-        layer(0)
+                tt(xa[:, 1280 + 320 * lo + b:1600 + 320 * hi:4], T["p%d" % (4 + b)][:, w - n:w],
+                   T.bt[:, 192 + 320 * i + b:192 + 320 * i + 4 * n:4], OP.add,
+                   ["p%d" % (4 + b)] + four("bt", i, i + hi - lo, "ab"), ["%s/n%d%d" % (X, lo, b)])
+        unpack(0, 0)
+        pack_z(0, 0)
+        layer(0, 0)
         ge, sa, sc, se, sf = T.ge, T.sa, T.sc, T.se, T.sf
-        ts(se[:, 60:80], T.rk[:], -4.0, 1279.0, OP.mult, OP.add, ["rk"], ["se/r"])
+        ts(se[:, 60:80], T.rk16[:], -4.0, 1279.0, OP.mult, OP.add, ["rk16"], ["se/r"])
         ts(sm[:, 32:36], ge[:, 0:4], -320.0, None, OP.add, None, ["ge"], ["sm/l1"])
         tt(sm[:, 40:44], ge[:, 0:4], T.kc[:], OP.add, ["ge", "kc"], ["sm/h"])
         tt(sm[:, 36:40], sm[:, 32:36], ge[:, 4:8], OP.max, ["ge", "sm/l1"], ["sm/lo"])
-        if r == 0:
-            ts(T.old[:], T.cz[:], -1296.0, 4.0, OP.add, OP.mult, ["cz"], ["old"])
         for k in range(4):
             ts(sa[:, 20 * k:20 * k + 20], se[:, 60:80], ge[:, k:k + 1], sm[:, 40 + k:41 + k], OP.is_lt, OP.mult,
                ["se/r", "ge", "sm/h"], ["sa/%d" % k])
-        pack_h(0)
+        pack_h(0, 0)
         for k in range(4):
             ts(sc[:, 20 * k:20 * k + 20], se[:, 60:80], sm[:, 36 + k:37 + k], None, OP.is_gt, None,
                ["se/r", "sm/lo"], ["sc/%d" % k])
@@ -505,12 +557,8 @@ def rank_program(g, core, T, topo):
         if r == 0:
             quant("quo", 128, 256, "uo", 2, ["uo"], [1])
         tt(se[:, 40:60], se[:, 0:20], se[:, 20:40], OP.add, ["se/a"], ["se/b"])
-        layer(1)
-        pack_h(1)
-        layer(2)
-        pack_h(2)
-        layer(3)
-        pack_h(3)
+        for step in PLAN.split():
+            {"U": unpack, "Z": pack_z, "W": layer, "H": pack_h}[step[0]](int(step[1]), int(step[-1]))
         tt(sa[:, 0:20], se[:, 40:60], se[:, 60:80], OP.subtract, ["se/b", "se/r"], ["sa/0"])
         if r == 0:
             quant("quo", 256, 384, "uo", 1, ["uo"], [2])
@@ -519,7 +567,7 @@ def rank_program(g, core, T, topo):
             quant("quo", 384, 512, "uo", 0, ["uo"], [3])
         for t in range(4):
             ts(T.po16[:, 20 * t:20 * t + 20], sa[:, 20:40], float(t), None, OP.add, None, ["sa/1"], ["po16/%d" % t])
-        renew(0)
+        renew(0, 0)
         if r == NR - 1:
             ts(T.po16[:, 80:100], sa[:, 20:40], 0.25, None, OP.mult, None, ["sa/1"], ["po16/s"])
             act(T.eq[:], T.slt[:].indirect(T.po16[:, 80:100]), AF.Copy, ["slt", "po16/s"], ["eq"])
@@ -527,8 +575,8 @@ def rank_program(g, core, T, topo):
                 dma("S", lambda e, q=q: e.dma_start(T.sl[q:q + 1, :], T.eq[16 * q:16 * q + 1, :]), ("out", 0),
                     ["eq"], [])
             quant("qv", 0, 128, "vt", 0, ["vt"])
-        for k in (1, 2, 3):
-            renew(k)
+        for step in BACK.split():
+            renew(int(step[0]), int(step[-1]))
         for t in range(4):
             o, w = xn[:, t:1280:4], xa[:].indirect(T.po16[:, 20 * t:20 * t + 20])
             if t % 2:

@@ -9,11 +9,12 @@ B16 = 1024.0
 B4 = 2.0 ** 21
 CUT = ((46, 128), (101, 224), (174, 288))
 CT = (0, 320, 576, 768, 896, 1024)
-ALONE = (16, 15)
-LATER = ()
-RCFIRST = False
-VSORT = 32
-PLAN = "U1 Z1 U2 Z2 W1 H1 U3 Z3 W2 H2 W3 H3"
+ALONE = (15, 14, 13, 12, 11, 10)
+S0 = 16
+ORDER = "c19 c18 c17 d0 c16 q0 c9 c8 c7 c6 c5 c4 c3 c2 c1 q1 s19 s18 s17 s16 r1 q2 b1 q3 q4 r0 b0"
+VSORT = 16
+ASORT = 64
+PLAN = "U0 Z0 O0 O1 O2 O3 U1 Z1 U2 Z2 W1 S0 H1 U3 Z3 W2 S1 H2 W3 S2 H3 W0 S3 S4 S5 S6 H0 S7 S8 R0"
 BACK = "1 2 3"
 
 
@@ -27,8 +28,8 @@ def _scratch():
     def code(n, w):
         s[n] = ("sbuf", [128, w], F8)
         s[n + "s"] = ("sbuf", [128, w], U8)
-    sb(BF, x0=2560, x1=2560, x2=1280, xs=1296, ut=512, vt=512, eg=512, one=528, id4=512, uo=528, uh=528, bt=1472,
-       eh=960, z=1472, h=1472, junk=1280, sg=640, ct=4096)
+    sb(BF, x0=2560, x1=2560, x2=1280, xs=1296, ut=512, vt=512, eg=512, one=528, uo=528, uh=528, bt=1472,
+       eh=960, z=1472, h=1472, junk=1280, sg=1280, ct=4096, rs=320, rc=320, rb=608)
     for n, w in (("qu", 128), ("qur", 128), ("qv", 128), ("wq", 512), ("qx", 320), ("qeg", 128), ("quh", 512),
                  ("quo", 512), ("qz", 512), ("qc", 1024)):
         code(n, w)
@@ -37,9 +38,9 @@ def _scratch():
             code("%s%d" % (n, r), 368)
         for n in ("qb", "qh"):
             code("%s%d" % (n, r), 384)
-    sb(F32, i16=320, i4=320, ij=320, mm=320, d0=320, rs=320, k16=320, k4=320, d1=320, st=320, eq=320, rc=320,
-       rcb=20, pc=8, v4=320, wrow=320, cw=656, on=320, rx=320, rk=20, acc=8, rsum=32, ox=320, cst=8, fm=32, m2=32,
-       m3=16, g1=32, g2=32, g3=16, sm=64, ge=8, ta=8, tb=8, cz=20, ncs=20, old=20, kc=4, ya=80, za=80, wa=80, sa=80,
+    sb(F32, i16=320, i4=320, ij=320, mm=320, d0=320, k16=320, k4=320, d1=320, st=320, eq=320, e8=8,
+       rcb=20, pc=8, v4=320, wrow=320, cw=664, on=320, rx=320, rk=20, acc=8, rsum=32, ox=320, cst=6, fm=32,
+       g1=32, g2=32, g3=16, sm=64, ge=8, ta=8, tb=8, cz=20, ncs=20, old=20, kc=4, ya=80, za=80, wa=80, sa=80,
        sc=80, se=80, sf=80, slt=640)
     sb(I32, pi=8, xi=8, oi=160)
     sb(U16, ul=8, rk16=20, e16=8, ol=80, ob=80, po16=100)
@@ -197,47 +198,59 @@ def rank_program(g, core, T, topo):
     iota(T.pi[:, 0:1], [[0, 1]], 0, 1, ["pi/0"], False)
     iota(T.xi[:, 0:8], [[16, 8]], 4, 0, ["xi"], False)
     iota(T.i16[:], [[0, 20], [1, 16]], 0, 0, ["i16"])
-    fill(T.one[:], 1.0, ["one"])
-    select(T.id4[:], T.one[:, 0:512], [[-16, 8], [0, 64]], OP.is_ge, 0, 1, ["one"], ["id4"])
-    select(T.eg[:], T.id4[:], [[16, 8], [0, 64]], OP.is_ge, 15, -1, ["id4"], ["eg"])
+    iota(T.e8[:], [[16, 8]], 0, -1, ["e8"])
     iota(T.ij[:], [[1, 320]], 0, 0, ["ij"])
+    iota(T.rs[:, 0:16 * S0], [[-16, S0], [32767, 16]], 152, 0, ["rs/0"])
+    iota(T.rs[:, 16 * S0:320], [[-16, 20 - S0], [32767, 16]], 304 - 16 * S0, 0, ["rs/1"])
 
+    fill(T.one[:], 1.0, ["one"])
     cp(T.ul[:], T.xi[:], ["xi"], ["ul"])
     ts(T.pi[:, 1:2], T.pi[:, 0:1], 15, None, OP.bitwise_and, None, ["pi/0"], ["pi/1"])
     ts(T.pi[:, 2:3], T.pi[:, 0:1], 3, None, OP.bitwise_and, None, ["pi/0"], ["pi/2"])
+    fill(T.rsum[:, 0:1], 0.0, ["rsum/0"])
+    ts(T.pi[:, 3:4], T.pi[:, 1:2], 2, None, OP.logical_shift_right, None, ["pi/1"], ["pi/3"])
     for b in range(5):
         fill(T.ct[:, 4 * (CT[b + 1] - (48 if b < 4 else 112)):4 * CT[b + 1]], 0.0, ["ct/z%d" % b])
-    ts(T.pi[:, 3:4], T.pi[:, 1:2], 2, None, OP.logical_shift_right, None, ["pi/1"], ["pi/3"])
-    fill(T.rsum[:, 0:1], 0.0, ["rsum/0"])
-    fill(T.m2[:], 0.0, ["m2"])
-    cp(T.pc[:, 0:3], T.pi[:, 1:4], ["pi"], ["pc/0"])
-    fill(T.m3[:], 0.0, ["m3"])
-    fill(T.cw[:, 320:336], 0.0, ["cw/z"])
-    fill(T.xs[:, 0:16], 0.0, ["xs/z"])
-    ts(T.pc[:, 3:4], T.pc[:, 0:1], 1.0 - B16, 15 * B16 - 15.0, OP.mult, OP.add, ["pc/0"], ["pc/3"])
-    ts(T.pc[:, 4:5], T.pc[:, 0:1], 1296.0, None, OP.add, None, ["pc/0"], ["pc/4"])
-    for s in range(3):
-        lo, hi = CUT[s]
-        fill(T.cst[:, 2 * s:2 * s + 1], float(lo + hi - 2), ["cst/%da" % s])
-        fill(T.cst[:, 2 * s + 1:2 * s + 2], float(lo + hi - 2 + 672), ["cst/%db" % s])
+        if b == 0:
+            cp(T.pc[:, 0:3], T.pi[:, 1:4], ["pi"], ["pc/0"])
     ts(T.mm[:], T.i16[:], T.pc[:, 0:1], -2.0 * NEG, OP.not_equal, OP.mult, ["i16", "pc/0"], ["mm"])
-    ts(T.k16[:], T.i16[:], T.pc[:, 0:1], 34 * B16, OP.is_gt, OP.mult, ["i16", "pc/0"], ["k16"])
+    ts(T.e8[:], T.e8[:], T.pc[:, 0:1], 0.0, OP.add, OP.is_equal, ["e8", "pc/0"], ["e8"])
     act(T.d0[:], T.i16[:], AF.Copy, ["i16"], ["d0"], scale=2.0 * NEG, bias=-NEG)
-    act(T.fm[:, 0:16], T.i16[:, 0:16], AF.Copy, ["i16"], ["fm/a"], scale=0.0, bias=1.0)
-    act(T.fm[:, 16:32], T.i16[:, 0:16], AF.Copy, ["i16"], ["fm/b"], scale=-2.0 ** -16, bias=1.0)
-    act(T.on[:], T.i16[:], AF.Copy, ["i16"], ["on"], scale=0.0, bias=-UNIT)
     quant("qu", 0, 128, "ut", 0, ["ut"])
     cp(T.qur[:].bitcast(dt.uint32), T.qu[:].bitcast(dt.uint32).indirect(T.ul[:, 0:8]), ["qu", "ul"], ["qur"])
+    for j in range(4):
+        act(T.eg[:, 64 * j:64 * j + 64], T.one[:, 0:64], AF.Copy, ["one", "e8"], ["eg/%d" % j], scale=T.e8[:, j:j + 1])
     act(T.qurs[:], T.qus[:].indirect(T.ul[:, 0:8]), AF.Copy, ["qus", "ul"], ["qurs"])
-    act(T.k16[:], T.k16[:], AF.Copy, ["k16"], ["k16"], bias=-33 * B16)
-    for n in ("bt", "z", "h"):
-        act(T[n][:, 0:192], T.i16[:, 0:192], AF.Copy, ["i16"], [n + "/pad"], scale=0.0)
+    for j in range(4, 8):
+        act(T.eg[:, 64 * j:64 * j + 64], T.one[:, 0:64], AF.Copy, ["one", "e8"], ["eg/%d" % j], scale=T.e8[:, j:j + 1])
+
+    select(T.uo[:], T.one[:], [[1, 528]], OP.is_equal, -3, -4, ["one"], ["uo"])
+
+    def product_constants():
+        ts(T.k16[:], T.i16[:], T.pc[:, 0:1], 34 * B16, OP.is_gt, OP.mult, ["i16", "pc/0"], ["k16"])
+        ts(T.pc[:, 3:4], T.pc[:, 0:1], 1.0 - B16, 15 * B16 - 167.0, OP.mult, OP.add, ["pc/0"], ["pc/3"])
+        act(T.k16[:], T.k16[:], AF.Copy, ["k16"], ["k16"], bias=-33 * B16)
+
+    def count_constants():
+        act(T.on[:], T.i16[:], AF.Copy, ["i16"], ["on"], scale=0.0, bias=-UNIT)
+        act(T.fm[:, 0:16], T.i16[:, 0:16], AF.Copy, ["i16"], ["fm/a"], scale=0.0, bias=1.0)
+        act(T.fm[:, 16:32], T.i16[:, 0:16], AF.Copy, ["i16"], ["fm/b"], scale=-2.0 ** -16, bias=1.0)
+        act(T.pc[:, 4:5], T.pc[:, 0:1], AF.Copy, ["pc/0"], ["pc/4"], bias=1296.0)
+        act(T.pc[:, 5:6], T.pc[:, 0:1], AF.Copy, ["pc/0"], ["pc/5"], scale=-2.0 ** -15, bias=2.0)
 
     def late_constants():
-        iota(T.rs[:], [[-16, 20], [32767, 16]], 0, 0, ["rs"])
         iota(T.i4[:], [[0, 80], [1, 4]], 0, 0, ["i4"])
-        iota(T.cw[:, 336:656], [[-4, 320]], 1276, 0, ["cw/i"])
-        select(T.uo[:], T.one[:], [[1, 528]], OP.is_equal, -3, -4, ["one"], ["uo"])
+        iota(T.cw[:, 344:664], [[-4, 320]], 1276, 0, ["cw/i"])
+        iota(T.cw[:, 0:8], [[0, 8]], 0, 0, ["cw/y"])
+        iota(T.cw[:, 328:344], [[0, 16]], 0, 0, ["cw/z"])
+        iota(T.xs[:, 0:16], [[0, 16]], 0, 0, ["xs/z"])
+        for s in range(3):
+            iota(T.cst[:, 2 * s:2 * s + 2], [[672, 2]], CUT[s][0] + CUT[s][1] + 14, 0, ["cst/%d" % s])
+        for k in range(4):
+            iota(T.kc[:, k:k + 1], [[0, 1]], 1279 + 320 * far.index(k), 0, ["kc/%d" % k])
+        for n in ("bt", "z"):
+            iota(T[n][:, 0:192], [[0, 192]], 0, 0, [n + "/pad"])
+        iota(T.h[:, 0:512], [[0, 512]], 0, 0, ["h"])
 
     gdn, jn, lsn = [0], [0], [0]
 
@@ -248,9 +261,6 @@ def rank_program(g, core, T, topo):
             n += 0 if a == b else 1 if topo.mates(a, b) or topo.same_plane(a, b) else 2
         return n
     far = [0] + sorted((1, 2, 3), key=lambda k: -hops(k))
-
-    for k in range(4):
-        act(T.kc[:, k:k + 1], T.i16[:, 0:1], AF.Copy, ["i16"], ["kc/%d" % k], bias=1279.0 + 320 * far.index(k))
 
     def send(src, a, i, dst, step):
         to = T.cores[(rank + step * far[i]) % N]
@@ -279,7 +289,7 @@ def rank_program(g, core, T, topo):
         mm(2, 320, "qu", 0, "qx", 0)
         mm(1, 320, "qur", 0, "qx", 0)
         if r == 0:
-            quant("qeg", 0, 128, "eg", 0, ["eg"])
+            product_constants()
         tt(T.d1[:], T.p0[:, 0:320], T.mm[:], OP.add, ["p0", "mm"], ["d1"])
         scan(T.st[:], T.d0[:], T.d1[:], -NEG, OP.min, OP.max, ["d0", "d1"], ["st"])
         act(T.v4[:], T.p2[:, 0:320], AF.Sign, ["p2"], ["v4"])
@@ -311,43 +321,55 @@ def rank_program(g, core, T, topo):
                 accum_out=T.rsum[:, c:c + 1])
 
         def alone(cs):
-            for i, c in enumerate(cs):
+            for c in cs:
+                i = c % 4
                 act(T.sg[:, 320 * i:320 * i + 16 * c], T.p1[:, 0:16 * c], AF.Sign, ["p1", "st"], ["sg/%d" % i],
                     scale=-1.0, bias=own(c))
-            for i, c in enumerate(cs):
+            for c in cs:
+                i = c % 4
                 o, key = place(c)
                 act(o, T.sg[:, 320 * i:320 * i + 16 * c], AF.Relu, ["sg/%d" % i, "ct/z%d" % ((20 - c) // 4)],
                     [key, "rsum/%d" % c], accum_out=T.rsum[:, c:c + 1])
+
+        def sums(c):
+            b, t = (20 - c) // 4, (20 - c) % 4
+            a = 4 * CT[b] + t
+            scan(T.rb[:, 4 * (152 - 8 * c) + c - S0:608:4], T.ct[:, a:a + 32 * c:4],
+                 T.ct[:, a + 32 * c:4 * (CT[b] + 16 * c):4], -152.0, OP.add, OP.add, ["ct/%d" % c], ["rb/%d" % c])
 
         def count(b):
             w = CT[b + 1] - CT[b]
             quant("qc", CT[b], CT[b + 1], "ct", 4 * CT[b],
                   ["ct/z%d" % b] + ["ct/%d" % (20 - 4 * b - t) for t in range(4)], [b])
             mm(3, w, "qeg", 0, "qc", CT[b], b == 0, b == 4, msub=[b])
-        alone(ALONE)
+        for i in range(0, len(ALONE), 2):
+            alone(ALONE[i:i + 2])
         act(T.acc[:, 5:6], T.acc[:, 4:5], AF.Copy, ["acc/t"], ["acc/T"], bias=319.6 * UNIT)
-        for c in (19, 18, 17):
-            compare(c)
-            rows(c)
-        tt(T.ct[:, 0:1280:4], T.st[:], T.p0[:, 0:320], OP.is_ge, ["p0", "st", "ct/z0"], ["ct/20"])
-        due = [0]
-        for c in range(16, 0, -1):
-            if c in LATER:
-                alone((c,))
-            elif c not in ALONE:
+        for step in ORDER.split():
+            c = int(step[1:])
+            if step[0] == "c":
                 compare(c)
-                rows(c)
-                for b in due:
-                    count(b)
-                due = []
-            if c % 4 == 1:
-                due.append((20 - c) // 4)
-        if RCFIRST:
-            scan(T.rc[:], T.rs[:], T.ct[:, 0:1280:4], 1.0e6, OP.min, OP.add, ["rs", "ct/20"], ["rc"])
-        count(4)
-        if not RCFIRST:
-            scan(T.rc[:], T.rs[:], T.ct[:, 0:1280:4], 1.0e6, OP.min, OP.add, ["rs", "ct/20"], ["rc"])
+                if c < S0:
+                    rows(c)
+            elif step[0] == "s":
+                sums(c)
+            elif step[0] == "q":
+                if r == 0 and c == 0:
+                    quant("qeg", 0, 128, "eg", 0, ["eg"])
+                count(c)
+            elif step[0] == "d":
+                tt(T.ct[:, 0:1280:4], T.st[:], T.p0[:, 0:320], OP.is_ge, ["p0", "st", "ct/z0"], ["ct/20"])
+            elif step[0] == "r":
+                lo, hi = ((0, 16 * S0), (16 * S0, 320))[c]
+                scan(T.rc[:, lo:hi], T.rs[:, lo:hi], T.ct[:, 4 * lo:4 * hi:4], 1.0e4, OP.min, OP.add,
+                     ["rs", "ct/20"], ["rc/%d" % c])
+            elif c == 0:
+                tt(T.rcb[:, 0:S0], T.rc[:, 15:16 * S0:16], T.rsum[:, 0:S0], OP.add, ["rc/0", "rsum"], ["rcb/0"])
+            else:
+                tt(T.rcb[:, S0:20], T.rc[:, 16 * S0 + 15:320:16], T.rb[:, 604:624 - S0], OP.add, ["rc/1", "rb"],
+                   ["rcb/1"])
         if r == 0:
+            count_constants()
             act(T.k4[:], T.i4[:], AF.Sign, ["i4", "pc/0"], ["k4"], scale=-1.0, bias=T.pc[:, 2:3])
             act(T.k4[:], T.k4[:], AF.Relu, ["k4"], ["k4"], scale=-9 * B4)
             act(T.k4[:], T.k4[:], AF.Copy, ["k4"], ["k4"], bias=-8 * B4)
@@ -355,32 +377,36 @@ def rank_program(g, core, T, topo):
             act(T.ncs[:], T.cz[:], AF.Copy, ["cz"], ["ncs"], scale=-1.0, bias=1295.5)
             act(T.old[:], T.cz[:], AF.Copy, ["cz"], ["old"], scale=4.0, bias=-4.0 * 1296)
             act(T.uh[:], T.uo[:], AF.Copy, ["uo"], ["uh"], scale=0.5)
-        if RCFIRST:
-            tt(T.rcb[:], T.rc[:, 15:320:16], T.rsum[:, 0:20], OP.add, ["rc", "rsum"], ["rcb"])
-            scan(T.rx[:], T.k16[:], T.p3[:, 0:320], 0.0, OP.add, OP.max, ["k16", "p3"], ["rx"])
-            tt(T.rk[:], T.rx[:, 15:320:16], T.rcb[:], OP.subtract, ["rx", "rcb"], ["rk"])
-        else:
-            scan(T.rx[:], T.k16[:], T.p3[:, 0:320], 0.0, OP.add, OP.max, ["k16", "p3"], ["rx"])
-            tt(T.rcb[:], T.rc[:, 15:320:16], T.rsum[:, 0:20], OP.add, ["rc", "rsum"], ["rcb"])
-            tt(T.rk[:], T.rx[:, 15:320:16], T.rcb[:], OP.subtract, ["rx", "rcb"], ["rk"])
+        scan(T.rx[:], T.k16[:], T.p3[:, 0:320], 0.0, OP.add, OP.max, ["k16", "p3"], ["rx"])
+        tt(T.rk[:], T.rx[:, 15:320:16], T.rcb[:], OP.subtract, ["rx", "rcb"], ["rk"])
         ts(T.rk16[:], T.rk[:], T.pc[:, 3:4], None, OP.subtract, None, ["rk", "pc/3"], ["rk16"])
         cp(T.wrow[:].indirect(T.rk16[:, 0:20]), T.v4[:], ["rk16", "v4"], ["wrow"])
-        scan(T.cw[:, 0:320], T.on[:], T.wrow[:], T.acc[:, 5:6], OP.add, OP.subtract, ["wrow", "on", "acc/T"],
+        scan(T.cw[:, 8:328], T.on[:], T.wrow[:], T.acc[:, 5:6], OP.add, OP.subtract, ["wrow", "on", "acc/T"],
              ["cw/s"])
         sm = T.sm
         th = [T.acc[:, 5:6], sm[:, 0:1], sm[:, 1:2]]
         ke = [sm[:, 2:3], sm[:, 3:4], sm[:, 4:5]]
+        left = [0.5, sm[:, 5:6], sm[:, 6:7]]
 
         def cut(s):
             lo, hi = CUT[s]
-            act(T.junk[:, 320 * s:320 * s + hi - lo], T.cw[:, lo - 1:hi - 1], AF.Sign,
+            act(T.junk[:, 320 * s:320 * s + hi - lo], T.cw[:, lo + 7:hi + 7], AF.Sign,
                 ["cw/s", "acc/T" if s == 0 else "sm/th%d" % s], ["junk/%d" % s, "acc/%d" % s],
                 bias=th[s], scale=-(4.0 - s) / (3.0 - s), accum_out=T.acc[:, s:s + 1])
 
         def ends(s):
             a = 2 * s + (s == 2)
-            ts(T.e16[:, 2 * s:2 * s + 2 * s + 2 - a], T.cst[:, a:2 * s + 2], T.acc[:, s:s + 1], 0.5, OP.subtract,
-               OP.mult, ["acc/%d" % s, "cst"], ["e16/%d" % s])
+            ts(T.e16[:, 2 * s:2 * s + 2 * s + 2 - a], T.cst[:, a:2 * s + 2], T.acc[:, s:s + 1], left[s], OP.subtract,
+               OP.mult, ["acc/%d" % s, "cst"] + ["sm/left%d" % s] * (s > 0), ["e16/%d" % s])
+
+        def mine(s):
+            lo, hi = CUT[s]
+            ts(sm[:, 24 + s:25 + s], T.acc[:, s:s + 1], 640.0 - lo - hi, T.pc[:, 5:6], OP.add, OP.mult,
+               ["acc/%d" % s, "pc/5"], ["sm/mine%d" % s])
+
+        def stays(s):
+            ts(left[s + 1], sm[:, 24 + s:25 + s], ke[s], left[s], OP.not_equal, OP.mult,
+               ["sm/mine%d" % s, "sm/ke%d" % s] + ["sm/left%d" % s] * (s > 0), ["sm/left%d" % (s + 1)])
 
         def sort(lo, hi, eng="A"):
             o, i = T.xs[:, 16 + 4 * lo:16 + 4 * hi], xa[:, 0:1280].indirect(T.ol[:, lo // 4:hi // 4])
@@ -397,40 +423,42 @@ def rank_program(g, core, T, topo):
         ts(T.oi[:, 80:160], T.oi[:, 0:80], 511, None, OP.bitwise_and, None, ["oi/a"], ["oi/b"])
         most(th[1], g1[:, 0:4], ["g1"], ["sm/th1"])
         cut(1)
-        ts(T.ol[:], T.oi[:, 80:160], 4.0, T.pc[:, 1:2], OP.mult, OP.add, ["oi/b", "pc/0"], ["ol"])
-        sort(0, 64)
         most(ke[0], g1[:, 16:20], ["g1"], ["sm/ke0"])
-        ends(1)
-        ts(T.m2[:, 0:4], g1[:, 16:20], ke[0], None, OP.not_equal, None, ["g1", "sm/ke0"], ["m2/a"])
+        ts(T.ol[:], T.oi[:, 80:160], 4.0, T.pc[:, 1:2], OP.mult, OP.add, ["oi/b", "pc/0"], ["ol"])
+        sort(0, ASORT)
+        mine(0)
         ts(sm[:, 8:12], g1[:, 16:20], ke[0], 1280.0, OP.is_equal, OP.mult, ["g1", "sm/ke0"], ["sm/a1"])
-        tt(T.m2[:, 16:20], T.m2[:, 0:4], T.fm[:, 16:20], OP.mult, ["m2/a", "fm"], ["m2/b"])
+        stays(0)
+        mine(1)
+        ends(1)
         ts(sm[:, 12:16], g1[:, 16:20], ke[0], ke[0], OP.is_equal, OP.mult, ["g1", "sm/ke0"], ["sm/a2"])
-        tt(g2[:], T.cw[:].indirect(T.e16[:, 2:4]), T.m2[:], OP.mult, ["cw", "e16/1", "m2"], ["g2"])
+        tt(g2[:], T.cw[:].indirect(T.e16[:, 2:4]), T.fm[:], OP.mult, ["cw", "e16/1", "fm"], ["g2"])
         most(th[2], g2[:, 0:4], ["g2"], ["sm/th2"])
         cut(2)
-        sort(64, 320 - VSORT)
+        sort(ASORT, 320 - VSORT)
         most(ke[1], g2[:, 16:20], ["g2"], ["sm/ke1"])
         if VSORT:
             sort(320 - VSORT, 320, "V")
-        ts(sm[:, 24:28], g2[:, 16:20], ke[1], None, OP.not_equal, None, ["g2", "sm/ke1"], ["sm/n2"])
-        ends(2)
-        tt(T.m3[:, 0:4], sm[:, 24:28], T.m2[:, 16:20], OP.mult, ["sm/n2", "m2/b"], ["m3/a"])
+        stays(1)
         ts(sm[:, 16:20], g2[:, 16:20], ke[1], ke[0], OP.is_equal, OP.mult, ["g2", "sm/ke1", "sm/ke0"], ["sm/b1"])
-        tt(g3[:], T.cw[:].indirect(T.e16[:, 4:5]), T.m3[:], OP.mult, ["cw", "e16/2", "m3"], ["g3"])
+        ends(2)
         ts(sm[:, 20:24], g2[:, 16:20], ke[1], ke[1], OP.is_equal, OP.mult, ["g2", "sm/ke1"], ["sm/b2"])
-        most(ke[2], g3[:, 0:4], ["g3"], ["sm/ke2"])
+        tt(g3[:], T.cw[:].indirect(T.e16[:, 4:5]), T.fm[:, 16:32], OP.mult, ["cw", "e16/2", "fm"], ["g3"])
         tt(T.tb[:], sm[:, 8:16], sm[:, 16:24], OP.add, ["sm/a1", "sm/a2", "sm/b1", "sm/b2"], ["tb"])
+        most(ke[2], g3[:, 0:4], ["g3"], ["sm/ke2"])
         ts(T.ta[:, 0:4], g3[:, 0:4], ke[2], ke[1], OP.is_equal, OP.mult, ["g3", "sm/ke2", "sm/ke1"], ["ta/a"])
         ts(T.ta[:, 4:8], g3[:, 0:4], ke[2], ke[2], OP.is_equal, OP.mult, ["g3", "sm/ke2"], ["ta/b"])
         ts(T.tb[:, 0:4], T.tb[:, 0:4], ke[2], None, OP.max, None, ["tb", "sm/ke2"], ["tb"])
         tt(T.ge[:], T.ta[:], T.tb[:], OP.max, ["ta", "tb"], ["ge"])
 
-        def slots(i):
+        def slots(i, what):
             k = far[(i + 1) % 4]
-            ts(T.ya[:, 20 * i:20 * i + 20], T.ncs[:], T.ge[:, k:k + 1], T.ge[:, 4 + k:5 + k], OP.add, OP.is_gt,
-               ["ncs", "ge"], ["ya/%d" % i])
-            ts(T.za[:, 20 * i:20 * i + 20], T.cz[:], T.ge[:, k:k + 1], None, OP.subtract, None, ["cz", "ge"],
-               ["za/%d" % i])
+            if "y" in what:
+                ts(T.ya[:, 20 * i:20 * i + 20], T.ncs[:], T.ge[:, k:k + 1], T.ge[:, 4 + k:5 + k], OP.add, OP.is_gt,
+                   ["ncs", "ge"], ["ya/%d" % i])
+            if "z" in what:
+                ts(T.za[:, 20 * i:20 * i + 20], T.cz[:], T.ge[:, k:k + 1], None, OP.subtract, None, ["cz", "ge"],
+                   ["za/%d" % i])
 
         def slots2(a, b):
             tt(T.wa[:, 20 * a:20 * b], T.ya[:, 20 * a:20 * b], T.za[:, 20 * a:20 * b], OP.mult,
@@ -457,16 +485,19 @@ def rank_program(g, core, T, topo):
                 send(qb, 128 * i + 48, i + 1, came, 1)
             else:
                 quant(came, 0, 128, "bt", 960, two("bt", 3), [0])
-        slots(0)
-        slots(1)
+        slots(0, "yz")
+        slots(1, "y")
         slots2(0, 1)
-        slots(2)
+        slots(1, "z")
+        slots(2, "y")
         slots3(0, 1)
-        take("A", 0, 0, 40)
-        take("V", 0, 40, 80)
-        slots(3)
-        slots2(1, 4)
+        take("A", 0, 0, 48)
+        slots(2, "z")
+        slots(3, "y")
+        take("V", 0, 48, 80)
+        slots(3, "z")
         pack_b(0)
+        slots2(1, 4)
         slots3(1, 4)
         take("A", 1, 0, 40)
         take("V", 1, 40, 80)
@@ -535,39 +566,43 @@ def rank_program(g, core, T, topo):
                 tt(xa[:, 1280 + 320 * lo + b:1600 + 320 * hi:4], T["p%d" % (4 + b)][:, w - n:w],
                    T.bt[:, 192 + 320 * i + b:192 + 320 * i + 4 * n:4], OP.add,
                    ["p%d" % (4 + b)] + four("bt", i, i + hi - lo, "ab"), ["%s/n%d%d" % (X, lo, b)])
-        unpack(0, 0)
-        pack_z(0, 0)
-        layer(0, 0)
         ge, sa, sc, se, sf = T.ge, T.sa, T.sc, T.se, T.sf
-        ts(se[:, 60:80], T.rk16[:], -4.0, 1279.0, OP.mult, OP.add, ["rk16"], ["se/r"])
-        ts(sm[:, 32:36], ge[:, 0:4], -320.0, None, OP.add, None, ["ge"], ["sm/l1"])
-        tt(sm[:, 40:44], ge[:, 0:4], T.kc[:], OP.add, ["ge", "kc"], ["sm/h"])
-        tt(sm[:, 36:40], sm[:, 32:36], ge[:, 4:8], OP.max, ["ge", "sm/l1"], ["sm/lo"])
-        for k in range(4):
-            ts(sa[:, 20 * k:20 * k + 20], se[:, 60:80], ge[:, k:k + 1], sm[:, 40 + k:41 + k], OP.is_lt, OP.mult,
-               ["se/r", "ge", "sm/h"], ["sa/%d" % k])
-        pack_h(0, 0)
-        for k in range(4):
-            ts(sc[:, 20 * k:20 * k + 20], se[:, 60:80], sm[:, 36 + k:37 + k], None, OP.is_gt, None,
-               ["se/r", "sm/lo"], ["sc/%d" % k])
-        tt(sf[:], sa[:], sc[:], OP.mult, ["sa", "sc"], ["sf"])
-        if r == 0:
-            quant("quo", 0, 128, "uo", 3, ["uo"], [0])
-        tt(se[:, 0:40], sf[:, 0:40], sf[:, 40:80], OP.add, ["sf"], ["se/a"])
-        if r == 0:
-            quant("quo", 128, 256, "uo", 2, ["uo"], [1])
-        tt(se[:, 40:60], se[:, 0:20], se[:, 20:40], OP.add, ["se/a"], ["se/b"])
+
+        def where(step, same):
+            if step == 0:
+                ts(se[:, 60:80], T.rk16[:], -4.0, 1279.0, OP.mult, OP.add, ["rk16"], ["se/r"])
+                ts(sm[:, 32:36], ge[:, 0:4], -320.0, None, OP.add, None, ["ge"], ["sm/l1"])
+                tt(sm[:, 40:44], ge[:, 0:4], T.kc[:], OP.add, ["ge", "kc"], ["sm/h"])
+                tt(sm[:, 36:40], sm[:, 32:36], ge[:, 4:8], OP.max, ["ge", "sm/l1"], ["sm/lo"])
+            elif step == 1:
+                for k in range(4):
+                    ts(sa[:, 20 * k:20 * k + 20], se[:, 60:80], ge[:, k:k + 1], sm[:, 40 + k:41 + k], OP.is_lt,
+                       OP.mult, ["se/r", "ge", "sm/h"], ["sa/%d" % k])
+            elif step == 2:
+                for k in range(4):
+                    ts(sc[:, 20 * k:20 * k + 20], se[:, 60:80], sm[:, 36 + k:37 + k], None, OP.is_gt, None,
+                       ["se/r", "sm/lo"], ["sc/%d" % k])
+            elif step == 3:
+                tt(sf[:], sa[:], sc[:], OP.mult, ["sa", "sc"], ["sf"])
+            elif step == 4:
+                tt(se[:, 0:40], sf[:, 0:40], sf[:, 40:80], OP.add, ["sf"], ["se/a"])
+            elif step == 5:
+                tt(se[:, 40:60], se[:, 0:20], se[:, 20:40], OP.add, ["se/a"], ["se/b"])
+            elif step == 6:
+                tt(sa[:, 0:20], se[:, 40:60], se[:, 60:80], OP.subtract, ["se/b", "se/r"], ["sa/0"])
+            elif step == 7:
+                tt(sa[:, 20:40], sa[:, 0:20], T.old[:], OP.max, ["sa/0", "old"], ["sa/1"])
+            else:
+                for t in range(4):
+                    ts(T.po16[:, 20 * t:20 * t + 20], sa[:, 20:40], float(t), None, OP.add, None, ["sa/1"],
+                       ["po16/%d" % t])
+
+        def ones(b, same):
+            if r == 0:
+                quant("quo", 128 * b, 128 * b + 128, "uo", 3 - b, ["uo"], [b])
         for step in PLAN.split():
-            {"U": unpack, "Z": pack_z, "W": layer, "H": pack_h}[step[0]](int(step[1]), int(step[-1]))
-        tt(sa[:, 0:20], se[:, 40:60], se[:, 60:80], OP.subtract, ["se/b", "se/r"], ["sa/0"])
-        if r == 0:
-            quant("quo", 256, 384, "uo", 1, ["uo"], [2])
-        tt(sa[:, 20:40], sa[:, 0:20], T.old[:], OP.max, ["sa/0", "old"], ["sa/1"])
-        if r == 0:
-            quant("quo", 384, 512, "uo", 0, ["uo"], [3])
-        for t in range(4):
-            ts(T.po16[:, 20 * t:20 * t + 20], sa[:, 20:40], float(t), None, OP.add, None, ["sa/1"], ["po16/%d" % t])
-        renew(0, 0)
+            {"U": unpack, "Z": pack_z, "W": layer, "H": pack_h, "S": where, "O": ones,
+             "R": renew}[step[0]](int(step[1]), int(step[-1]))
         if r == NR - 1:
             ts(T.po16[:, 80:100], sa[:, 20:40], 0.25, None, OP.mult, None, ["sa/1"], ["po16/s"])
             act(T.eq[:], T.slt[:].indirect(T.po16[:, 80:100]), AF.Copy, ["slt", "po16/s"], ["eq"])

@@ -9,13 +9,13 @@ B16 = 1024.0
 B4 = 2.0 ** 21
 CUT = ((46, 128), (101, 224), (174, 288))
 CT = (0, 320, 576, 768, 896, 1024)
-ALONE = (15, 14, 13, 12, 11, 10)
 S0 = 16
-ORDER = "c19 c18 c17 d0 c16 q0 c9 c8 c7 c6 c5 c4 c3 c2 c1 q1 s19 s18 s17 s16 r1 q2 b1 q3 q4 r0 b0"
-VSORT = 16
-ASORT = 64
-PLAN = "U0 Z0 O0 O1 O2 O3 U1 Z1 U2 Z2 W1 S0 H1 U3 Z3 W2 S1 H2 W3 S2 H3 W0 S3 S4 S5 S6 H0 S7 S8 R0"
-BACK = "1 2 3"
+ORDER = "V00 A30 V20 A10 A11 x0 V21 k0 A31 K0 V01 D0 x1 T0 K1 k1 m0 m1 v0 u0 c8 c9 D1 w8 v1 w9 c7 c6 N0 w6 T1 c4 d0 c19 c18 w7 u1 a15 d1 c17 c16 a14 c2 e15 c3 c1 a13 c5 q0 e14 e13 a12 a11 s16 e12 c10 e11 q4 w1 q1 s19 w2 q3 r1 N1 w5 s17 q2 s18 r0 w4 w3 w10 b1 b0"
+END = "V00 A10 V20 A30 V01 A11 x0 A31 V21 y0A x1 o0A s0S s1A s2S s3A y1V o1S"
+SPLIT = (0, 320)
+CLAIMS = "c0 x0 w1 e0 m0 i0 g0 n0 t0 c1 k0 l0 a0 s0 A000096 b0 e1 g1 m1 t1 c2 k1 A096304 V304320 s1 e2 b1 a1 g2 d0 k2 a2 b2 d1 d2"
+PLAN0 = "f0 m0 a0 m1 f1 g0 a1 f2 b0 m2 g1 a2 f3 m3 b1 g2 a3 e0 b2 g3 b3 h0 h1 h2 h3 S0 U0 Z0 O0 W0 U1 Z1 O1 O2 U2 S1 H0 W1 Z2 H1 U3 Z3 W2 W3 S2 H2 O3 S3 S4 H3 R0 S5 S6 S7 S8 R1 R2 R3"
+PLAN = "f0 m0 a0 m1 f2 f1 g0 m2 a1 b0 g1 m3 a2 f3 e0 b1 a3 g2 g3 b2 b3 U0 U1 Z1 Z0 U2 Z2 S0 W1 H1 U3 Z3 S1 S2 W2 H2 S3 W3 W0 S4 H3 S5 S6 H0 S7 R0 L0 R1 L1 R2 S8 R3"
 
 
 def _scratch():
@@ -28,7 +28,7 @@ def _scratch():
     def code(n, w):
         s[n] = ("sbuf", [128, w], F8)
         s[n + "s"] = ("sbuf", [128, w], U8)
-    sb(BF, x0=2560, x1=2560, x2=1280, xs=1296, ut=512, vt=512, eg=512, one=528, uo=528, uh=528, bt=1472,
+    sb(BF, x0=2560, x1=2560, x2=1280, xs=1488, nr=192, mk=768, ut=512, vt=512, eg=512, one=528, uo=528, uh=528, bt=1472,
        eh=960, z=1472, h=1472, junk=1280, sg=1280, ct=4096, rs=320, rc=320, rb=608)
     for n, w in (("qu", 128), ("qur", 128), ("qv", 128), ("wq", 512), ("qx", 320), ("qeg", 128), ("quh", 512),
                  ("quo", 512), ("qz", 512), ("qc", 1024)):
@@ -50,7 +50,7 @@ def _scratch():
 
 
 SCRATCH = _scratch()
-SEMAPHORES = (["sV", "sA", "sP", "sG", "gd", "ls", "dx", "du", "dw", "dv", "out"]
+SEMAPHORES = (["sV", "sA", "sP", "sG", "gd", "ls", "dx", "dy", "du", "dw", "dv", "out"]
               + ["%s%d_%d" % (p, r, i) for p in ("came", "back") for r in range(NR) for i in (1, 2, 3)])
 
 
@@ -189,11 +189,11 @@ def rank_program(g, core, T, topo):
                                       T[mov][:, ma:ma + n], T[mov + "s"][:, ma:ma + n], start, stop),
            keys(sta, ssub) + keys(mov, msub), [p], acc=not start)
 
-    dma("S", lambda e: e.dma_start(T.x0[:, 0:1280], T.x[:]), ("dx", 16), [], ["x0/x"])
+    dma("S", lambda e: e.dma_start(T.x0[:, 0:640], T.x[:, 0:640]), ("dx", 16), [], ["x0/x0"])
     dma("A", lambda e: e.dma_start(T.ut[:], T.u[:]), ("du", 16), [], ["ut"])
-    dma("S", lambda e: e.dma_start(T.wq[:].bitcast(dt.uint8), T.wc[:]), ("dw", 32), ["x0/x", "ut"], ["wq"])
+    dma("S", lambda e: e.dma_start(T.x0[:, 640:1280], T.x[:, 640:1280]), ("dy", 16), [], ["x0/x1"])
+    dma("S", lambda e: e.dma_start(T.wq[:].bitcast(dt.uint8), T.wc[:]), ("dw", 32), ["x0/x1", "ut"], ["wq"])
     dma("S", lambda e: e.dma_start(T.wqs[:], T.ws[:]), ("dw", 32), [], ["wqs"])
-    dma("S", lambda e: e.dma_start(T.vt[:], T.v[:]), ("dv", 16), [], ["vt"])
 
     iota(T.pi[:, 0:1], [[0, 1]], 0, 1, ["pi/0"], False)
     iota(T.xi[:, 0:8], [[16, 8]], 4, 0, ["xi"], False)
@@ -224,7 +224,7 @@ def rank_program(g, core, T, topo):
     for j in range(4, 8):
         act(T.eg[:, 64 * j:64 * j + 64], T.one[:, 0:64], AF.Copy, ["one", "e8"], ["eg/%d" % j], scale=T.e8[:, j:j + 1])
 
-    select(T.uo[:], T.one[:], [[1, 528]], OP.is_equal, -3, -4, ["one"], ["uo"])
+    dma("G", lambda e: e.dma_start(T.vt[:], T.v[:]), ("dv", 16), [], ["vt"])
 
     def product_constants():
         ts(T.k16[:], T.i16[:], T.pc[:, 0:1], 34 * B16, OP.is_gt, OP.mult, ["i16", "pc/0"], ["k16"])
@@ -240,17 +240,20 @@ def rank_program(g, core, T, topo):
 
     def late_constants():
         iota(T.i4[:], [[0, 80], [1, 4]], 0, 0, ["i4"])
-        iota(T.cw[:, 344:664], [[-4, 320]], 1276, 0, ["cw/i"])
+        select(T.uo[:], T.one[:], [[1, 528]], OP.is_equal, -3, -4, ["one"], ["uo"])
+        iota(T.cw[:, 8:328], [[-4, 320]], 1276, 0, ["cw/i"])
         iota(T.cw[:, 0:8], [[0, 8]], 0, 0, ["cw/y"])
         iota(T.cw[:, 328:344], [[0, 16]], 0, 0, ["cw/z"])
         iota(T.xs[:, 0:16], [[0, 16]], 0, 0, ["xs/z"])
+        iota(T.xs[:, 1296:1488], [[0, 192]], 0, 0, ["xs/y"])
+        iota(T.nr[:], [[-4, 48], [0, 4]], -130, 0, ["nr"])
         for s in range(3):
-            iota(T.cst[:, 2 * s:2 * s + 2], [[672, 2]], CUT[s][0] + CUT[s][1] + 14, 0, ["cst/%d" % s])
+            iota(T.cst[:, 2 * s:2 * s + 2], [[-672, 2]], CUT[s][0] + CUT[s][1] + 686, 0, ["cst/%d" % s])
         for k in range(4):
             iota(T.kc[:, k:k + 1], [[0, 1]], 1279 + 320 * far.index(k), 0, ["kc/%d" % k])
-        for n in ("bt", "z"):
+        iota(T.bt[:, 320:512], [[0, 192]], 0, 0, ["bt/0a", "bt/0b"])
+        for n in ("bt", "z", "h"):
             iota(T[n][:, 0:192], [[0, 192]], 0, 0, [n + "/pad"])
-        iota(T.h[:, 0:512], [[0, 512]], 0, 0, ["h"])
 
     gdn, jn, lsn = [0], [0], [0]
 
@@ -264,12 +267,15 @@ def rank_program(g, core, T, topo):
 
     def send(src, a, i, dst, step):
         to = T.cores[(rank + step * far[i]) % N]
-        en = topo.engines(core, to)
-        mask = topo.mask(core, to)
         ad = topo.addr(to)
         b = 48 + 80 * i
         name = "%s_%d" % (dst, i)
+        apart = lsn[0] == 0
         for planes in (False, True):
+            en = topo.engines(core, to)
+            if apart:
+                en = en[len(en) // 2:] if planes else en[:len(en) // 2]
+            mask = sum(1 << x for x in en)
             if planes:
                 s_ap, d_ap = T[src + "s"][:, a:a + 80], T[dst + "s"][:, b:b + 80]
             else:
@@ -279,29 +285,61 @@ def rank_program(g, core, T, topo):
                    ["%s%s/%d" % (src, "s" if planes else "", i)])
         arrive((name, 2 * len(en)), keys(dst, [i]))
 
+    def state(r, h):
+        return ["x%d/x%d" % (r, h)] if r == 0 else ["x%d/x%d%d" % (r, t, h) for t in range(4)]
+
+    def collect(r, step):
+        t, h = int(step[1]), int(step[2])
+        old = "x%d" % (r - 1)
+        o = T["x%d" % r][:, 640 * h + t:640 * h + 640:4]
+        w = T[old][:].indirect(T.po16[:, 20 * t + 10 * h:20 * t + 10 * h + 10])
+        if step[0] == "A":
+            act(o, w, AF.Copy, [old, "po16/%d" % t], ["x%d/x%d%d" % (r, t, h)])
+        else:
+            cp(o, w, [old, "po16/%d" % t], ["x%d/x%d%d" % (r, t, h)])
+
     for r in range(NR):
-        X, XN = "x%d" % r, "x%d" % (r + 1)
-        xa, xn = T[X], T[XN]
-        xk = [X + "/x"] if r == 0 else [X + "/x%d" % t for t in range(4)]
+        X = "x%d" % r
+        xa = T[X]
+        xk = state(r, 0) + state(r, 1)
         came, back, qb, qh = "came%d" % r, "back%d" % r, "qb%d" % r, "qh%d" % r
-        quant("qx", 0, 320, X, 0, xk)
-        mm(0, 320, "qur", 0, "qx", 0)
-        mm(2, 320, "qu", 0, "qx", 0)
-        mm(1, 320, "qur", 0, "qx", 0)
-        if r == 0:
-            product_constants()
-        tt(T.d1[:], T.p0[:, 0:320], T.mm[:], OP.add, ["p0", "mm"], ["d1"])
-        scan(T.st[:], T.d0[:], T.d1[:], -NEG, OP.min, OP.max, ["d0", "d1"], ["st"])
-        act(T.v4[:], T.p2[:, 0:320], AF.Sign, ["p2"], ["v4"])
-        act(T.v4[:], T.v4[:], AF.Relu, ["v4"], ["v4", "acc/t"], scale=UNIT, accum_out=T.acc[:, 4:5])
-        gdn[0] += 16
-        dma("G", lambda e: e.dma_start(T.v4[:], T.ij[:], accum_op=OP.add), ("gd", gdn[0]), ["ij"], ["v4"])
-        if r == 0:
-            late_constants()
-        if r == NR - 1:
-            iota(T.slt[:, 0:320], [[0, 320]], -1, 0, ["slt/n"])
-            for j in range(4):
-                iota(T.slt[:, 320 + 80 * j:400 + 80 * j], [[1, 80]], 80 * far[j], 0, ["slt/%d" % j])
+
+        def half(step):
+            h = int(step[1])
+            lo, hi, pa, pb = 160 * h, 160 * h + 160, "p%d" % (4 + 2 * h), "p%d" % (5 + 2 * h)
+            if step[0] == "x":
+                quant("qx", lo, hi, X, 4 * lo, state(r, h), [h])
+                mm(4 + 2 * h, 160, "qur", 0, "qx", lo, msub=[h])
+            elif step[0] == "k":
+                mm(5 + 2 * h, 160, "qu", 0, "qx", lo, msub=[h])
+            elif step[0] == "m":
+                mm(h, 320, "qur", 0, "qx", 0)
+            elif step[0] == "D":
+                tt(T.d1[:, lo:hi], T[pa][:, 0:160], T.mm[:, lo:hi], OP.add, [pa, "mm"], ["d1/%d" % h])
+            elif step[0] == "T":
+                scan(T.st[:, lo:hi], T.d0[:, lo:hi], T.d1[:, lo:hi], -NEG, OP.min, OP.max, ["d0", "d1/%d" % h],
+                     ["st/%d" % h])
+            elif step[0] == "d":
+                tt(T.ct[:, 4 * lo:4 * hi:4], T.st[:, lo:hi], T[pa][:, 0:160], OP.is_ge, [pa, "st/%d" % h, "ct/z0"],
+                   ["ct/20" + "ab"[h]])
+            elif step[0] == "v":
+                act(T.v4[:, lo:hi], T[pb][:, 0:160], AF.Sign, [pb], ["v4/%d" % h])
+            elif step[0] == "u":
+                act(T.v4[:, lo:hi], T.v4[:, lo:hi], AF.Relu, ["v4/%d" % h], ["v4/%d" % h, "acc/t%d" % h], scale=UNIT,
+                    accum_out=T.acc[:, 6 + h:7 + h])
+                dma("G", lambda e: e.dma_start(T.v4[:, lo:hi], T.ij[:, lo:hi], accum_op=OP.add), ("gd", 32 * r + 32),
+                    ["ij"], ["v4/%d" % h])
+                if h:
+                    if r == 0:
+                        late_constants()
+                    if r == NR - 1:
+                        iota(T.slt[:, 0:320], [[0, 320]], -1, 0, ["slt/n"])
+                        for j in range(4):
+                            iota(T.slt[:, 320 + 80 * j:400 + 80 * j], [[1, 80]], 80 * far[j], 0, ["slt/%d" % j])
+            elif h == 0:
+                act(T.acc[:, 4:5], T.acc[:, 6:7], AF.Copy, ["acc/t0"], ["acc/t"], bias=319.6 * UNIT)
+            else:
+                act(T.acc[:, 5:6], T.acc[:, 7:8], AF.Identity, ["acc/t", "acc/t1"], ["acc/T"], bias=T.acc[:, 4:5])
 
         def place(c):
             b, t = (20 - c) // 4, (20 - c) % 4
@@ -312,7 +350,9 @@ def rank_program(g, core, T, topo):
 
         def compare(c):
             o, key = place(c)
-            ts(o, T.p0[:, 0:16 * c], own(c), None, OP.is_lt, None, ["p0", "st", "ct/z%d" % ((20 - c) // 4)], [key])
+            p = "p4" if c <= 10 else "p0"
+            ts(o, T[p][:, 0:16 * c], own(c), None, OP.is_lt, None,
+               [p, "st/%d" % (c // 10), "ct/z%d" % ((20 - c) // 4)], [key])
 
         def rows(c):
             o, key = place(c)
@@ -320,13 +360,12 @@ def rank_program(g, core, T, topo):
             act(T.junk[:, 320 * jn[0]:320 * jn[0] + 16 * c], o, AF.Copy, [key], ["junk/%d" % jn[0], "rsum/%d" % c],
                 accum_out=T.rsum[:, c:c + 1])
 
-        def alone(cs):
-            for c in cs:
-                i = c % 4
-                act(T.sg[:, 320 * i:320 * i + 16 * c], T.p1[:, 0:16 * c], AF.Sign, ["p1", "st"], ["sg/%d" % i],
-                    scale=-1.0, bias=own(c))
-            for c in cs:
-                i = c % 4
+        def alone(what, c):
+            i = c % 4
+            if what == "a":
+                act(T.sg[:, 320 * i:320 * i + 16 * c], T.p1[:, 0:16 * c], AF.Sign, ["p1", "st/%d" % (c // 10)],
+                    ["sg/%d" % i], scale=-1.0, bias=own(c))
+            else:
                 o, key = place(c)
                 act(o, T.sg[:, 320 * i:320 * i + 16 * c], AF.Relu, ["sg/%d" % i, "ct/z%d" % ((20 - c) // 4)],
                     [key, "rsum/%d" % c], accum_out=T.rsum[:, c:c + 1])
@@ -340,29 +379,36 @@ def rank_program(g, core, T, topo):
         def count(b):
             w = CT[b + 1] - CT[b]
             quant("qc", CT[b], CT[b + 1], "ct", 4 * CT[b],
-                  ["ct/z%d" % b] + ["ct/%d" % (20 - 4 * b - t) for t in range(4)], [b])
-            mm(3, w, "qeg", 0, "qc", CT[b], b == 0, b == 4, msub=[b])
-        for i in range(0, len(ALONE), 2):
-            alone(ALONE[i:i + 2])
-        act(T.acc[:, 5:6], T.acc[:, 4:5], AF.Copy, ["acc/t"], ["acc/T"], bias=319.6 * UNIT)
+                  ["ct/z%d" % b, "ct/20a", "ct/20b"][:3 if b == 0 else 1]
+                  + ["ct/%d" % (20 - 4 * b - t) for t in range(4)], [b])
+            turn = [int(s[1]) for s in ORDER.split() if s[0] == "q"]
+            mm(3, w, "qeg", 0, "qc", CT[b], b == turn[0], b == turn[-1], msub=[b])
         for step in ORDER.split():
+            if step[0] in "VA":
+                if r:
+                    collect(r, step)
+                continue
+            if step[0] in "xkmDTdvuN":
+                half(step)
+                continue
             c = int(step[1:])
             if step[0] == "c":
                 compare(c)
-                if c < S0:
-                    rows(c)
+            elif step[0] == "w":
+                rows(c)
+            elif step[0] in "ae":
+                alone(step[0], c)
             elif step[0] == "s":
                 sums(c)
+            elif step[0] == "K":
+                if r == 0:
+                    (product_constants, lambda: quant("qeg", 0, 128, "eg", 0, ["eg"]))[c]()
             elif step[0] == "q":
-                if r == 0 and c == 0:
-                    quant("qeg", 0, 128, "eg", 0, ["eg"])
                 count(c)
-            elif step[0] == "d":
-                tt(T.ct[:, 0:1280:4], T.st[:], T.p0[:, 0:320], OP.is_ge, ["p0", "st", "ct/z0"], ["ct/20"])
             elif step[0] == "r":
                 lo, hi = ((0, 16 * S0), (16 * S0, 320))[c]
                 scan(T.rc[:, lo:hi], T.rs[:, lo:hi], T.ct[:, 4 * lo:4 * hi:4], 1.0e4, OP.min, OP.add,
-                     ["rs", "ct/20"], ["rc/%d" % c])
+                     ["rs", "ct/20a", "ct/20b"], ["rc/%d" % c])
             elif c == 0:
                 tt(T.rcb[:, 0:S0], T.rc[:, 15:16 * S0:16], T.rsum[:, 0:S0], OP.add, ["rc/0", "rsum"], ["rcb/0"])
             else:
@@ -381,8 +427,8 @@ def rank_program(g, core, T, topo):
         tt(T.rk[:], T.rx[:, 15:320:16], T.rcb[:], OP.subtract, ["rx", "rcb"], ["rk"])
         ts(T.rk16[:], T.rk[:], T.pc[:, 3:4], None, OP.subtract, None, ["rk", "pc/3"], ["rk16"])
         cp(T.wrow[:].indirect(T.rk16[:, 0:20]), T.v4[:], ["rk16", "v4"], ["wrow"])
-        scan(T.cw[:, 8:328], T.on[:], T.wrow[:], T.acc[:, 5:6], OP.add, OP.subtract, ["wrow", "on", "acc/T"],
-             ["cw/s"])
+        scan(T.cw[:, 344:472], T.on[:, 0:128], T.wrow[:, 0:128], T.acc[:, 5:6], OP.add, OP.subtract,
+             ["wrow", "on", "acc/T"], ["cw/s"])
         sm = T.sm
         th = [T.acc[:, 5:6], sm[:, 0:1], sm[:, 1:2]]
         ke = [sm[:, 2:3], sm[:, 3:4], sm[:, 4:5]]
@@ -390,8 +436,8 @@ def rank_program(g, core, T, topo):
 
         def cut(s):
             lo, hi = CUT[s]
-            act(T.junk[:, 320 * s:320 * s + hi - lo], T.cw[:, lo + 7:hi + 7], AF.Sign,
-                ["cw/s", "acc/T" if s == 0 else "sm/th%d" % s], ["junk/%d" % s, "acc/%d" % s],
+            act(T.junk[:, 320 * s:320 * s + hi - lo], T.cw[:, lo + 343:hi + 343], AF.Sign,
+                ["cw/s", "acc/T"] if s == 0 else ["cw/s", "cw/t", "sm/th%d" % s], ["junk/%d" % s, "acc/%d" % s],
                 bias=th[s], scale=-(4.0 - s) / (3.0 - s), accum_out=T.acc[:, s:s + 1])
 
         def ends(s):
@@ -410,46 +456,61 @@ def rank_program(g, core, T, topo):
 
         def sort(lo, hi, eng="A"):
             o, i = T.xs[:, 16 + 4 * lo:16 + 4 * hi], xa[:, 0:1280].indirect(T.ol[:, lo // 4:hi // 4])
+            k = xk + ["ol/%d" % h for h in range(len(SPLIT) - 1) if lo < SPLIT[h + 1] and hi > SPLIT[h]]
             if eng == "A":
-                act(o, i, AF.Copy, xk + ["ol"], ["xs/%d" % lo])
+                act(o, i, AF.Copy, k, ["xs/%d" % lo])
             else:
-                cp(o, i, xk + ["ol"], ["xs/%d" % lo])
+                cp(o, i, k, ["xs/%d" % lo])
         g1, g2, g3 = T.g1, T.g2, T.g3
-        cut(0)
-        scan(T.ox[:], T.k4[:], T.wrow[:], 0.0, OP.add, OP.max, ["k4", "wrow"], ["ox"])
-        ends(0)
-        cp(T.oi[:, 0:80], T.ox[:, 3:320:4], ["ox"], ["oi/a"])
-        tt(g1[:], T.cw[:].indirect(T.e16[:, 0:2]), T.fm[:], OP.mult, ["cw", "e16/0", "fm"], ["g1"])
-        ts(T.oi[:, 80:160], T.oi[:, 0:80], 511, None, OP.bitwise_and, None, ["oi/a"], ["oi/b"])
-        most(th[1], g1[:, 0:4], ["g1"], ["sm/th1"])
-        cut(1)
-        most(ke[0], g1[:, 16:20], ["g1"], ["sm/ke0"])
-        ts(T.ol[:], T.oi[:, 80:160], 4.0, T.pc[:, 1:2], OP.mult, OP.add, ["oi/b", "pc/0"], ["ol"])
-        sort(0, ASORT)
-        mine(0)
-        ts(sm[:, 8:12], g1[:, 16:20], ke[0], 1280.0, OP.is_equal, OP.mult, ["g1", "sm/ke0"], ["sm/a1"])
-        stays(0)
-        mine(1)
-        ends(1)
-        ts(sm[:, 12:16], g1[:, 16:20], ke[0], ke[0], OP.is_equal, OP.mult, ["g1", "sm/ke0"], ["sm/a2"])
-        tt(g2[:], T.cw[:].indirect(T.e16[:, 2:4]), T.fm[:], OP.mult, ["cw", "e16/1", "fm"], ["g2"])
-        most(th[2], g2[:, 0:4], ["g2"], ["sm/th2"])
-        cut(2)
-        sort(ASORT, 320 - VSORT)
-        most(ke[1], g2[:, 16:20], ["g2"], ["sm/ke1"])
-        if VSORT:
-            sort(320 - VSORT, 320, "V")
-        stays(1)
-        ts(sm[:, 16:20], g2[:, 16:20], ke[1], ke[0], OP.is_equal, OP.mult, ["g2", "sm/ke1", "sm/ke0"], ["sm/b1"])
-        ends(2)
-        ts(sm[:, 20:24], g2[:, 16:20], ke[1], ke[1], OP.is_equal, OP.mult, ["g2", "sm/ke1"], ["sm/b2"])
-        tt(g3[:], T.cw[:].indirect(T.e16[:, 4:5]), T.fm[:, 16:32], OP.mult, ["cw", "e16/2", "fm"], ["g3"])
-        tt(T.tb[:], sm[:, 8:16], sm[:, 16:24], OP.add, ["sm/a1", "sm/a2", "sm/b1", "sm/b2"], ["tb"])
-        most(ke[2], g3[:, 0:4], ["g3"], ["sm/ke2"])
-        ts(T.ta[:, 0:4], g3[:, 0:4], ke[2], ke[1], OP.is_equal, OP.mult, ["g3", "sm/ke2", "sm/ke1"], ["ta/a"])
-        ts(T.ta[:, 4:8], g3[:, 0:4], ke[2], ke[2], OP.is_equal, OP.mult, ["g3", "sm/ke2"], ["ta/b"])
-        ts(T.tb[:, 0:4], T.tb[:, 0:4], ke[2], None, OP.max, None, ["tb", "sm/ke2"], ["tb"])
-        tt(T.ge[:], T.ta[:], T.tb[:], OP.max, ["ta", "tb"], ["ge"])
+
+        def won(o, gs, s, by, key, more=()):
+            ts(o, gs, ke[s], by, OP.is_equal, OP.mult, ["g%d" % (s + 1), "sm/ke%d" % s] + list(more), [key])
+
+        def listed(what, h):
+            lo, hi = SPLIT[h], SPLIT[h + 1]
+            a, b = lo // 4, hi // 4
+            if what == "x":
+                scan(T.ox[:, lo:hi], T.k4[:, lo:hi], T.wrow[:, lo:hi], 0.0, OP.add, OP.max, ["k4", "wrow"],
+                     ["ox/%d" % h])
+            elif what == "i":
+                cp(T.oi[:, a:b], T.ox[:, lo + 3:hi:4], ["ox/%d" % h], ["oi/a%d" % h])
+            elif what == "n":
+                ts(T.oi[:, 80 + a:80 + b], T.oi[:, a:b], 511, None, OP.bitwise_and, None, ["oi/a%d" % h],
+                   ["oi/b%d" % h])
+            else:
+                ts(T.ol[:, a:b], T.oi[:, 80 + a:80 + b], 4.0, T.pc[:, 1:2], OP.mult, OP.add, ["oi/b%d" % h, "pc/0"],
+                   ["ol/%d" % h])
+        steps = {
+            "g0": lambda: tt(g1[:], T.cw[:, 0:472].indirect(T.e16[:, 0:2]), T.fm[:], OP.mult,
+                             ["cw/s", "cw/i", "cw/y", "cw/z", "e16/0", "fm"], ["g1"]),
+            "g1": lambda: tt(g2[:], T.cw[:].indirect(T.e16[:, 2:4]), T.fm[:], OP.mult, ["cw", "e16/1", "fm"], ["g2"]),
+            "g2": lambda: tt(g3[:], T.cw[:].indirect(T.e16[:, 4:5]), T.fm[:, 16:32], OP.mult, ["cw", "e16/2", "fm"],
+                             ["g3"]),
+            "w1": lambda: scan(T.cw[:, 472:664], T.on[:, 128:320], T.wrow[:, 128:320], T.cw[:, 471:472], OP.add,
+                               OP.subtract, ["wrow", "on", "cw/s"], ["cw/t"]),
+            "t0": lambda: most(th[1], g1[:, 0:4], ["g1"], ["sm/th1"]),
+            "t1": lambda: most(th[2], g2[:, 0:4], ["g2"], ["sm/th2"]),
+            "k0": lambda: most(ke[0], g1[:, 16:20], ["g1"], ["sm/ke0"]),
+            "k1": lambda: most(ke[1], g2[:, 16:20], ["g2"], ["sm/ke1"]),
+            "k2": lambda: most(ke[2], g3[:, 0:4], ["g3"], ["sm/ke2"]),
+            "a0": lambda: won(sm[:, 8:12], g1[:, 16:20], 0, 1280.0, "sm/a1"),
+            "b0": lambda: won(sm[:, 12:16], g1[:, 16:20], 0, ke[0], "sm/a2"),
+            "a1": lambda: won(sm[:, 16:20], g2[:, 16:20], 1, ke[0], "sm/b1", ["sm/ke0"]),
+            "b1": lambda: won(sm[:, 20:24], g2[:, 16:20], 1, ke[1], "sm/b2"),
+            "a2": lambda: won(T.ta[:, 0:4], g3[:, 0:4], 2, ke[1], "ta/a", ["sm/ke1"]),
+            "b2": lambda: won(T.ta[:, 4:8], g3[:, 0:4], 2, ke[2], "ta/b"),
+            "d0": lambda: tt(T.tb[:], sm[:, 8:16], sm[:, 16:24], OP.add, ["sm/a1", "sm/a2", "sm/b1", "sm/b2"], ["tb"]),
+            "d1": lambda: ts(T.tb[:, 0:4], T.tb[:, 0:4], ke[2], None, OP.max, None, ["tb", "sm/ke2"], ["tb"]),
+            "d2": lambda: tt(T.ge[:], T.ta[:], T.tb[:], OP.max, ["ta", "tb"], ["ge"])}
+        for step in CLAIMS.split():
+            if step in steps:
+                steps[step]()
+            elif step[0] in "AV":
+                sort(int(step[1:4]), int(step[4:7]), step[0])
+            elif step[0] in "xinl":
+                listed(step[0], int(step[1]))
+            else:
+                {"c": cut, "e": ends, "m": mine, "s": stays}[step[0]](int(step[1]))
 
         def slots(i, what):
             k = far[(i + 1) % 4]
@@ -468,9 +529,10 @@ def rank_program(g, core, T, topo):
             cp(T.ob[:, 20 * a:20 * b], T.wa[:, 20 * a:20 * b], ["wa/%d" % a], ["ob/%d" % i for i in range(a, b)])
 
         def take(eng, i, lo, hi):
-            o = T.bt[:, 192 + 320 * i + 4 * lo:192 + 320 * i + 4 * hi]
+            j = (i + 1) % 4
+            o = T.bt[:, 192 + 320 * j + 4 * lo:192 + 320 * j + 4 * hi]
             w = T.xs[:].indirect(T.ob[:, 20 * i + lo // 4:20 * i + hi // 4])
-            k = ["bt/%d%s" % (i, "a" if lo == 0 else "b")] + (["bt/%db" % i] if (lo, hi) == (0, 80) else [])
+            k = ["bt/%d%s" % (j, "a" if lo == 0 else "b")] + (["bt/%db" % j] if (lo, hi) == (0, 80) else [])
             if eng == "V":
                 cp(o, w, ["xs", "ob/%d" % i], k)
             else:
@@ -481,38 +543,41 @@ def rank_program(g, core, T, topo):
 
         def pack_b(i):
             if i < 3:
-                quant(qb, 128 * i, 128 * i + 128, "bt", 320 * i, two("bt", i), [i + 1])
+                quant(qb, 128 * i, 128 * i + 128, "bt", 320 * i + 320, two("bt", i + 1), [i + 1])
                 send(qb, 128 * i + 48, i + 1, came, 1)
             else:
-                quant(came, 0, 128, "bt", 960, two("bt", 3), [0])
-        slots(0, "yz")
-        slots(1, "y")
-        slots2(0, 1)
-        slots(1, "z")
-        slots(2, "y")
-        slots3(0, 1)
-        take("A", 0, 0, 48)
-        slots(2, "z")
-        slots(3, "y")
-        take("V", 0, 48, 80)
-        slots(3, "z")
-        pack_b(0)
-        slots2(1, 4)
-        slots3(1, 4)
-        take("A", 1, 0, 40)
-        take("V", 1, 40, 80)
-        take("A", 2, 0, 56)
-        pack_b(1)
-        take("V", 2, 56, 80)
-        take("A", 3, 0, 40)
-        pack_b(2)
-        take("V", 3, 40, 80)
-        for i in range(max(int(s[-1]) - int(s[1]) + 1 for s in PLAN.split() if s[0] == "U")):
-            act(T.eh[:, 320 * i:320 * i + 320], T.xs[:, 16:336], AF.Copy, ["xs"], ["eh/%d" % i], scale=0.5)
-        if r == 0:
-            for b in range(4):
-                quant("quh", 128 * b, 128 * b + 128, "uh", 3 - b, ["uh"], [b])
-        pack_b(3)
+                quant(came, 0, 128, "bt", 0, two("bt", 0), [0])
+
+        def deal(step):
+            i = int(step[1])
+            if step[0] == "p":
+                if r == 0:
+                    quant(("came0", "back0", "came1", "back1")[i], 0, 128, "z", 0, four("z", -1, 0), [0])
+            elif step[0] in "fmga":
+                j, k = (i + 1) % 4, far[(i + 1) % 4]
+                if step[0] == "f":
+                    ts(T.ob[:, 20 * i:20 * i + 20], T.cz[:], T.ge[:, k:k + 1], None, OP.subtract, None, ["cz", "ge"],
+                       ["ob/%d" % i])
+                elif step[0] == "m":
+                    ts(T.mk[:, 192 * i:192 * i + 192], T.nr[:], T.ge[:, k:k + 1], T.ge[:, 4 + k:5 + k], OP.add,
+                       OP.is_gt, ["nr", "ge"], ["mk/%d" % i])
+                elif step[0] == "g":
+                    tt(T.bt[:, 320 + 320 * j:512 + 320 * j], T.xs[:].indirect(T.ob[:, 20 * i + 8:20 * i + 20]),
+                       T.mk[:, 192 * i:192 * i + 192], OP.mult, ["xs", "ob/%d" % i, "mk/%d" % i], ["bt/%db" % j])
+                else:
+                    take("A", i, 0, 32)
+            elif step[0] in "yz":
+                slots(i, step[0])
+            elif step[0] in "wo":
+                (slots2 if step[0] == "w" else slots3)(i, int(step[2]))
+            elif step[0] in "AV":
+                take(step[0], i, int(step[2:4]), int(step[4:6]))
+            elif step[0] == "b":
+                pack_b(i)
+            elif step[0] == "e":
+                act(T.eh[:, 320 * i:320 * i + 320], T.xs[:, 16:336], AF.Copy, ["xs"], ["eh/%d" % i], scale=0.5)
+            elif r == 0:
+                quant("quh", 128 * i, 128 * i + 128, "uh", 3 - i, ["uh"], [i])
 
         def span(lo, hi):
             n = 80 * (hi - lo + 1)
@@ -559,7 +624,7 @@ def rank_program(g, core, T, topo):
 
         def renew(lo, hi):
             n, w, end = span(lo, hi)
-            i = (lo + 3) % 4
+            i = lo
             for b in range(4):
                 mm(4 + b, w, "quo", 128 * b, back, end - w, ssub=[b], msub=range(max(lo - 1, 0), hi + 1))
             for b in range(4):
@@ -600,37 +665,45 @@ def rank_program(g, core, T, topo):
         def ones(b, same):
             if r == 0:
                 quant("quo", 128 * b, 128 * b + 128, "uo", 3 - b, ["uo"], [b])
-        for step in PLAN.split():
-            {"U": unpack, "Z": pack_z, "W": layer, "H": pack_h, "S": where, "O": ones,
-             "R": renew}[step[0]](int(step[1]), int(step[-1]))
-        if r == NR - 1:
-            ts(T.po16[:, 80:100], sa[:, 20:40], 0.25, None, OP.mult, None, ["sa/1"], ["po16/s"])
-            act(T.eq[:], T.slt[:].indirect(T.po16[:, 80:100]), AF.Copy, ["slt", "po16/s"], ["eq"])
-            for q in range(8):
-                dma("S", lambda e, q=q: e.dma_start(T.sl[q:q + 1, :], T.eq[16 * q:16 * q + 1, :]), ("out", 0),
-                    ["eq"], [])
-            quant("qv", 0, 128, "vt", 0, ["vt"])
-        for step in BACK.split():
-            renew(int(step[0]), int(step[-1]))
-        for t in range(4):
-            o, w = xn[:, t:1280:4], xa[:].indirect(T.po16[:, 20 * t:20 * t + 20])
-            if t % 2:
-                act(o, w, AF.Copy, [X, "po16/%d" % t], [XN + "/x%d" % t])
+
+        def last(step, same):
+            if r == NR - 1 and step == 0:
+                ts(T.po16[:, 80:100], sa[:, 20:40], 0.25, None, OP.mult, None, ["sa/1"], ["po16/s"])
+                act(T.eq[:], T.slt[:].indirect(T.po16[:, 80:100]), AF.Copy, ["slt", "po16/s"], ["eq"])
+                for q in range(8):
+                    dma("S", lambda e, q=q: e.dma_start(T.sl[q:q + 1, :], T.eq[16 * q:16 * q + 1, :]), ("out", 0),
+                        ["eq"], [])
+            elif r == NR - 1:
+                quant("qv", 0, 128, "vt", 0, ["vt"])
+        for step in (PLAN0 if r == 0 else PLAN).split():
+            if step[0] in "UZWHSOLR":
+                {"U": unpack, "Z": pack_z, "W": layer, "H": pack_h, "S": where, "O": ones, "L": last,
+                 "R": renew}[step[0]](int(step[1]), int(step[-1]))
             else:
-                cp(o, w, [X, "po16/%d" % t], [XN + "/x%d" % t])
+                deal(step)
 
     X = "x%d" % NR
-    quant("qx", 0, 320, X, 0, [X + "/x%d" % t for t in range(4)])
-    mm(0, 160, "qv", 0, "qx", 0)
-    mm(1, 160, "qv", 0, "qx", 160)
-    dma("S", lambda e: e.dma_start(T.oc[:], T.qx[:].bitcast(dt.uint8)), ("out", 0), ["qx"], [])
-    for k in range(4):
-        dma("SA"[k % 2], lambda e, k=k: e.dma_start(T.osc[4 * k:4 * k + 4, :], T.qxs[32 * k:32 * k + 4, :]),
-            ("out", 0), ["qxs"], [])
-    cp(T.d1[:, 0:160], T.p0[:, 0:160], ["p0"], ["d1/a"])
-    act(T.d1[:, 160:320], T.p1[:, 0:160], AF.Copy, ["p1"], ["d1/b"])
-    dma("S", lambda e: e.dma_start(T.y[:, 0:160], T.d1[:, 0:160]), ("out", 0), ["d1/a"], [])
-    dma("A", lambda e: e.dma_start(T.y[:, 160:320], T.d1[:, 160:320]), ("out", 0), ["d1/b"], [])
-    g.wait_ge(T.sem.out, 16 * (8 + 1 + 4 + 2))
+    for step in END.split():
+        if step[0] in "VA":
+            collect(NR, step)
+            continue
+        h = int(step[1])
+        lo, hi = 160 * h, 160 * h + 160
+        if step[0] == "x":
+            quant("qx", lo, hi, X, 4 * lo, state(NR, h), [h])
+            mm(h, 160, "qv", 0, "qx", lo, msub=[h])
+            dma("S", lambda e: e.dma_start(T.oc[:, 4 * lo:4 * hi], T.qx[:, lo:hi].bitcast(dt.uint8)), ("out", 0),
+                ["qx/%d" % h], [])
+        elif step[0] == "s":
+            dma(step[2], lambda e: e.dma_start(T.osc[4 * h:4 * h + 4, :], T.qxs[32 * h:32 * h + 4, :]),
+                ("out", 0), ["qxs"], [])
+        elif step[0] == "y":
+            if step[2] == "V":
+                cp(T.d1[:, lo:hi], T["p%d" % h][:, 0:160], ["p%d" % h], ["d1/%d" % h])
+            else:
+                act(T.d1[:, lo:hi], T["p%d" % h][:, 0:160], AF.Copy, ["p%d" % h], ["d1/%d" % h])
+        else:
+            dma(step[2], lambda e: e.dma_start(T.y[:, lo:hi], T.d1[:, lo:hi]), ("out", 0), ["d1/%d" % h], [])
+    g.wait_ge(T.sem.out, 16 * (8 + 2 + 4 + 2))
     g.wait_ge(T.sem.ls, lsn[0])
     finish()

from concourse.bass import DstId, RemoteDMATransfer
from concourse.mybir import dt, AluOpType as OP, AxisListType, ActivationFunctionType as AF

F32, BF, I32, U16, U8, F8 = "float32", "bfloat16", "int32", "uint16", "uint8", "float8_e4m3fn_x4"
NR = 2
UNIT = 2.0 ** 20
NEG = 2.0 ** 97
B16 = 1024.0
B4 = 2.0 ** 21
CUT = ((46, 128), (101, 224), (174, 288))
CT = (0, 320, 576, 768, 896, 1024)
S0 = 16
ORDER = "V00 A30 V20 A10 A11 x0 V21 k0 A31 K0 V01 D0 x1 T0 K1 k1 m0 m1 v0 u0 c8 c9 D1 w8 v1 w9 c7 c6 N0 w6 T1 c4 d0 c19 c18 w7 u1 a15 d1 c17 c16 a14 c2 e15 c3 c1 a13 c5 q0 e14 e13 a12 a11 s16 e12 c10 e11 q4 w1 q1 s19 w2 q3 r1 N1 w5 s17 q2 s18 r0 w4 w3 w10 b1 b0"
END = "V00 A10 V20 A30 V01 A11 x0 A31 V21 y0A x1 o0A s0S s1A s2S s3A y1V o1S"
SPLIT = (0, 320)
CLAIMS = "c0 x0 w1 e0 m0 i0 g0 n0 t0 c1 k0 l0 a0 s0 A000096 b0 e1 g1 m1 t1 c2 k1 A096304 V304320 s1 e2 b1 a1 g2 d0 k2 a2 b2 d1 d2"
PLAN0 = "f0 m0 a0 m1 f1 g0 a1 f2 b0 m2 g1 a2 f3 m3 b1 g2 a3 e0 b2 g3 b3 h0 h1 h2 h3 S0 U0 Z0 O0 W0 U1 Z1 O1 O2 U2 S1 H0 W1 Z2 H1 U3 Z3 W2 W3 S2 H2 O3 S3 S4 H3 R0 S5 S6 S7 S8 R1 R2 R3"
PLAN = "f0 m0 a0 m1 f2 f1 g0 m2 a1 b0 g1 m3 a2 f3 e0 b1 a3 g2 g3 b2 b3 U0 U1 Z1 Z0 U2 Z2 S0 W1 H1 U3 Z3 S1 S2 W2 H2 S3 W3 W0 S4 H3 S5 S6 H0 S7 R0 L0 R1 L1 R2 S8 R3"


def _scratch():
    s = {}

    def sb(dtype, **kw):
        for n in kw:
            s[n] = ("sbuf", [128, kw[n]], dtype)

    def code(n, w):
        s[n] = ("sbuf", [128, w], F8)
        s[n + "s"] = ("sbuf", [128, w], U8)
    sb(BF, x0=2560, x1=2560, x2=1280, xs=1488, nr=192, mk=768, ut=512, vt=512, eg=512, one=528, uo=528, uh=528, bt=1472,
       eh=960, z=1472, h=1472, junk=1280, sg=1280, ct=4096, rs=320, rc=320, rb=608)
    for n, w in (("qu", 128), ("qur", 128), ("qv", 128), ("wq", 512), ("qx", 320), ("qeg", 128), ("quh", 512),
                 ("quo", 512), ("qz", 512), ("qc", 1024)):
        code(n, w)
    for r in range(NR):
        for n in ("came", "back"):
            code("%s%d" % (n, r), 368)
        for n in ("qb", "qh"):
            code("%s%d" % (n, r), 384)
    sb(F32, i16=320, i4=320, ij=320, mm=320, d0=320, k16=320, k4=320, d1=320, st=320, eq=320, e8=8,
       rcb=20, pc=8, v4=320, wrow=320, cw=664, on=320, rx=320, rk=20, acc=8, rsum=32, ox=320, cst=6, fm=32,
       g1=32, g2=32, g3=16, sm=64, ge=8, ta=8, tb=8, cz=20, ncs=20, old=20, kc=4, ya=80, za=80, wa=80, sa=80,
       sc=80, se=80, sf=80, slt=640)
    sb(I32, pi=8, xi=8, oi=160)
    sb(U16, ul=8, rk16=20, e16=8, ol=80, ob=80, po16=100)
    for b in range(8):
        s["p%d" % b] = ("psum", [128, 512], F32)
    return s


SCRATCH = _scratch()
SEMAPHORES = (["sV", "sA", "sP", "sG", "gd", "ls", "dx", "dy", "du", "dw", "dv", "out"]
              + ["%s%d_%d" % (p, r, i) for p in ("came", "back") for r in range(NR) for i in (1, 2, 3)])


def tracker(g, T):
    eng = {"V": g.vector, "A": g.scalar, "P": g.tensor, "G": g, "S": g.sync}
    sem = {"V": "sV", "A": "sA", "P": "sP", "G": "sG"}
    count = {q: 0 for q in sem}
    known = {q: {} for q in eng}
    known["far"] = {}
    clock = {}
    log = {}

    def split(k):
        a = k.split("/")
        return a[0], (a[1] if len(a) > 1 else None)

    def need(q, reads, writes, acc):
        out = {}
        for keys, w in ((reads, False), (writes, True)):
            for k in keys:
                n, s = split(k)
                psum = n[0] == "p" and n[1:].isdigit()
                for (s2, q2, tok, w2) in log.get(n, []):
                    if not psum and s is not None and s2 is not None and s != s2:
                        continue
                    dma = tok[0] not in ("sV", "sA", "sP", "sG")
                    if q2 == q and not dma:
                        if (not w2 and not w) or (acc and w):
                            continue
                    elif not w and not w2 and not psum:
                        continue
                    out[tok[0]] = max(out.get(tok[0], 0), tok[1])
        return out

    def wait(q, toks):
        for s in sorted(toks):
            if known[q].get(s, 0) < toks[s]:
                eng[q].wait_ge(T.sem[s], toks[s])
                for (s2, v2) in clock.get((s, toks[s]), {}).items():
                    known[q][s2] = max(known[q].get(s2, 0), v2)
                known[q][s] = max(known[q].get(s, 0), toks[s])

    def note(q, tok, reads, writes):
        c = dict(known[q])
        c[tok[0]] = max(c.get(tok[0], 0), tok[1])
        if tok in clock:
            for s2 in clock[tok]:
                c[s2] = max(c.get(s2, 0), clock[tok][s2])
        clock[tok] = c
        for k in writes:
            n, s = split(k)
            log[n] = [e for e in log.get(n, []) if not (s is None or e[0] == s)] + [(s, q, tok, True)]
        for k in reads:
            n, s = split(k)
            log[n] = [e for e in log.get(n, []) if not (not e[3] and e[1] == q and e[0] == s)] + [(s, q, tok, False)]

    def tr(q, fn, reads, writes, acc=False):
        wait(q, need(q, reads, writes, acc))
        count[q] += 1
        fn(eng[q]).then_inc(T.sem[sem[q]], 1)
        note(q, (sem[q], count[q]), reads, writes)

    def dma(q, fn, tok, reads, writes):
        wait(q, need(q, reads, writes, False))
        fn(eng[q]).then_inc(T.sem[tok[0]], 16)
        note(q, tok, reads, writes)

    def remote(fn, tok, reads):
        wait("G", need("G", reads, [], False))
        fn(g)
        note("G", tok, reads, [])

    def arrive(tok, writes):
        note("far", tok, [], writes)

    def finish():
        wait("G", {sem[q]: count[q] for q in sem if count[q]})
    return tr, dma, remote, arrive, finish


def rank_program(g, core, T, topo):
    rank = T.rank_of(core)
    if rank is None:
        return
    N = len(T.cores)
    tr, dma, remote, arrive, finish = tracker(g, T)

    def V(fn, r, w):
        tr("V", fn, r, w)

    def ts(out, in0, s1, s2, op0, op1, r, w):
        if op1 is None:
            V(lambda e: e.tensor_scalar(out, in0, s1, None, op0), r, w)
        else:
            V(lambda e: e.tensor_scalar(out, in0, s1, s2, op0, op1), r, w)

    def tt(out, a, b, op, r, w):
        V(lambda e: e.tensor_tensor(out, a, b, op), r, w)

    def cp(out, in_, r, w):
        V(lambda e: e.tensor_copy(out, in_), r, w)

    def scan(out, a, b, init, op0, op1, r, w):
        V(lambda e: e.tensor_tensor_scan(out, a, b, init, op0, op1), r, w)

    def most(out, in_, r, w):
        V(lambda e: e.tensor_reduce(out, in_, AxisListType.X, OP.max), r, w)

    def fill(ap, c, w):
        V(lambda e: e.memset(ap, c), [], w)

    def act(out, in_, func, r, w, **kw):
        tr("A", lambda e: e.activation(out, in_, func, **kw), r, w)

    def iota(out, pat, base, cm, w, flag=True):
        if flag:
            tr("G", lambda e: e.iota(out, pat, base, cm, allow_small_or_imprecise_dtypes=True), [], w)
        else:
            tr("G", lambda e: e.iota(out, pat, base, cm), [], w)

    def select(out, in_, pat, op, base, cm, r, w, c=0.0):
        tr("G", lambda e: e.affine_select(out, in_, pat, op, c, base, cm), r, w)

    def keys(n, subs):
        if subs is None:
            return [n, n + "s"]
        return [n + x + "/" + str(s) for s in subs for x in ("", "s")]

    def quant(name, a, b, src, lo, r, sub=None):
        V(lambda e: e.quantize_mx(T[name][:, a:b], T[name + "s"][:, a:b], T[src][:, lo:lo + 4 * (b - a)]),
          r, keys(name, sub))

    def mm(bank, n, sta, sa, mov, ma, start=True, stop=True, ssub=None, msub=None):
        p = "p%d" % bank
        tr("P", lambda e: e.matmul_mx(T[p][:, 0:n], T[sta][:, sa:sa + 128], T[sta + "s"][:, sa:sa + 128],
                                      T[mov][:, ma:ma + n], T[mov + "s"][:, ma:ma + n], start, stop),
           keys(sta, ssub) + keys(mov, msub), [p], acc=not start)

    dma("S", lambda e: e.dma_start(T.x0[:, 0:640], T.x[:, 0:640]), ("dx", 16), [], ["x0/x0"])
    dma("A", lambda e: e.dma_start(T.ut[:], T.u[:]), ("du", 16), [], ["ut"])
    dma("S", lambda e: e.dma_start(T.x0[:, 640:1280], T.x[:, 640:1280]), ("dy", 16), [], ["x0/x1"])
    dma("S", lambda e: e.dma_start(T.wq[:].bitcast(dt.uint8), T.wc[:]), ("dw", 32), ["x0/x1", "ut"], ["wq"])
    dma("S", lambda e: e.dma_start(T.wqs[:], T.ws[:]), ("dw", 32), [], ["wqs"])

    iota(T.pi[:, 0:1], [[0, 1]], 0, 1, ["pi/0"], False)
    iota(T.xi[:, 0:8], [[16, 8]], 4, 0, ["xi"], False)
    iota(T.i16[:], [[0, 20], [1, 16]], 0, 0, ["i16"])
    iota(T.e8[:], [[16, 8]], 0, -1, ["e8"])
    iota(T.ij[:], [[1, 320]], 0, 0, ["ij"])
    iota(T.rs[:, 0:16 * S0], [[-16, S0], [32767, 16]], 152, 0, ["rs/0"])
    iota(T.rs[:, 16 * S0:320], [[-16, 20 - S0], [32767, 16]], 304 - 16 * S0, 0, ["rs/1"])

    fill(T.one[:], 1.0, ["one"])
    cp(T.ul[:], T.xi[:], ["xi"], ["ul"])
    ts(T.pi[:, 1:2], T.pi[:, 0:1], 15, None, OP.bitwise_and, None, ["pi/0"], ["pi/1"])
    ts(T.pi[:, 2:3], T.pi[:, 0:1], 3, None, OP.bitwise_and, None, ["pi/0"], ["pi/2"])
    fill(T.rsum[:, 0:1], 0.0, ["rsum/0"])
    ts(T.pi[:, 3:4], T.pi[:, 1:2], 2, None, OP.logical_shift_right, None, ["pi/1"], ["pi/3"])
    for b in range(5):
        fill(T.ct[:, 4 * (CT[b + 1] - (48 if b < 4 else 112)):4 * CT[b + 1]], 0.0, ["ct/z%d" % b])
        if b == 0:
            cp(T.pc[:, 0:3], T.pi[:, 1:4], ["pi"], ["pc/0"])
    ts(T.mm[:], T.i16[:], T.pc[:, 0:1], -2.0 * NEG, OP.not_equal, OP.mult, ["i16", "pc/0"], ["mm"])
    ts(T.e8[:], T.e8[:], T.pc[:, 0:1], 0.0, OP.add, OP.is_equal, ["e8", "pc/0"], ["e8"])
    act(T.d0[:], T.i16[:], AF.Copy, ["i16"], ["d0"], scale=2.0 * NEG, bias=-NEG)
    quant("qu", 0, 128, "ut", 0, ["ut"])
    cp(T.qur[:].bitcast(dt.uint32), T.qu[:].bitcast(dt.uint32).indirect(T.ul[:, 0:8]), ["qu", "ul"], ["qur"])
    for j in range(4):
        act(T.eg[:, 64 * j:64 * j + 64], T.one[:, 0:64], AF.Copy, ["one", "e8"], ["eg/%d" % j], scale=T.e8[:, j:j + 1])
    act(T.qurs[:], T.qus[:].indirect(T.ul[:, 0:8]), AF.Copy, ["qus", "ul"], ["qurs"])
    for j in range(4, 8):
        act(T.eg[:, 64 * j:64 * j + 64], T.one[:, 0:64], AF.Copy, ["one", "e8"], ["eg/%d" % j], scale=T.e8[:, j:j + 1])

    dma("G", lambda e: e.dma_start(T.vt[:], T.v[:]), ("dv", 16), [], ["vt"])

    def product_constants():
        ts(T.k16[:], T.i16[:], T.pc[:, 0:1], 34 * B16, OP.is_gt, OP.mult, ["i16", "pc/0"], ["k16"])
        ts(T.pc[:, 3:4], T.pc[:, 0:1], 1.0 - B16, 15 * B16 - 167.0, OP.mult, OP.add, ["pc/0"], ["pc/3"])
        act(T.k16[:], T.k16[:], AF.Copy, ["k16"], ["k16"], bias=-33 * B16)

    def count_constants():
        act(T.on[:], T.i16[:], AF.Copy, ["i16"], ["on"], scale=0.0, bias=-UNIT)
        act(T.fm[:, 0:16], T.i16[:, 0:16], AF.Copy, ["i16"], ["fm/a"], scale=0.0, bias=1.0)
        act(T.fm[:, 16:32], T.i16[:, 0:16], AF.Copy, ["i16"], ["fm/b"], scale=-2.0 ** -16, bias=1.0)
        act(T.pc[:, 4:5], T.pc[:, 0:1], AF.Copy, ["pc/0"], ["pc/4"], bias=1296.0)
        act(T.pc[:, 5:6], T.pc[:, 0:1], AF.Copy, ["pc/0"], ["pc/5"], scale=-2.0 ** -15, bias=2.0)

    def late_constants():
        iota(T.i4[:], [[0, 80], [1, 4]], 0, 0, ["i4"])
        select(T.uo[:], T.one[:], [[1, 528]], OP.is_equal, -3, -4, ["one"], ["uo"])
        iota(T.cw[:, 8:328], [[-4, 320]], 1276, 0, ["cw/i"])
        iota(T.cw[:, 0:8], [[0, 8]], 0, 0, ["cw/y"])
        iota(T.cw[:, 328:344], [[0, 16]], 0, 0, ["cw/z"])
        iota(T.xs[:, 0:16], [[0, 16]], 0, 0, ["xs/z"])
        iota(T.xs[:, 1296:1488], [[0, 192]], 0, 0, ["xs/y"])
        iota(T.nr[:], [[-4, 48], [0, 4]], -130, 0, ["nr"])
        for s in range(3):
            iota(T.cst[:, 2 * s:2 * s + 2], [[-672, 2]], CUT[s][0] + CUT[s][1] + 686, 0, ["cst/%d" % s])
        for k in range(4):
            iota(T.kc[:, k:k + 1], [[0, 1]], 1279 + 320 * far.index(k), 0, ["kc/%d" % k])
        iota(T.bt[:, 320:512], [[0, 192]], 0, 0, ["bt/0a", "bt/0b"])
        for n in ("bt", "z", "h"):
            iota(T[n][:, 0:192], [[0, 192]], 0, 0, [n + "/pad"])

    gdn, jn, lsn = [0], [0], [0]

    def hops(k):
        n = 0
        for i in range(N):
            a, b = topo.chip(T.cores[i]), topo.chip(T.cores[(i + k) % N])
            n += 0 if a == b else 1 if topo.mates(a, b) or topo.same_plane(a, b) else 2
        return n
    far = [0] + sorted((1, 2, 3), key=lambda k: -hops(k))

    def send(src, a, i, dst, step):
        to = T.cores[(rank + step * far[i]) % N]
        ad = topo.addr(to)
        b = 48 + 80 * i
        name = "%s_%d" % (dst, i)
        apart = lsn[0] == 0
        for planes in (False, True):
            en = topo.engines(core, to)
            if apart:
                en = en[len(en) // 2:] if planes else en[:len(en) // 2]
            mask = sum(1 << x for x in en)
            if planes:
                s_ap, d_ap = T[src + "s"][:, a:a + 80], T[dst + "s"][:, b:b + 80]
            else:
                s_ap, d_ap = T[src][:, a:a + 80].bitcast(dt.uint8), T[dst][:, b:b + 80].bitcast(dt.uint8)
            lsn[0] += len(en)
            remote(lambda e: e.remote_dma(d_ap, s_ap, T.sem[name], T.sem.ls, ad[1], ad[0], mask), ("ls", lsn[0]),
                   ["%s%s/%d" % (src, "s" if planes else "", i)])
        arrive((name, 2 * len(en)), keys(dst, [i]))

    def state(r, h):
        return ["x%d/x%d" % (r, h)] if r == 0 else ["x%d/x%d%d" % (r, t, h) for t in range(4)]

    def collect(r, step):
        t, h = int(step[1]), int(step[2])
        old = "x%d" % (r - 1)
        o = T["x%d" % r][:, 640 * h + t:640 * h + 640:4]
        w = T[old][:].indirect(T.po16[:, 20 * t + 10 * h:20 * t + 10 * h + 10])
        if step[0] == "A":
            act(o, w, AF.Copy, [old, "po16/%d" % t], ["x%d/x%d%d" % (r, t, h)])
        else:
            cp(o, w, [old, "po16/%d" % t], ["x%d/x%d%d" % (r, t, h)])

    for r in range(NR):
        X = "x%d" % r
        xa = T[X]
        xk = state(r, 0) + state(r, 1)
        came, back, qb, qh = "came%d" % r, "back%d" % r, "qb%d" % r, "qh%d" % r

        def half(step):
            h = int(step[1])
            lo, hi, pa, pb = 160 * h, 160 * h + 160, "p%d" % (4 + 2 * h), "p%d" % (5 + 2 * h)
            if step[0] == "x":
                quant("qx", lo, hi, X, 4 * lo, state(r, h), [h])
                mm(4 + 2 * h, 160, "qur", 0, "qx", lo, msub=[h])
            elif step[0] == "k":
                mm(5 + 2 * h, 160, "qu", 0, "qx", lo, msub=[h])
            elif step[0] == "m":
                mm(h, 320, "qur", 0, "qx", 0)
            elif step[0] == "D":
                tt(T.d1[:, lo:hi], T[pa][:, 0:160], T.mm[:, lo:hi], OP.add, [pa, "mm"], ["d1/%d" % h])
            elif step[0] == "T":
                scan(T.st[:, lo:hi], T.d0[:, lo:hi], T.d1[:, lo:hi], -NEG, OP.min, OP.max, ["d0", "d1/%d" % h],
                     ["st/%d" % h])
            elif step[0] == "d":
                tt(T.ct[:, 4 * lo:4 * hi:4], T.st[:, lo:hi], T[pa][:, 0:160], OP.is_ge, [pa, "st/%d" % h, "ct/z0"],
                   ["ct/20" + "ab"[h]])
            elif step[0] == "v":
                act(T.v4[:, lo:hi], T[pb][:, 0:160], AF.Sign, [pb], ["v4/%d" % h])
            elif step[0] == "u":
                act(T.v4[:, lo:hi], T.v4[:, lo:hi], AF.Relu, ["v4/%d" % h], ["v4/%d" % h, "acc/t%d" % h], scale=UNIT,
                    accum_out=T.acc[:, 6 + h:7 + h])
                dma("G", lambda e: e.dma_start(T.v4[:, lo:hi], T.ij[:, lo:hi], accum_op=OP.add), ("gd", 32 * r + 32),
                    ["ij"], ["v4/%d" % h])
                if h:
                    if r == 0:
                        late_constants()
                    if r == NR - 1:
                        iota(T.slt[:, 0:320], [[0, 320]], -1, 0, ["slt/n"])
                        for j in range(4):
                            iota(T.slt[:, 320 + 80 * j:400 + 80 * j], [[1, 80]], 80 * far[j], 0, ["slt/%d" % j])
            elif h == 0:
                act(T.acc[:, 4:5], T.acc[:, 6:7], AF.Copy, ["acc/t0"], ["acc/t"], bias=319.6 * UNIT)
            else:
                act(T.acc[:, 5:6], T.acc[:, 7:8], AF.Identity, ["acc/t", "acc/t1"], ["acc/T"], bias=T.acc[:, 4:5])

        def place(c):
            b, t = (20 - c) // 4, (20 - c) % 4
            return T.ct[:, 4 * CT[b] + t:4 * (CT[b] + 16 * c):4], "ct/%d" % c

        def own(c):
            return T.st[:, 16 * c + 15:16 * c + 16]

        def compare(c):
            o, key = place(c)
            p = "p4" if c <= 10 else "p0"
            ts(o, T[p][:, 0:16 * c], own(c), None, OP.is_lt, None,
               [p, "st/%d" % (c // 10), "ct/z%d" % ((20 - c) // 4)], [key])

        def rows(c):
            o, key = place(c)
            jn[0] = (jn[0] + 1) % 4
            act(T.junk[:, 320 * jn[0]:320 * jn[0] + 16 * c], o, AF.Copy, [key], ["junk/%d" % jn[0], "rsum/%d" % c],
                accum_out=T.rsum[:, c:c + 1])

        def alone(what, c):
            i = c % 4
            if what == "a":
                act(T.sg[:, 320 * i:320 * i + 16 * c], T.p1[:, 0:16 * c], AF.Sign, ["p1", "st/%d" % (c // 10)],
                    ["sg/%d" % i], scale=-1.0, bias=own(c))
            else:
                o, key = place(c)
                act(o, T.sg[:, 320 * i:320 * i + 16 * c], AF.Relu, ["sg/%d" % i, "ct/z%d" % ((20 - c) // 4)],
                    [key, "rsum/%d" % c], accum_out=T.rsum[:, c:c + 1])

        def sums(c):
            b, t = (20 - c) // 4, (20 - c) % 4
            a = 4 * CT[b] + t
            scan(T.rb[:, 4 * (152 - 8 * c) + c - S0:608:4], T.ct[:, a:a + 32 * c:4],
                 T.ct[:, a + 32 * c:4 * (CT[b] + 16 * c):4], -152.0, OP.add, OP.add, ["ct/%d" % c], ["rb/%d" % c])

        def count(b):
            w = CT[b + 1] - CT[b]
            quant("qc", CT[b], CT[b + 1], "ct", 4 * CT[b],
                  ["ct/z%d" % b, "ct/20a", "ct/20b"][:3 if b == 0 else 1]
                  + ["ct/%d" % (20 - 4 * b - t) for t in range(4)], [b])
            turn = [int(s[1]) for s in ORDER.split() if s[0] == "q"]
            mm(3, w, "qeg", 0, "qc", CT[b], b == turn[0], b == turn[-1], msub=[b])
        for step in ORDER.split():
            if step[0] in "VA":
                if r:
                    collect(r, step)
                continue
            if step[0] in "xkmDTdvuN":
                half(step)
                continue
            c = int(step[1:])
            if step[0] == "c":
                compare(c)
            elif step[0] == "w":
                rows(c)
            elif step[0] in "ae":
                alone(step[0], c)
            elif step[0] == "s":
                sums(c)
            elif step[0] == "K":
                if r == 0:
                    (product_constants, lambda: quant("qeg", 0, 128, "eg", 0, ["eg"]))[c]()
            elif step[0] == "q":
                count(c)
            elif step[0] == "r":
                lo, hi = ((0, 16 * S0), (16 * S0, 320))[c]
                scan(T.rc[:, lo:hi], T.rs[:, lo:hi], T.ct[:, 4 * lo:4 * hi:4], 1.0e4, OP.min, OP.add,
                     ["rs", "ct/20a", "ct/20b"], ["rc/%d" % c])
            elif c == 0:
                tt(T.rcb[:, 0:S0], T.rc[:, 15:16 * S0:16], T.rsum[:, 0:S0], OP.add, ["rc/0", "rsum"], ["rcb/0"])
            else:
                tt(T.rcb[:, S0:20], T.rc[:, 16 * S0 + 15:320:16], T.rb[:, 604:624 - S0], OP.add, ["rc/1", "rb"],
                   ["rcb/1"])
        if r == 0:
            count_constants()
            act(T.k4[:], T.i4[:], AF.Sign, ["i4", "pc/0"], ["k4"], scale=-1.0, bias=T.pc[:, 2:3])
            act(T.k4[:], T.k4[:], AF.Relu, ["k4"], ["k4"], scale=-9 * B4)
            act(T.k4[:], T.k4[:], AF.Copy, ["k4"], ["k4"], bias=-8 * B4)
            act(T.cz[:], T.ij[:, 0:320:16], AF.Identity, ["ij", "pc/4"], ["cz"], bias=T.pc[:, 4:5])
            act(T.ncs[:], T.cz[:], AF.Copy, ["cz"], ["ncs"], scale=-1.0, bias=1295.5)
            act(T.old[:], T.cz[:], AF.Copy, ["cz"], ["old"], scale=4.0, bias=-4.0 * 1296)
            act(T.uh[:], T.uo[:], AF.Copy, ["uo"], ["uh"], scale=0.5)
        scan(T.rx[:], T.k16[:], T.p3[:, 0:320], 0.0, OP.add, OP.max, ["k16", "p3"], ["rx"])
        tt(T.rk[:], T.rx[:, 15:320:16], T.rcb[:], OP.subtract, ["rx", "rcb"], ["rk"])
        ts(T.rk16[:], T.rk[:], T.pc[:, 3:4], None, OP.subtract, None, ["rk", "pc/3"], ["rk16"])
        cp(T.wrow[:].indirect(T.rk16[:, 0:20]), T.v4[:], ["rk16", "v4"], ["wrow"])
        scan(T.cw[:, 344:472], T.on[:, 0:128], T.wrow[:, 0:128], T.acc[:, 5:6], OP.add, OP.subtract,
             ["wrow", "on", "acc/T"], ["cw/s"])
        sm = T.sm
        th = [T.acc[:, 5:6], sm[:, 0:1], sm[:, 1:2]]
        ke = [sm[:, 2:3], sm[:, 3:4], sm[:, 4:5]]
        left = [0.5, sm[:, 5:6], sm[:, 6:7]]

        def cut(s):
            lo, hi = CUT[s]
            act(T.junk[:, 320 * s:320 * s + hi - lo], T.cw[:, lo + 343:hi + 343], AF.Sign,
                ["cw/s", "acc/T"] if s == 0 else ["cw/s", "cw/t", "sm/th%d" % s], ["junk/%d" % s, "acc/%d" % s],
                bias=th[s], scale=-(4.0 - s) / (3.0 - s), accum_out=T.acc[:, s:s + 1])

        def ends(s):
            a = 2 * s + (s == 2)
            ts(T.e16[:, 2 * s:2 * s + 2 * s + 2 - a], T.cst[:, a:2 * s + 2], T.acc[:, s:s + 1], left[s], OP.subtract,
               OP.mult, ["acc/%d" % s, "cst"] + ["sm/left%d" % s] * (s > 0), ["e16/%d" % s])

        def mine(s):
            lo, hi = CUT[s]
            ts(sm[:, 24 + s:25 + s], T.acc[:, s:s + 1], 640.0 - lo - hi, T.pc[:, 5:6], OP.add, OP.mult,
               ["acc/%d" % s, "pc/5"], ["sm/mine%d" % s])

        def stays(s):
            ts(left[s + 1], sm[:, 24 + s:25 + s], ke[s], left[s], OP.not_equal, OP.mult,
               ["sm/mine%d" % s, "sm/ke%d" % s] + ["sm/left%d" % s] * (s > 0), ["sm/left%d" % (s + 1)])

        def sort(lo, hi, eng="A"):
            o, i = T.xs[:, 16 + 4 * lo:16 + 4 * hi], xa[:, 0:1280].indirect(T.ol[:, lo // 4:hi // 4])
            k = xk + ["ol/%d" % h for h in range(len(SPLIT) - 1) if lo < SPLIT[h + 1] and hi > SPLIT[h]]
            if eng == "A":
                act(o, i, AF.Copy, k, ["xs/%d" % lo])
            else:
                cp(o, i, k, ["xs/%d" % lo])
        g1, g2, g3 = T.g1, T.g2, T.g3

        def won(o, gs, s, by, key, more=()):
            ts(o, gs, ke[s], by, OP.is_equal, OP.mult, ["g%d" % (s + 1), "sm/ke%d" % s] + list(more), [key])

        def listed(what, h):
            lo, hi = SPLIT[h], SPLIT[h + 1]
            a, b = lo // 4, hi // 4
            if what == "x":
                scan(T.ox[:, lo:hi], T.k4[:, lo:hi], T.wrow[:, lo:hi], 0.0, OP.add, OP.max, ["k4", "wrow"],
                     ["ox/%d" % h])
            elif what == "i":
                cp(T.oi[:, a:b], T.ox[:, lo + 3:hi:4], ["ox/%d" % h], ["oi/a%d" % h])
            elif what == "n":
                ts(T.oi[:, 80 + a:80 + b], T.oi[:, a:b], 511, None, OP.bitwise_and, None, ["oi/a%d" % h],
                   ["oi/b%d" % h])
            else:
                ts(T.ol[:, a:b], T.oi[:, 80 + a:80 + b], 4.0, T.pc[:, 1:2], OP.mult, OP.add, ["oi/b%d" % h, "pc/0"],
                   ["ol/%d" % h])
        steps = {
            "g0": lambda: tt(g1[:], T.cw[:, 0:472].indirect(T.e16[:, 0:2]), T.fm[:], OP.mult,
                             ["cw/s", "cw/i", "cw/y", "cw/z", "e16/0", "fm"], ["g1"]),
            "g1": lambda: tt(g2[:], T.cw[:].indirect(T.e16[:, 2:4]), T.fm[:], OP.mult, ["cw", "e16/1", "fm"], ["g2"]),
            "g2": lambda: tt(g3[:], T.cw[:].indirect(T.e16[:, 4:5]), T.fm[:, 16:32], OP.mult, ["cw", "e16/2", "fm"],
                             ["g3"]),
            "w1": lambda: scan(T.cw[:, 472:664], T.on[:, 128:320], T.wrow[:, 128:320], T.cw[:, 471:472], OP.add,
                               OP.subtract, ["wrow", "on", "cw/s"], ["cw/t"]),
            "t0": lambda: most(th[1], g1[:, 0:4], ["g1"], ["sm/th1"]),
            "t1": lambda: most(th[2], g2[:, 0:4], ["g2"], ["sm/th2"]),
            "k0": lambda: most(ke[0], g1[:, 16:20], ["g1"], ["sm/ke0"]),
            "k1": lambda: most(ke[1], g2[:, 16:20], ["g2"], ["sm/ke1"]),
            "k2": lambda: most(ke[2], g3[:, 0:4], ["g3"], ["sm/ke2"]),
            "a0": lambda: won(sm[:, 8:12], g1[:, 16:20], 0, 1280.0, "sm/a1"),
            "b0": lambda: won(sm[:, 12:16], g1[:, 16:20], 0, ke[0], "sm/a2"),
            "a1": lambda: won(sm[:, 16:20], g2[:, 16:20], 1, ke[0], "sm/b1", ["sm/ke0"]),
            "b1": lambda: won(sm[:, 20:24], g2[:, 16:20], 1, ke[1], "sm/b2"),
            "a2": lambda: won(T.ta[:, 0:4], g3[:, 0:4], 2, ke[1], "ta/a", ["sm/ke1"]),
            "b2": lambda: won(T.ta[:, 4:8], g3[:, 0:4], 2, ke[2], "ta/b"),
            "d0": lambda: tt(T.tb[:], sm[:, 8:16], sm[:, 16:24], OP.add, ["sm/a1", "sm/a2", "sm/b1", "sm/b2"], ["tb"]),
            "d1": lambda: ts(T.tb[:, 0:4], T.tb[:, 0:4], ke[2], None, OP.max, None, ["tb", "sm/ke2"], ["tb"]),
            "d2": lambda: tt(T.ge[:], T.ta[:], T.tb[:], OP.max, ["ta", "tb"], ["ge"])}
        for step in CLAIMS.split():
            if step in steps:
                steps[step]()
            elif step[0] in "AV":
                sort(int(step[1:4]), int(step[4:7]), step[0])
            elif step[0] in "xinl":
                listed(step[0], int(step[1]))
            else:
                {"c": cut, "e": ends, "m": mine, "s": stays}[step[0]](int(step[1]))

        def slots(i, what):
            k = far[(i + 1) % 4]
            if "y" in what:
                ts(T.ya[:, 20 * i:20 * i + 20], T.ncs[:], T.ge[:, k:k + 1], T.ge[:, 4 + k:5 + k], OP.add, OP.is_gt,
                   ["ncs", "ge"], ["ya/%d" % i])
            if "z" in what:
                ts(T.za[:, 20 * i:20 * i + 20], T.cz[:], T.ge[:, k:k + 1], None, OP.subtract, None, ["cz", "ge"],
                   ["za/%d" % i])

        def slots2(a, b):
            tt(T.wa[:, 20 * a:20 * b], T.ya[:, 20 * a:20 * b], T.za[:, 20 * a:20 * b], OP.mult,
               ["%s/%d" % (n, i) for n in ("ya", "za") for i in range(a, b)], ["wa/%d" % a])

        def slots3(a, b):
            cp(T.ob[:, 20 * a:20 * b], T.wa[:, 20 * a:20 * b], ["wa/%d" % a], ["ob/%d" % i for i in range(a, b)])

        def take(eng, i, lo, hi):
            j = (i + 1) % 4
            o = T.bt[:, 192 + 320 * j + 4 * lo:192 + 320 * j + 4 * hi]
            w = T.xs[:].indirect(T.ob[:, 20 * i + lo // 4:20 * i + hi // 4])
            k = ["bt/%d%s" % (j, "a" if lo == 0 else "b")] + (["bt/%db" % j] if (lo, hi) == (0, 80) else [])
            if eng == "V":
                cp(o, w, ["xs", "ob/%d" % i], k)
            else:
                act(o, w, AF.Copy, ["xs", "ob/%d" % i], k)

        def two(n, i):
            return ["%s/%d%s" % (n, j, x) if j >= 0 else n + "/pad" for j in (i - 1, i) for x in "ab"]

        def pack_b(i):
            if i < 3:
                quant(qb, 128 * i, 128 * i + 128, "bt", 320 * i + 320, two("bt", i + 1), [i + 1])
                send(qb, 128 * i + 48, i + 1, came, 1)
            else:
                quant(came, 0, 128, "bt", 0, two("bt", 0), [0])

        def deal(step):
            i = int(step[1])
            if step[0] == "p":
                if r == 0:
                    quant(("came0", "back0", "came1", "back1")[i], 0, 128, "z", 0, four("z", -1, 0), [0])
            elif step[0] in "fmga":
                j, k = (i + 1) % 4, far[(i + 1) % 4]
                if step[0] == "f":
                    ts(T.ob[:, 20 * i:20 * i + 20], T.cz[:], T.ge[:, k:k + 1], None, OP.subtract, None, ["cz", "ge"],
                       ["ob/%d" % i])
                elif step[0] == "m":
                    ts(T.mk[:, 192 * i:192 * i + 192], T.nr[:], T.ge[:, k:k + 1], T.ge[:, 4 + k:5 + k], OP.add,
                       OP.is_gt, ["nr", "ge"], ["mk/%d" % i])
                elif step[0] == "g":
                    tt(T.bt[:, 320 + 320 * j:512 + 320 * j], T.xs[:].indirect(T.ob[:, 20 * i + 8:20 * i + 20]),
                       T.mk[:, 192 * i:192 * i + 192], OP.mult, ["xs", "ob/%d" % i, "mk/%d" % i], ["bt/%db" % j])
                else:
                    take("A", i, 0, 32)
            elif step[0] in "yz":
                slots(i, step[0])
            elif step[0] in "wo":
                (slots2 if step[0] == "w" else slots3)(i, int(step[2]))
            elif step[0] in "AV":
                take(step[0], i, int(step[2:4]), int(step[4:6]))
            elif step[0] == "b":
                pack_b(i)
            elif step[0] == "e":
                act(T.eh[:, 320 * i:320 * i + 320], T.xs[:, 16:336], AF.Copy, ["xs"], ["eh/%d" % i], scale=0.5)
            elif r == 0:
                quant("quh", 128 * i, 128 * i + 128, "uh", 3 - i, ["uh"], [i])

        def span(lo, hi):
            n = 80 * (hi - lo + 1)
            return n, max(n, 128), 128 + 80 * hi

        def four(n, lo, hi, x="abcd"):
            return ["%s/%d%s" % (n, j, c) if j >= 0 else n + "/pad" for j in range(lo, hi + 1) for c in x]

        def unpack(lo, hi):
            n, w, end = span(lo, hi)
            for b in range(4):
                mm(4 + b, w, "quh", 128 * b, came, end - w, ssub=[b], msub=range(max(lo - 1, 0), hi + 1))
            for b in range(4):
                tt(T.z[:, 4 * (end - n) + b:4 * end:4], T["p%d" % (4 + b)][:, w - n:w], T.eh[:, b:4 * n:4], OP.add,
                   ["p%d" % (4 + b)] + ["eh/%d" % i for i in range(n // 80)], four("z", lo, hi, "abcd"[b]))
        at = {"z": 0, "h": 0}

        def pack_z(lo, hi):
            n, w, end = span(lo, hi)
            at[lo] = at["z"]
            at["z"] += w
            quant("qz", at[lo], at[lo] + w, "z", 4 * (end - w), four("z", lo - 1, hi), range(lo, hi + 1))

        def layer(lo, hi):
            n, w, end = span(lo, hi)
            for b in range(4):
                mm(b, w, "wq", 128 * b, "qz", at[lo], msub=[lo])
            for b in range(4):
                o, i = T.h[:, 4 * (end - n) + b:4 * end:4], T["p%d" % b][:, w - n:w]
                if n > 80 and b % 2:
                    ts(o, i, 0.03125, None, OP.mult, None, ["p%d" % b], four("h", lo, hi, "abcd"[b]))
                else:
                    act(o, i, AF.Copy, ["p%d" % b], four("h", lo, hi, "abcd"[b]), scale=0.03125)

        def pack_h(lo, hi):
            n, w, end = span(lo, hi)
            if lo == 0:
                quant(back, 0, 128, "h", 0, four("h", -1, 0), [0])
            else:
                quant(qh, at["h"], at["h"] + w, "h", 4 * (end - w), four("h", lo - 1, hi), range(lo, hi + 1))
                for i in range(lo, hi + 1):
                    send(qh, at["h"] + w - 80 * (hi + 1 - i), i, back, -1)
                at["h"] += w

        def renew(lo, hi):
            n, w, end = span(lo, hi)
            i = lo
            for b in range(4):
                mm(4 + b, w, "quo", 128 * b, back, end - w, ssub=[b], msub=range(max(lo - 1, 0), hi + 1))
            for b in range(4):
                tt(xa[:, 1280 + 320 * lo + b:1600 + 320 * hi:4], T["p%d" % (4 + b)][:, w - n:w],
                   T.bt[:, 192 + 320 * i + b:192 + 320 * i + 4 * n:4], OP.add,
                   ["p%d" % (4 + b)] + four("bt", i, i + hi - lo, "ab"), ["%s/n%d%d" % (X, lo, b)])
        ge, sa, sc, se, sf = T.ge, T.sa, T.sc, T.se, T.sf

        def where(step, same):
            if step == 0:
                ts(se[:, 60:80], T.rk16[:], -4.0, 1279.0, OP.mult, OP.add, ["rk16"], ["se/r"])
                ts(sm[:, 32:36], ge[:, 0:4], -320.0, None, OP.add, None, ["ge"], ["sm/l1"])
                tt(sm[:, 40:44], ge[:, 0:4], T.kc[:], OP.add, ["ge", "kc"], ["sm/h"])
                tt(sm[:, 36:40], sm[:, 32:36], ge[:, 4:8], OP.max, ["ge", "sm/l1"], ["sm/lo"])
            elif step == 1:
                for k in range(4):
                    ts(sa[:, 20 * k:20 * k + 20], se[:, 60:80], ge[:, k:k + 1], sm[:, 40 + k:41 + k], OP.is_lt,
                       OP.mult, ["se/r", "ge", "sm/h"], ["sa/%d" % k])
            elif step == 2:
                for k in range(4):
                    ts(sc[:, 20 * k:20 * k + 20], se[:, 60:80], sm[:, 36 + k:37 + k], None, OP.is_gt, None,
                       ["se/r", "sm/lo"], ["sc/%d" % k])
            elif step == 3:
                tt(sf[:], sa[:], sc[:], OP.mult, ["sa", "sc"], ["sf"])
            elif step == 4:
                tt(se[:, 0:40], sf[:, 0:40], sf[:, 40:80], OP.add, ["sf"], ["se/a"])
            elif step == 5:
                tt(se[:, 40:60], se[:, 0:20], se[:, 20:40], OP.add, ["se/a"], ["se/b"])
            elif step == 6:
                tt(sa[:, 0:20], se[:, 40:60], se[:, 60:80], OP.subtract, ["se/b", "se/r"], ["sa/0"])
            elif step == 7:
                tt(sa[:, 20:40], sa[:, 0:20], T.old[:], OP.max, ["sa/0", "old"], ["sa/1"])
            else:
                for t in range(4):
                    ts(T.po16[:, 20 * t:20 * t + 20], sa[:, 20:40], float(t), None, OP.add, None, ["sa/1"],
                       ["po16/%d" % t])

        def ones(b, same):
            if r == 0:
                quant("quo", 128 * b, 128 * b + 128, "uo", 3 - b, ["uo"], [b])

        def last(step, same):
            if r == NR - 1 and step == 0:
                ts(T.po16[:, 80:100], sa[:, 20:40], 0.25, None, OP.mult, None, ["sa/1"], ["po16/s"])
                act(T.eq[:], T.slt[:].indirect(T.po16[:, 80:100]), AF.Copy, ["slt", "po16/s"], ["eq"])
                for q in range(8):
                    dma("S", lambda e, q=q: e.dma_start(T.sl[q:q + 1, :], T.eq[16 * q:16 * q + 1, :]), ("out", 0),
                        ["eq"], [])
            elif r == NR - 1:
                quant("qv", 0, 128, "vt", 0, ["vt"])
        for step in (PLAN0 if r == 0 else PLAN).split():
            if step[0] in "UZWHSOLR":
                {"U": unpack, "Z": pack_z, "W": layer, "H": pack_h, "S": where, "O": ones, "L": last,
                 "R": renew}[step[0]](int(step[1]), int(step[-1]))
            else:
                deal(step)

    X = "x%d" % NR
    for step in END.split():
        if step[0] in "VA":
            collect(NR, step)
            continue
        h = int(step[1])
        lo, hi = 160 * h, 160 * h + 160
        if step[0] == "x":
            quant("qx", lo, hi, X, 4 * lo, state(NR, h), [h])
            mm(h, 160, "qv", 0, "qx", lo, msub=[h])
            dma("S", lambda e: e.dma_start(T.oc[:, 4 * lo:4 * hi], T.qx[:, lo:hi].bitcast(dt.uint8)), ("out", 0),
                ["qx/%d" % h], [])
        elif step[0] == "s":
            dma(step[2], lambda e: e.dma_start(T.osc[4 * h:4 * h + 4, :], T.qxs[32 * h:32 * h + 4, :]),
                ("out", 0), ["qxs"], [])
        elif step[0] == "y":
            if step[2] == "V":
                cp(T.d1[:, lo:hi], T["p%d" % h][:, 0:160], ["p%d" % h], ["d1/%d" % h])
            else:
                act(T.d1[:, lo:hi], T["p%d" % h][:, 0:160], AF.Copy, ["p%d" % h], ["d1/%d" % h])
        else:
            dma(step[2], lambda e: e.dma_start(T.y[:, lo:hi], T.d1[:, lo:hi]), ("out", 0), ["d1/%d" % h], [])
    g.wait_ge(T.sem.out, 16 * (8 + 2 + 4 + 2))
    g.wait_ge(T.sem.ls, lsn[0])
    finish()
